import numpy as np
import ml_dtypes


def mxq(x, axis, fmt="e4m3"):
    dtype, down = {"e4m3": (ml_dtypes.float8_e4m3fn, 7), "e5m2": (ml_dtypes.float8_e5m2, 14)}[fmt]
    v = np.moveaxis(np.asarray(x, np.float32).astype(ml_dtypes.bfloat16).astype(np.float64), axis, -1)
    blocks = v.reshape(v.shape[:-1] + (-1, 32))
    amax = np.abs(blocks).max(-1, keepdims=True)
    byte = np.maximum(np.where(amax > 0, np.frexp(amax)[1] - 1 + 127, 0) - down, 1)
    scale = np.exp2(byte - 127.0)
    codes = (blocks / scale).astype(np.float32).astype(dtype).astype(np.float64)
    return np.moveaxis((codes * scale).reshape(v.shape), -1, axis)


WIDE = False


def mx_kscale(k):
    if not WIDE:
        return np.ones(k)
    levels = np.array([30, -30])
    if k % 512:
        return np.exp2(np.random.permutation(np.resize(levels, k // 32))).repeat(32)
    a = np.empty((k // 512, 16))
    for p in range(k // 512):
        a[p, :8] = np.random.permutation(np.resize(levels, 8))
        for g in range(8):
            far = levels[np.abs(levels - a[p, g]) >= 10]
            a[p, g + 8] = far[np.random.randint(len(far))]
    return np.exp2(a.ravel()).repeat(32)


def f64(x):
    return np.asarray(x).astype(np.float64)


def striped8(idx):
    return np.concatenate([v.reshape(-1, 16).T for v in idx]).astype(np.uint16)


def unstriped8(offs):
    return np.stack([offs[16 * g:16 * g + 16].T.reshape(-1) for g in range(8)]).astype(np.int64)


K, N, T, J = 1024, 512, 2048, 1024


def setup_inputs():
    n = np.random.standard_normal
    s = mx_kscale(K)[:, None]
    m = np.exp(0.5 * n((1, J)))
    return {
        "dy": (m * n((K, J)) * s).astype(np.float32),
        "w": (n((K, N)) / np.sqrt(K) / s).astype(np.float32),
        "ls": (np.random.uniform(0.25, 1.0, N)).astype(np.float32),
        "wgo": np.repeat(np.random.uniform(0.5, 2.0, (8, J)), 16, axis=0).astype(np.float32),
        "offs": striped8(np.stack([np.random.permutation(T)[:J] for _ in range(8)])),
    }


def reference(dy, w, ls, wgo, offs):
    idx = unstriped8(offs)
    dy_q_ = mxq(f64(dy), 0, "e5m2")
    dy_r_ = mxq(f64(dy) - dy_q_, 0, "e4m3")
    w_ = mxq(f64(w), 0, "e4m3")
    dx = w_.T @ dy_q_ + w_.T @ dy_r_
    out = np.zeros((N, T))
    rows = np.arange(N)
    out[rows[:, None], idx[rows % 128 // 16]] = f64(wgo)[rows % 128] * (dx * f64(ls)[:, None])
    return out

@@ -1,0 +1,237 @@
+from contextlib import ExitStack
+
+import concourse.mybir as mybir
+
+K, N, T, J = 1024, 512, 2048, 1024
+FLOPS = 3221225472
+
+F32 = mybir.dt.float32
+BF16 = mybir.dt.bfloat16
+U32 = mybir.dt.uint32
+U16 = mybir.dt.uint16
+U8 = mybir.dt.uint8
+E4M3 = mybir.dt.float8_e4m3fn_x4
+E5M2 = mybir.dt.float8_e5m2_x4
+COPY = mybir.ActivationFunctionType.Copy
+MULT = mybir.AluOpType.mult
+ADD = mybir.AluOpType.add
+IS_EQUAL = mybir.AluOpType.is_equal
+SUBTRACT = mybir.AluOpType.subtract
+
+P = 128
+PACK = 4
+K_PASS = P * PACK
+PASSES = K // K_PASS
+J_TILE = 512
+J_TILES = J // J_TILE
+N_TILES = N // P
+RUN = 4
+QUAD = 32
+EYE_WIDTH = P - QUAD * 0 + 3 * P + PACK * K_PASS
+HALF = J_TILE // 2
+
+
+def tile_list_embg_tgf32_ls_kernel(tc, dy, w, ls, wgo, offs, out):
+    nc = tc.nc
+    with ExitStack() as ctx:
+        keep = ctx.enter_context(tc.tile_pool(name="keep", bufs=1))
+        dq_psum = ctx.enter_context(tc.psum_pool(name="dq_psum", bufs=6))
+        dx_psum = ctx.enter_context(tc.psum_pool(name="dx_psum", bufs=2))
+
+        def sb(name, shape, dtype, slot=None):
+            return keep.tile(shape, dtype, name=name, tag=slot or name, align_bytes=64)
+
+        def interleave(copy, dst, src):
+            copy(
+                out=dst.rearrange("p (c i) t -> p c t i", i=RUN),
+                in_=src.rearrange("p t (c i) -> p c t i", i=RUN),
+            )
+
+        def scalar_cast(out, in_):
+            nc.scalar.activation(out=out, in_=in_, func=COPY)
+
+        def quantize(codes, scales, grouped, fmt):
+            nc.vector.quantize_mx(out=codes.bitcast(fmt), scales=scales, in_=grouped.rearrange("p c t -> p (c t)"))
+
+        def k_rows(x, a, cols):
+            return x[a * K_PASS : (a + 1) * K_PASS, cols].rearrange("(p t) c -> p t c", t=PACK)
+
+        units = [(a, h) for h in range(J_TILES) for a in range(PASSES)]
+        halves = [slice(c * HALF, (c + 1) * HALF) for c in range(2)]
+
+        offsets = keep.tile([P, J // 16], U16, name="offsets")
+        ls_sb = sb("ls_sb", [P, N_TILES], F32)
+        wgo_sb = [sb("wgo%d" % h, [P, J_TILE], F32) for h in range(J_TILES)]
+        dy_raw = {(a, 0): [sb("dy_raw%d0%d" % (a, c), [P, PACK, HALF], F32)[:] for c in range(2)] for a in range(PASSES)}
+        dy_late = [sb("dy_raw%d1" % a, [P, PACK, J_TILE], F32) for a in range(PASSES)]
+        for a in range(PASSES):
+            dy_raw[a, 1] = [dy_late[a][:, :, cols] for cols in halves]
+        w_early = [sb("w_early%d" % n, [P, PASSES, PACK, P], F32) for n in range(2)]
+
+        with nc.allow_non_contiguous_dma(reason="one factor for each partition"):
+            nc.scalar.dma_start(out=ls_sb[:], in_=ls.rearrange("(c p) -> p c", p=P))
+        for a in range(PASSES):
+            for c in range(2):
+                nc.sync.dma_start(out=dy_raw[a, 0][c], in_=k_rows(dy, a, halves[c]))
+        for a in range(PASSES):
+            nc.sync.dma_start(out=w_early[0][:, a], in_=k_rows(w, a, slice(0, P)))
+        nc.sync.dma_start(offsets[:], offs)
+        nc.sync.dma_start(out=wgo_sb[0][:], in_=wgo[:, 0:J_TILE])
+        for a in range(PASSES):
+            nc.sync.dma_start(out=w_early[1][:, a], in_=k_rows(w, a, slice(P, 2 * P)))
+        for a in range(PASSES):
+            nc.sync.dma_start(out=dy_late[a][:], in_=k_rows(dy, a, slice(J_TILE, J)))
+        nc.sync.dma_start(out=wgo_sb[1][:], in_=wgo[:, J_TILE:J])
+
+        ones = sb("ones", [P, QUAD + 1], F32)
+        nc.vector.memset(ones[:], 1.0)
+        eye = sb("eye", [P, EYE_WIDTH], BF16)
+        nc.vector.memset(eye[:, 0 : PACK * K_PASS + 2].bitcast(U32), 0)
+        column = sb("column", [P, QUAD], F32)
+        nc.vector.tensor_tensor_scan(column[:], ones[:, 0:QUAD], ones[:, 0:QUAD], 0.0, MULT, ADD)
+        row = sb("row", [P, QUAD], F32)
+        nc.vector.transpose(row[:], column[:])
+        diagonal = sb("diagonal", [P, QUAD], BF16)
+        nc.vector.tensor_tensor(diagonal[:], column[:], row[:], IS_EQUAL)
+        for b in range(P // QUAD):
+            rows = slice(b * QUAD, (b + 1) * QUAD)
+            run = eye[rows, b * P : b * P + PACK * (K_PASS + 1)].rearrange("p (t x) -> p t x", t=PACK)
+            nc.vector.tensor_copy(
+                out=run[:, :, 0:P:PACK], in_=diagonal[rows, :].unsqueeze(1).to_broadcast([QUAD, PACK, QUAD])
+            )
+        eye_codes = sb("eye_codes", [P, PACK * P], U32)
+        eye_scales = sb("eye_scales", [P, PACK * P], U8)
+        nc.vector.quantize_mx(out=eye_codes[:].bitcast(E4M3), scales=eye_scales[:], in_=eye[:, 0 : PACK * K_PASS])
+
+        dq_codes = {u: sb("dq_codes%d%d" % u, [P, J_TILE], U32) for u in units}
+        dq_scales = {u: sb("dq_scales%d%d" % u, [P, J_TILE], U8) for u in units}
+        dr_codes = {u: sb("dr_codes%d%d" % u, [P, J_TILE], U32) for u in units}
+        dr_scales = {u: sb("dr_scales%d%d" % u, [P, J_TILE], U8) for u in units}
+        w_codes = [sb("w_codes%d" % n, [P, PASSES * P], U32) for n in range(N_TILES)]
+        w_scales = [sb("w_scales%d" % n, [P, PASSES * P], U8) for n in range(N_TILES)]
+        dx_sb = {}
+        windows = {}
+
+        def window(n, memset, slot=None):
+            windows[n] = sb("window%d" % n, [P, T], F32, slot)
+            memset(windows[n][:], 0.0)
+
+        def first_tier_early(a):
+            grouped = [sb("dy_grouped%d%d" % (a, c), [P, HALF, PACK], BF16) for c in range(2)]
+            for c in range(2):
+                interleave(scalar_cast, grouped[c][:], dy_raw[a, 0][c])
+            for c in range(2):
+                quantize(dq_codes[a, 0][:, halves[c]], dq_scales[a, 0][:, halves[c]], grouped[c][:], E5M2)
+
+        def first_tier_late(a, slot):
+            grouped = sb("dy_grouped_late%d" % a, [P, J_TILE, PACK], BF16, slot)
+            for c in range(2):
+                interleave(scalar_cast, grouped[:, halves[c], :], dy_raw[a, 1][c])
+            quantize(dq_codes[a, 1][:], dq_scales[a, 1][:], grouped[:], E5M2)
+
+        def decode(u):
+            banks = []
+            for t in range(PACK):
+                bank = dq_psum.tile([P, J_TILE], F32, name="dq_bank")
+                nc.tensor.matmul_mx(
+                    out=bank[:],
+                    lhsT=eye_codes[:, t * P : (t + 1) * P].bitcast(E4M3),
+                    lhsT_scale=eye_scales[:, t * P : (t + 1) * P],
+                    rhs=dq_codes[u][:].bitcast(E5M2),
+                    rhs_scale=dq_scales[u][:],
+                    start=True,
+                    stop=True,
+                )
+                banks.append(bank)
+            return banks
+
+        def second_tier_early(a):
+            banks = decode((a, 0))
+            left = [sb("left%d0%d" % (a, c), [P, PACK, HALF], BF16) for c in range(2)]
+            grouped = [sb("dr_grouped%d0%d" % (a, c), [P, HALF, PACK], BF16) for c in range(2)]
+            for c in range(2):
+                for t in range(PACK):
+                    nc.vector.tensor_tensor(left[c][:, t, :], dy_raw[a, 0][c][:, t, :], banks[t][:, halves[c]], SUBTRACT)
+            for c in range(2):
+                interleave(nc.scalar.copy, grouped[c][:], left[c][:])
+            for c in range(2):
+                quantize(dr_codes[a, 0][:, halves[c]], dr_scales[a, 0][:, halves[c]], grouped[c][:], E4M3)
+
+        def second_tier_late(a):
+            banks = decode((a, 1))
+            left = sb("left%d1" % a, [P, PACK, J_TILE], BF16)
+            grouped = sb("dr_grouped%d1" % a, [P, J_TILE, PACK], BF16)
+            for t in range(PACK):
+                nc.vector.tensor_tensor(left[:, t, :], dy_late[a][:, t, :], banks[t][:], SUBTRACT)
+            for cols in halves:
+                interleave(nc.scalar.copy, grouped[:, cols, :], left[:, :, cols])
+            quantize(dr_codes[a, 1][:], dr_scales[a, 1][:], grouped[:], E4M3)
+
+        def weights(n, raw, copy, slot=None):
+            grouped = sb("w_grouped%d" % n, [P, PASSES * P, PACK], BF16, slot)
+            for a in range(PASSES):
+                interleave(copy, grouped[:, a * P : (a + 1) * P, :], raw[:, a])
+            quantize(w_codes[n][:], w_scales[n][:], grouped[:], E4M3)
+
+        def weights_by_pass(n, raw, slots):
+            grouped = [sb("w_grouped%d%d" % (n, a), [P, P, PACK], BF16, slots[a]) for a in range(PASSES)]
+            for a in range(PASSES):
+                interleave(nc.scalar.copy, grouped[a][:], raw[:, a])
+            for a in range(PASSES):
+                cols = slice(a * P, (a + 1) * P)
+                quantize(w_codes[n][:, cols], w_scales[n][:, cols], grouped[a][:], E4M3)
+
+        def product(n, h, slot=None):
+            dx_sb[n, h] = sb("dx%d%d" % (n, h), [P, J_TILE], F32, slot)
+            acc = dx_psum.tile([P, J_TILE], F32, name="acc")
+            passes = [(a, dq_codes, dq_scales, E5M2) for a in range(PASSES)]
+            passes += [(a, dr_codes, dr_scales, E4M3) for a in range(PASSES)]
+            for i, (a, codes, scales, fmt) in enumerate(passes):
+                nc.tensor.matmul_mx(
+                    out=acc[:],
+                    lhsT=w_codes[n][:, a * P : (a + 1) * P].bitcast(E4M3),
+                    lhsT_scale=w_scales[n][:, a * P : (a + 1) * P],
+                    rhs=codes[a, h][:].bitcast(fmt),
+                    rhs_scale=scales[a, h][:],
+                    start=(i == 0),
+                    stop=(i == len(passes) - 1),
+                )
+            nc.scalar.activation(out=dx_sb[n, h][:], in_=acc[:], func=COPY, scale=ls_sb[:, n : n + 1])
+
+        def scatter(n, h):
+            cols = J_TILE // 16
+            nc.vector.tensor_tensor(
+                windows[n][:].indirect(offsets[:, h * cols : (h + 1) * cols]), dx_sb[n, h][:], wgo_sb[h][:], MULT
+            )
+
+        window(0, nc.gpsimd.memset)
+        for a in range(PASSES):
+            first_tier_early(a)
+        second_tier_early(0)
+        weights(0, w_early[0], nc.vector.tensor_copy, "dy_grouped11")
+        second_tier_early(1)
+        w_late = sb("w_late", [P, PASSES, PACK, 2 * P], F32)
+        for a in range(PASSES):
+            nc.sync.dma_start(out=w_late[:, a], in_=k_rows(w, a, slice(2 * P, N)))
+        window(1, nc.vector.memset, "dr_grouped101")
+        weights_by_pass(1, w_early[1], ["dy_raw101", "left101"])
+        window(2, nc.gpsimd.memset, "dy_raw101")
+        product(0, 0)
+        product(1, 0)
+        scatter(0, 0)
+        first_tier_late(0, "left101")
+        scatter(1, 0)
+        first_tier_late(1, "left101")
+        weights(2, w_late[:, :, :, 0:P], nc.scalar.copy, "dx10")
+        weights(3, w_late[:, :, :, P : 2 * P], nc.scalar.copy, "dx10")
+        second_tier_late(0)
+        window(3, nc.gpsimd.memset, "dr_grouped01")
+        second_tier_late(1)
+        product(2, 0, "dy_raw11")
+        product(3, 0, "left11")
+        scatter(2, 0)
+        scatter(3, 0)
+        for n in range(N_TILES):
+            product(n, 1)
+            scatter(n, 1)
+            nc.sync.dma_start(out=out[n * P : (n + 1) * P, :], in_=windows[n][:])

@@ -27,7 +27,7 @@ J_TILES = J // J_TILE
 N_TILES = N // P
 RUN = 4
 QUAD = 32
-EYE_WIDTH = P - QUAD * 0 + 3 * P + PACK * K_PASS
+EYE_WIDTH = PACK * (K_PASS + P)
 HALF = J_TILE // 2
 
 
@@ -62,7 +62,8 @@ def tile_list_embg_tgf32_ls_kernel(tc, dy, w, ls, wgo, offs, out):
         offsets = keep.tile([P, J // 16], U16, name="offsets")
         ls_sb = sb("ls_sb", [P, N_TILES], F32)
         wgo_sb = [sb("wgo%d" % h, [P, J_TILE], F32) for h in range(J_TILES)]
-        dy_raw = {(a, 0): [sb("dy_raw%d0%d" % (a, c), [P, PACK, HALF], F32)[:] for c in range(2)] for a in range(PASSES)}
+        dy_early = [sb("dy_raw%d0" % a, [P, 2, PACK, HALF], F32) for a in range(PASSES)]
+        dy_raw = {(a, 0): [dy_early[a][:, c] for c in range(2)] for a in range(PASSES)}
         dy_late = [sb("dy_raw%d1" % a, [P, PACK, J_TILE], F32) for a in range(PASSES)]
         for a in range(PASSES):
             dy_raw[a, 1] = [dy_late[a][:, :, cols] for cols in halves]
@@ -83,10 +84,11 @@ def tile_list_embg_tgf32_ls_kernel(tc, dy, w, ls, wgo, offs, out):
             nc.sync.dma_start(out=dy_late[a][:], in_=k_rows(dy, a, slice(J_TILE, J)))
         nc.sync.dma_start(out=wgo_sb[1][:], in_=wgo[:, J_TILE:J])
 
-        ones = sb("ones", [P, QUAD + 1], F32)
+        windows = {0: sb("window0", [P, T], F32)}
+        ones = sb("ones", [P, QUAD], F32)
         nc.vector.memset(ones[:], 1.0)
         eye = sb("eye", [P, EYE_WIDTH], BF16)
-        nc.vector.memset(eye[:, 0 : PACK * K_PASS + 2].bitcast(U32), 0)
+        nc.vector.memset(eye[:, 0 : PACK * K_PASS].bitcast(U32), 0)
         column = sb("column", [P, QUAD], F32)
         nc.vector.tensor_tensor_scan(column[:], ones[:, 0:QUAD], ones[:, 0:QUAD], 0.0, MULT, ADD)
         row = sb("row", [P, QUAD], F32)
@@ -99,6 +101,8 @@ def tile_list_embg_tgf32_ls_kernel(tc, dy, w, ls, wgo, offs, out):
             nc.vector.tensor_copy(
                 out=run[:, :, 0:P:PACK], in_=diagonal[rows, :].unsqueeze(1).to_broadcast([QUAD, PACK, QUAD])
             )
+        for c in range(4):
+            nc.vector.memset(windows[0][:, max(c * 512 - 8, 0) : (c + 1) * 512], 0.0)
         eye_codes = sb("eye_codes", [P, PACK * P], U32)
         eye_scales = sb("eye_scales", [P, PACK * P], U8)
         nc.vector.quantize_mx(out=eye_codes[:].bitcast(E4M3), scales=eye_scales[:], in_=eye[:, 0 : PACK * K_PASS])
@@ -110,7 +114,6 @@ def tile_list_embg_tgf32_ls_kernel(tc, dy, w, ls, wgo, offs, out):
         w_codes = [sb("w_codes%d" % n, [P, PASSES * P], U32) for n in range(N_TILES)]
         w_scales = [sb("w_scales%d" % n, [P, PASSES * P], U8) for n in range(N_TILES)]
         dx_sb = {}
-        windows = {}
 
         def window(n, memset, slot=None):
             windows[n] = sb("window%d" % n, [P, T], F32, slot)
@@ -123,11 +126,18 @@ def tile_list_embg_tgf32_ls_kernel(tc, dy, w, ls, wgo, offs, out):
             for c in range(2):
                 quantize(dq_codes[a, 0][:, halves[c]], dq_scales[a, 0][:, halves[c]], grouped[c][:], E5M2)
 
-        def first_tier_late(a, slot):
-            grouped = sb("dy_grouped_late%d" % a, [P, J_TILE, PACK], BF16, slot)
+        def late_pair(a, n, slots):
+            first = sb("late%d0" % a, [P, PASSES * P + HALF, PACK], BF16, slots[0])
+            second = sb("late%d1" % a, [P, HALF, PACK], BF16, slots[1])
+            w_grouped = first[:, 0 : PASSES * P, :]
+            grouped = [first[:, PASSES * P :, :], second[:]]
+            for b in range(PASSES):
+                interleave(nc.scalar.copy, w_grouped[:, b * P : (b + 1) * P, :], w_late[:, b, :, (n - 2) * P : (n - 1) * P])
             for c in range(2):
-                interleave(scalar_cast, grouped[:, halves[c], :], dy_raw[a, 1][c])
-            quantize(dq_codes[a, 1][:], dq_scales[a, 1][:], grouped[:], E5M2)
+                interleave(scalar_cast, grouped[c], dy_raw[a, 1][c])
+            quantize(w_codes[n][:], w_scales[n][:], w_grouped, E4M3)
+            for c in range(2):
+                quantize(dq_codes[a, 1][:, halves[c]], dq_scales[a, 1][:, halves[c]], grouped[c], E5M2)
 
         def decode(u):
             banks = []
@@ -145,21 +155,24 @@ def tile_list_embg_tgf32_ls_kernel(tc, dy, w, ls, wgo, offs, out):
                 banks.append(bank)
             return banks
 
-        def second_tier_early(a):
+        def second_tier_early(a, whole_rows):
             banks = decode((a, 0))
-            left = [sb("left%d0%d" % (a, c), [P, PACK, HALF], BF16) for c in range(2)]
+            left = sb("left%d0" % a, [P, 2, PACK, HALF], BF16)
             grouped = [sb("dr_grouped%d0%d" % (a, c), [P, HALF, PACK], BF16) for c in range(2)]
+            for t in range(whole_rows):
+                bank = banks[t][:].rearrange("p (c j) -> p c j", c=2)
+                nc.vector.tensor_tensor(left[:, :, t, :], dy_early[a][:, :, t, :], bank, SUBTRACT)
             for c in range(2):
-                for t in range(PACK):
-                    nc.vector.tensor_tensor(left[c][:, t, :], dy_raw[a, 0][c][:, t, :], banks[t][:, halves[c]], SUBTRACT)
+                for t in range(whole_rows, PACK):
+                    nc.vector.tensor_tensor(left[:, c, t, :], dy_early[a][:, c, t, :], banks[t][:, halves[c]], SUBTRACT)
             for c in range(2):
-                interleave(nc.scalar.copy, grouped[c][:], left[c][:])
+                interleave(nc.scalar.copy, grouped[c][:], left[:, c])
             for c in range(2):
                 quantize(dr_codes[a, 0][:, halves[c]], dr_scales[a, 0][:, halves[c]], grouped[c][:], E4M3)
 
-        def second_tier_late(a):
+        def second_tier_late(a, slot=None):
             banks = decode((a, 1))
-            left = sb("left%d1" % a, [P, PACK, J_TILE], BF16)
+            left = sb("left%d1" % a, [P, PACK, J_TILE], BF16, slot)
             grouped = sb("dr_grouped%d1" % a, [P, J_TILE, PACK], BF16)
             for t in range(PACK):
                 nc.vector.tensor_tensor(left[:, t, :], dy_late[a][:, t, :], banks[t][:], SUBTRACT)
@@ -204,32 +217,29 @@ def tile_list_embg_tgf32_ls_kernel(tc, dy, w, ls, wgo, offs, out):
                 windows[n][:].indirect(offsets[:, h * cols : (h + 1) * cols]), dx_sb[n, h][:], wgo_sb[h][:], MULT
             )
 
-        window(0, nc.gpsimd.memset)
         for a in range(PASSES):
             first_tier_early(a)
-        second_tier_early(0)
+        second_tier_early(0, 2)
         weights(0, w_early[0], nc.vector.tensor_copy, "dy_grouped11")
-        second_tier_early(1)
+        second_tier_early(1, 0)
         w_late = sb("w_late", [P, PASSES, PACK, 2 * P], F32)
         for a in range(PASSES):
             nc.sync.dma_start(out=w_late[:, a], in_=k_rows(w, a, slice(2 * P, N)))
         window(1, nc.vector.memset, "dr_grouped101")
-        weights_by_pass(1, w_early[1], ["dy_raw101", "left101"])
-        window(2, nc.gpsimd.memset, "dy_raw101")
+        weights_by_pass(1, w_early[1], ["dy_raw10", "left10"])
         product(0, 0)
         product(1, 0)
         scatter(0, 0)
-        first_tier_late(0, "left101")
+        late_pair(0, 2, ["dy_raw10", "left10"])
         scatter(1, 0)
-        first_tier_late(1, "left101")
-        weights(2, w_late[:, :, :, 0:P], nc.scalar.copy, "dx10")
-        weights(3, w_late[:, :, :, P : 2 * P], nc.scalar.copy, "dx10")
-        second_tier_late(0)
-        window(3, nc.gpsimd.memset, "dr_grouped01")
+        late_pair(1, 3, ["dy_raw10", "left10"])
+        window(2, nc.gpsimd.memset, "dy_raw10")
+        second_tier_late(0, "left10")
+        product(2, 0, "dy_raw01")
         second_tier_late(1)
-        product(2, 0, "dy_raw11")
         product(3, 0, "left11")
         scatter(2, 0)
+        window(3, nc.vector.memset, "dy_raw11")
         scatter(3, 0)
         for n in range(N_TILES):
             product(n, 1)

@@ -67,7 +67,10 @@ def tile_list_embg_tgf32_ls_kernel(tc, dy, w, ls, wgo, offs, out):
         dy_late = [sb("dy_raw%d1" % a, [P, PACK, J_TILE], F32) for a in range(PASSES)]
         for a in range(PASSES):
             dy_raw[a, 1] = [dy_late[a][:, :, cols] for cols in halves]
-        w_early = [sb("w_early%d" % n, [P, PASSES, PACK, P], F32) for n in range(2)]
+        w_first = sb("w_first", [P, PASSES, PACK, P], F32)
+        w_middle = sb("w_middle", [P, PASSES, PACK, 2 * P], F32)
+        w_last = sb("w_last", [P, PASSES, PACK, P], F32)
+        w_raw = [w_first[:], w_middle[:, :, :, 0:P], w_middle[:, :, :, P : 2 * P], w_last[:]]
 
         with nc.allow_non_contiguous_dma(reason="one factor for each partition"):
             nc.scalar.dma_start(out=ls_sb[:], in_=ls.rearrange("(c p) -> p c", p=P))
@@ -75,20 +78,21 @@ def tile_list_embg_tgf32_ls_kernel(tc, dy, w, ls, wgo, offs, out):
             for c in range(2):
                 nc.sync.dma_start(out=dy_raw[a, 0][c], in_=k_rows(dy, a, halves[c]))
         for a in range(PASSES):
-            nc.sync.dma_start(out=w_early[0][:, a], in_=k_rows(w, a, slice(0, P)))
+            nc.sync.dma_start(out=w_first[:, a], in_=k_rows(w, a, slice(0, P)))
         nc.sync.dma_start(offsets[:], offs)
         nc.sync.dma_start(out=wgo_sb[0][:], in_=wgo[:, 0:J_TILE])
         for a in range(PASSES):
-            nc.sync.dma_start(out=w_early[1][:, a], in_=k_rows(w, a, slice(P, 2 * P)))
+            nc.sync.dma_start(out=w_middle[:, a], in_=k_rows(w, a, slice(P, 3 * P)))
         for a in range(PASSES):
             nc.sync.dma_start(out=dy_late[a][:], in_=k_rows(dy, a, slice(J_TILE, J)))
+        for a in range(PASSES):
+            nc.sync.dma_start(out=w_last[:, a], in_=k_rows(w, a, slice(3 * P, N)))
         nc.sync.dma_start(out=wgo_sb[1][:], in_=wgo[:, J_TILE:J])
 
-        windows = {0: sb("window0", [P, T], F32)}
-        ones = sb("ones", [P, QUAD], F32)
+        ones = sb("ones", [P, QUAD + 1], F32)
         nc.vector.memset(ones[:], 1.0)
         eye = sb("eye", [P, EYE_WIDTH], BF16)
-        nc.vector.memset(eye[:, 0 : PACK * K_PASS].bitcast(U32), 0)
+        nc.vector.memset(eye[:, 0 : PACK * K_PASS + 2].bitcast(U32), 0)
         column = sb("column", [P, QUAD], F32)
         nc.vector.tensor_tensor_scan(column[:], ones[:, 0:QUAD], ones[:, 0:QUAD], 0.0, MULT, ADD)
         row = sb("row", [P, QUAD], F32)
@@ -101,8 +105,6 @@ def tile_list_embg_tgf32_ls_kernel(tc, dy, w, ls, wgo, offs, out):
             nc.vector.tensor_copy(
                 out=run[:, :, 0:P:PACK], in_=diagonal[rows, :].unsqueeze(1).to_broadcast([QUAD, PACK, QUAD])
             )
-        for c in range(4):
-            nc.vector.memset(windows[0][:, max(c * 512 - 8, 0) : (c + 1) * 512], 0.0)
         eye_codes = sb("eye_codes", [P, PACK * P], U32)
         eye_scales = sb("eye_scales", [P, PACK * P], U8)
         nc.vector.quantize_mx(out=eye_codes[:].bitcast(E4M3), scales=eye_scales[:], in_=eye[:, 0 : PACK * K_PASS])
@@ -114,25 +116,25 @@ def tile_list_embg_tgf32_ls_kernel(tc, dy, w, ls, wgo, offs, out):
         w_codes = [sb("w_codes%d" % n, [P, PASSES * P], U32) for n in range(N_TILES)]
         w_scales = [sb("w_scales%d" % n, [P, PASSES * P], U8) for n in range(N_TILES)]
         dx_sb = {}
+        windows = {}
 
         def window(n, memset, slot=None):
             windows[n] = sb("window%d" % n, [P, T], F32, slot)
-            memset(windows[n][:], 0.0)
+            memset(windows[n][:].bitcast(U32), 0)
 
-        def first_tier_early(a):
+        def first_tier_early(a, casts):
             grouped = [sb("dy_grouped%d%d" % (a, c), [P, HALF, PACK], BF16) for c in range(2)]
             for c in range(2):
-                interleave(scalar_cast, grouped[c][:], dy_raw[a, 0][c])
+                interleave(casts[c], grouped[c][:], dy_raw[a, 0][c])
             for c in range(2):
                 quantize(dq_codes[a, 0][:, halves[c]], dq_scales[a, 0][:, halves[c]], grouped[c][:], E5M2)
 
-        def late_pair(a, n, slots):
-            first = sb("late%d0" % a, [P, PASSES * P + HALF, PACK], BF16, slots[0])
-            second = sb("late%d1" % a, [P, HALF, PACK], BF16, slots[1])
-            w_grouped = first[:, 0 : PASSES * P, :]
-            grouped = [first[:, PASSES * P :, :], second[:]]
+        def late_pair(a, n, layout):
+            pieces = [sb("late%d%d" % (a, i), [P, width, PACK], BF16, slot) for i, (slot, width) in enumerate(layout)]
+            w_grouped = pieces[0][:, 0 : PASSES * P, :]
+            grouped = [pieces[0][:, PASSES * P : PASSES * P + HALF, :], pieces[-1][:, layout[-1][1] - HALF :, :]]
             for b in range(PASSES):
-                interleave(nc.scalar.copy, w_grouped[:, b * P : (b + 1) * P, :], w_late[:, b, :, (n - 2) * P : (n - 1) * P])
+                interleave(nc.scalar.copy, w_grouped[:, b * P : (b + 1) * P, :], w_raw[n][:, b])
             for c in range(2):
                 interleave(scalar_cast, grouped[c], dy_raw[a, 1][c])
             quantize(w_codes[n][:], w_scales[n][:], w_grouped, E4M3)
@@ -169,6 +171,21 @@ def tile_list_embg_tgf32_ls_kernel(tc, dy, w, ls, wgo, offs, out):
                 interleave(nc.scalar.copy, grouped[c][:], left[:, c])
             for c in range(2):
                 quantize(dr_codes[a, 0][:, halves[c]], dr_scales[a, 0][:, halves[c]], grouped[c][:], E4M3)
+
+        def second_tier_last_early():
+            banks = decode((1, 0))
+            pieces = [(0, 0, HALF), (1, 0, HALF // 2), (1, HALF // 2, HALF // 2)]
+            left = [sb("left10%d" % i, [P, PACK, width], BF16) for i, (c, first, width) in enumerate(pieces)]
+            grouped = [sb("dr_grouped10%d" % i, [P, width, PACK], BF16) for i, (c, first, width) in enumerate(pieces)]
+            cols = [slice(c * HALF + first, c * HALF + first + width) for c, first, width in pieces]
+            for i, (c, first, width) in enumerate(pieces):
+                for t in range(PACK):
+                    raw = dy_early[1][:, c, t, first : first + width]
+                    nc.vector.tensor_tensor(left[i][:, t, :], raw, banks[t][:, cols[i]], SUBTRACT)
+            for i in range(len(pieces)):
+                interleave(nc.scalar.copy, grouped[i][:], left[i][:])
+            for i in range(len(pieces)):
+                quantize(dr_codes[1, 0][:, cols[i]], dr_scales[1, 0][:, cols[i]], grouped[i][:], E4M3)
 
         def second_tier_late(a, slot=None):
             banks = decode((a, 1))
@@ -217,29 +234,27 @@ def tile_list_embg_tgf32_ls_kernel(tc, dy, w, ls, wgo, offs, out):
                 windows[n][:].indirect(offsets[:, h * cols : (h + 1) * cols]), dx_sb[n, h][:], wgo_sb[h][:], MULT
             )
 
-        for a in range(PASSES):
-            first_tier_early(a)
+        window(0, nc.gpsimd.memset)
+        first_tier_early(0, [scalar_cast, nc.vector.tensor_copy])
+        first_tier_early(1, [scalar_cast, scalar_cast])
         second_tier_early(0, 2)
-        weights(0, w_early[0], nc.vector.tensor_copy, "dy_grouped11")
-        second_tier_early(1, 0)
-        w_late = sb("w_late", [P, PASSES, PACK, 2 * P], F32)
-        for a in range(PASSES):
-            nc.sync.dma_start(out=w_late[:, a], in_=k_rows(w, a, slice(2 * P, N)))
-        window(1, nc.vector.memset, "dr_grouped101")
-        weights_by_pass(1, w_early[1], ["dy_raw10", "left10"])
+        weights(0, w_raw[0], nc.vector.tensor_copy, "dy_grouped11")
+        second_tier_last_early()
+        window(1, nc.vector.memset, "dr_grouped102")
+        weights_by_pass(1, w_raw[1], ["left101", "left102"])
         product(0, 0)
-        product(1, 0)
         scatter(0, 0)
-        late_pair(0, 2, ["dy_raw10", "left10"])
+        late_pair(0, 2, [("left101", PASSES * P + HALF), ("left102", HALF)])
+        product(1, 0)
+        window(2, nc.gpsimd.memset, "left102")
         scatter(1, 0)
-        late_pair(1, 3, ["dy_raw10", "left10"])
-        window(2, nc.gpsimd.memset, "dy_raw10")
-        second_tier_late(0, "left10")
+        late_pair(1, 3, [("left101", PASSES * P + J_TILE)])
+        second_tier_late(0, "left101")
         product(2, 0, "dy_raw01")
         second_tier_late(1)
         product(3, 0, "left11")
         scatter(2, 0)
-        window(3, nc.vector.memset, "dy_raw11")
+        window(3, nc.gpsimd.memset, "dy_raw11")
         scatter(3, 0)
         for n in range(N_TILES):
             product(n, 1)

@@ -60,7 +60,9 @@ def tile_list_embg_tgf32_ls_kernel(tc, dy, w, ls, wgo, offs, out):
         halves = [slice(c * HALF, (c + 1) * HALF) for c in range(2)]
 
         offsets = keep.tile([P, J // 16], U16, name="offsets")
-        ls_sb = sb("ls_sb", [P, N_TILES], F32)
+        ls_rows = sb("ls_rows", [P, QUAD], F32)
+        ls_sb = sb("ls_sb", [P, QUAD], F32)
+        nc.vector.memset(ls_rows[:], 0.0)
         wgo_sb = [sb("wgo%d" % h, [P, J_TILE], F32) for h in range(J_TILES)]
         dy_early = [sb("dy_raw%d0" % a, [P, 2, PACK, HALF], F32) for a in range(PASSES)]
         dy_raw = {(a, 0): [dy_early[a][:, c] for c in range(2)] for a in range(PASSES)}
@@ -72,13 +74,14 @@ def tile_list_embg_tgf32_ls_kernel(tc, dy, w, ls, wgo, offs, out):
         w_last = sb("w_last", [P, PASSES, PACK, P], F32)
         w_raw = [w_first[:], w_middle[:, :, :, 0:P], w_middle[:, :, :, P : 2 * P], w_last[:]]
 
-        with nc.allow_non_contiguous_dma(reason="one factor for each partition"):
-            nc.scalar.dma_start(out=ls_sb[:], in_=ls.rearrange("(c p) -> p c", p=P))
         for a in range(PASSES):
             for c in range(2):
                 nc.sync.dma_start(out=dy_raw[a, 0][c], in_=k_rows(dy, a, halves[c]))
         for a in range(PASSES):
             nc.sync.dma_start(out=w_first[:, a], in_=k_rows(w, a, slice(0, P)))
+        ls_view = ls.rearrange("(n b i) -> b n i", n=N_TILES, i=QUAD)
+        for b in range(P // QUAD):
+            nc.sync.dma_start(out=ls_rows[b * QUAD : b * QUAD + N_TILES, :], in_=ls_view[b])
         nc.sync.dma_start(offsets[:], offs)
         nc.sync.dma_start(out=wgo_sb[0][:], in_=wgo[:, 0:J_TILE])
         for a in range(PASSES):
@@ -129,10 +132,7 @@ def tile_list_embg_tgf32_ls_kernel(tc, dy, w, ls, wgo, offs, out):
             for c in range(2):
                 quantize(dq_codes[a, 0][:, halves[c]], dq_scales[a, 0][:, halves[c]], grouped[c][:], E5M2)
 
-        def late_pair(a, n, layout):
-            pieces = [sb("late%d%d" % (a, i), [P, width, PACK], BF16, slot) for i, (slot, width) in enumerate(layout)]
-            w_grouped = pieces[0][:, 0 : PASSES * P, :]
-            grouped = [pieces[0][:, PASSES * P : PASSES * P + HALF, :], pieces[-1][:, layout[-1][1] - HALF :, :]]
+        def late_pair(a, n, w_grouped, grouped):
             for b in range(PASSES):
                 interleave(nc.scalar.copy, w_grouped[:, b * P : (b + 1) * P, :], w_raw[n][:, b])
             for c in range(2):
@@ -187,11 +187,14 @@ def tile_list_embg_tgf32_ls_kernel(tc, dy, w, ls, wgo, offs, out):
             for i in range(len(pieces)):
                 quantize(dr_codes[1, 0][:, cols[i]], dr_scales[1, 0][:, cols[i]], grouped[i][:], E4M3)
 
-        def second_tier_late(a, slot=None):
+        def second_tier_late(a, left, on_gpsimd=0):
             banks = decode((a, 1))
-            left = sb("left%d1" % a, [P, PACK, J_TILE], BF16, slot)
             grouped = sb("dr_grouped%d1" % a, [P, J_TILE, PACK], BF16)
-            for t in range(PACK):
+            for t in range(on_gpsimd):
+                decoded = sb("decoded%d" % t, [P, J_TILE], F32)
+                nc.scalar.copy(out=decoded[:], in_=banks[t][:])
+                nc.gpsimd.tensor_tensor(left[:, t, :], dy_late[a][:, t, :], decoded[:], SUBTRACT)
+            for t in range(on_gpsimd, PACK):
                 nc.vector.tensor_tensor(left[:, t, :], dy_late[a][:, t, :], banks[t][:], SUBTRACT)
             for cols in halves:
                 interleave(nc.scalar.copy, grouped[:, cols, :], left[:, :, cols])
@@ -240,19 +243,23 @@ def tile_list_embg_tgf32_ls_kernel(tc, dy, w, ls, wgo, offs, out):
         second_tier_early(0, 2)
         weights(0, w_raw[0], nc.vector.tensor_copy, "dy_grouped11")
         second_tier_last_early()
+        nc.vector.transpose(ls_sb[:], ls_rows[:])
         window(1, nc.vector.memset, "dr_grouped102")
         weights_by_pass(1, w_raw[1], ["left101", "left102"])
         product(0, 0)
         scatter(0, 0)
-        late_pair(0, 2, [("left101", PASSES * P + HALF), ("left102", HALF)])
+        late = [sb("late0%d" % i, [P, HALF, PACK], BF16, "left10%d" % i)[:] for i in range(3)]
+        late_pair(0, 2, late[0], late[1:])
         product(1, 0)
         window(2, nc.gpsimd.memset, "left102")
         scatter(1, 0)
-        late_pair(1, 3, [("left101", PASSES * P + J_TILE)])
-        second_tier_late(0, "left101")
-        product(2, 0, "dy_raw01")
-        second_tier_late(1)
-        product(3, 0, "left11")
+        joint = sb("late10", [P, 2, HALF, PACK], BF16, "left100")
+        late_pair(1, 3, joint[:, 0], [joint[:, 1], sb("late11", [P, HALF, PACK], BF16, "left101")[:]])
+        left_late = sb("left_late", [P, PASSES, PACK, J_TILE], BF16, "left101")
+        second_tier_late(0, left_late[:, 0], 2)
+        product(2, 0, "left100")
+        second_tier_late(1, left_late[:, 1])
+        product(3, 0, "left101")
         scatter(2, 0)
         window(3, nc.gpsimd.memset, "dy_raw11")
         scatter(3, 0)

@@ -3,7 +3,7 @@ from contextlib import ExitStack
 import concourse.mybir as mybir
 
 K, N, T, J = 1024, 512, 2048, 1024
-FLOPS = 3221225472
+FLOPS = 2 * (2 * K * N * J) + 2 * K * 512 * J
 
 F32 = mybir.dt.float32
 BF16 = mybir.dt.bfloat16
@@ -24,27 +24,33 @@ K_PASS = P * PACK
 PASSES = K // K_PASS
 J_TILE = 512
 J_TILES = J // J_TILE
+HALF = J_TILE // 2
+QUARTER = J_TILE // 4
 N_TILES = N // P
+LIST_GROUP = 16
 RUN = 4
 QUAD = 32
 EYE_WIDTH = PACK * (K_PASS + P)
-HALF = J_TILE // 2
+DECODE_BANKS = 6
+PRODUCT_BANKS = 2
+WHOLE_ROWS = 2
+GPSIMD_ROWS = 2
 
 
 def tile_list_embg_tgf32_ls_kernel(tc, dy, w, ls, wgo, offs, out):
     nc = tc.nc
     with ExitStack() as ctx:
         keep = ctx.enter_context(tc.tile_pool(name="keep", bufs=1))
-        dq_psum = ctx.enter_context(tc.psum_pool(name="dq_psum", bufs=6))
-        dx_psum = ctx.enter_context(tc.psum_pool(name="dx_psum", bufs=2))
+        decode_psum = ctx.enter_context(tc.psum_pool(name="decode_psum", bufs=DECODE_BANKS))
+        product_psum = ctx.enter_context(tc.psum_pool(name="product_psum", bufs=PRODUCT_BANKS))
 
         def sb(name, shape, dtype, slot=None):
             return keep.tile(shape, dtype, name=name, tag=slot or name, align_bytes=64)
 
-        def interleave(copy, dst, src):
+        def group(copy, grouped, rows):
             copy(
-                out=dst.rearrange("p (c i) t -> p c t i", i=RUN),
-                in_=src.rearrange("p t (c i) -> p c t i", i=RUN),
+                out=grouped.rearrange("p (c i) t -> p c t i", i=RUN),
+                in_=rows.rearrange("p t (c i) -> p c t i", i=RUN),
             )
 
         def scalar_cast(out, in_):
@@ -53,43 +59,36 @@ def tile_list_embg_tgf32_ls_kernel(tc, dy, w, ls, wgo, offs, out):
         def quantize(codes, scales, grouped, fmt):
             nc.vector.quantize_mx(out=codes.bitcast(fmt), scales=scales, in_=grouped.rearrange("p c t -> p (c t)"))
 
-        def k_rows(x, a, cols):
-            return x[a * K_PASS : (a + 1) * K_PASS, cols].rearrange("(p t) c -> p t c", t=PACK)
+        def k_rows(x, g, cols):
+            return x[g * K_PASS : (g + 1) * K_PASS, cols].rearrange("(p t) c -> p t c", t=PACK)
 
-        units = [(a, h) for h in range(J_TILES) for a in range(PASSES)]
+        units = [(g, h) for h in range(J_TILES) for g in range(PASSES)]
         halves = [slice(c * HALF, (c + 1) * HALF) for c in range(2)]
 
-        offsets = keep.tile([P, J // 16], U16, name="offsets")
-        ls_rows = sb("ls_rows", [P, QUAD], F32)
-        ls_sb = sb("ls_sb", [P, QUAD], F32)
-        nc.vector.memset(ls_rows[:], 0.0)
+        offsets = keep.tile([P, J // LIST_GROUP], U16, name="offsets")
+        ls_sb = sb("ls_sb", [P, N_TILES], F32)
         wgo_sb = [sb("wgo%d" % h, [P, J_TILE], F32) for h in range(J_TILES)]
-        dy_early = [sb("dy_raw%d0" % a, [P, 2, PACK, HALF], F32) for a in range(PASSES)]
-        dy_raw = {(a, 0): [dy_early[a][:, c] for c in range(2)] for a in range(PASSES)}
-        dy_late = [sb("dy_raw%d1" % a, [P, PACK, J_TILE], F32) for a in range(PASSES)]
-        for a in range(PASSES):
-            dy_raw[a, 1] = [dy_late[a][:, :, cols] for cols in halves]
-        w_first = sb("w_first", [P, PASSES, PACK, P], F32)
-        w_middle = sb("w_middle", [P, PASSES, PACK, 2 * P], F32)
-        w_last = sb("w_last", [P, PASSES, PACK, P], F32)
-        w_raw = [w_first[:], w_middle[:, :, :, 0:P], w_middle[:, :, :, P : 2 * P], w_last[:]]
+        dy_first = [sb("dy_first%d" % g, [P, 2, PACK, HALF], F32) for g in range(PASSES)]
+        dy_second = [sb("dy_second%d" % g, [P, PACK, J_TILE], F32) for g in range(PASSES)]
+        w_early = [sb("w_early%d" % n, [P, PASSES, PACK, P], F32) for n in range(2)]
+        w_late = sb("w_late", [P, PASSES, PACK, 2 * P], F32)
+        w_rows = [w_early[0][:], w_early[1][:], w_late[:, :, :, 0:P], w_late[:, :, :, P : 2 * P]]
 
-        for a in range(PASSES):
+        for g in range(PASSES):
             for c in range(2):
-                nc.sync.dma_start(out=dy_raw[a, 0][c], in_=k_rows(dy, a, halves[c]))
-        for a in range(PASSES):
-            nc.sync.dma_start(out=w_first[:, a], in_=k_rows(w, a, slice(0, P)))
-        ls_view = ls.rearrange("(n b i) -> b n i", n=N_TILES, i=QUAD)
-        for b in range(P // QUAD):
-            nc.sync.dma_start(out=ls_rows[b * QUAD : b * QUAD + N_TILES, :], in_=ls_view[b])
+                nc.sync.dma_start(out=dy_first[g][:, c], in_=k_rows(dy, g, halves[c]))
+        for g in range(PASSES):
+            nc.sync.dma_start(out=w_early[0][:, g], in_=k_rows(w, g, slice(0, P)))
         nc.sync.dma_start(offsets[:], offs)
         nc.sync.dma_start(out=wgo_sb[0][:], in_=wgo[:, 0:J_TILE])
-        for a in range(PASSES):
-            nc.sync.dma_start(out=w_middle[:, a], in_=k_rows(w, a, slice(P, 3 * P)))
-        for a in range(PASSES):
-            nc.sync.dma_start(out=dy_late[a][:], in_=k_rows(dy, a, slice(J_TILE, J)))
-        for a in range(PASSES):
-            nc.sync.dma_start(out=w_last[:, a], in_=k_rows(w, a, slice(3 * P, N)))
+        with nc.allow_non_contiguous_dma(reason="one factor for each partition and n tile"):
+            nc.sync.dma_start(out=ls_sb[:], in_=ls.rearrange("(c p) -> p c", p=P))
+        for g in range(PASSES):
+            nc.sync.dma_start(out=w_early[1][:, g], in_=k_rows(w, g, slice(P, 2 * P)))
+        nc.sync.dma_start(out=dy_second[0][:], in_=k_rows(dy, 0, slice(J_TILE, J)))
+        for g in range(PASSES):
+            nc.sync.dma_start(out=w_late[:, g], in_=k_rows(w, g, slice(2 * P, N)))
+        nc.sync.dma_start(out=dy_second[1][:], in_=k_rows(dy, 1, slice(J_TILE, J)))
         nc.sync.dma_start(out=wgo_sb[1][:], in_=wgo[:, J_TILE:J])
 
         ones = sb("ones", [P, QUAD + 1], F32)
@@ -103,10 +102,10 @@ def tile_list_embg_tgf32_ls_kernel(tc, dy, w, ls, wgo, offs, out):
         diagonal = sb("diagonal", [P, QUAD], BF16)
         nc.vector.tensor_tensor(diagonal[:], column[:], row[:], IS_EQUAL)
         for b in range(P // QUAD):
-            rows = slice(b * QUAD, (b + 1) * QUAD)
-            run = eye[rows, b * P : b * P + PACK * (K_PASS + 1)].rearrange("p (t x) -> p t x", t=PACK)
+            parts = slice(b * QUAD, (b + 1) * QUAD)
+            run = eye[parts, b * P : b * P + PACK * (K_PASS + 1)].rearrange("p (t x) -> p t x", t=PACK)
             nc.vector.tensor_copy(
-                out=run[:, :, 0:P:PACK], in_=diagonal[rows, :].unsqueeze(1).to_broadcast([QUAD, PACK, QUAD])
+                out=run[:, :, 0:P:PACK], in_=diagonal[parts, :].unsqueeze(1).to_broadcast([QUAD, PACK, QUAD])
             )
         eye_codes = sb("eye_codes", [P, PACK * P], U32)
         eye_scales = sb("eye_scales", [P, PACK * P], U8)
@@ -116,153 +115,156 @@ def tile_list_embg_tgf32_ls_kernel(tc, dy, w, ls, wgo, offs, out):
         dq_scales = {u: sb("dq_scales%d%d" % u, [P, J_TILE], U8) for u in units}
         dr_codes = {u: sb("dr_codes%d%d" % u, [P, J_TILE], U32) for u in units}
         dr_scales = {u: sb("dr_scales%d%d" % u, [P, J_TILE], U8) for u in units}
-        w_codes = [sb("w_codes%d" % n, [P, PASSES * P], U32) for n in range(N_TILES)]
+        w_codes = [sb("w_codes%d" % n, [P, PASSES * P], U32) for n in range(N_TILES - 1)]
         w_scales = [sb("w_scales%d" % n, [P, PASSES * P], U8) for n in range(N_TILES)]
         dx_sb = {}
         windows = {}
 
-        def window(n, memset, slot=None):
+        def window(n, slot=None):
             windows[n] = sb("window%d" % n, [P, T], F32, slot)
-            memset(windows[n][:].bitcast(U32), 0)
+            nc.gpsimd.memset(windows[n][:].bitcast(U32), 0)
 
-        def first_tier_early(a, casts):
-            grouped = [sb("dy_grouped%d%d" % (a, c), [P, HALF, PACK], BF16) for c in range(2)]
+        def first_tier(g, h, rows, casts, slots):
+            grouped = [sb("dy_grouped%d%d%d" % (g, h, c), [P, HALF, PACK], BF16, slots[c]) for c in range(2)]
             for c in range(2):
-                interleave(casts[c], grouped[c][:], dy_raw[a, 0][c])
+                group(casts[c], grouped[c][:], rows[c])
             for c in range(2):
-                quantize(dq_codes[a, 0][:, halves[c]], dq_scales[a, 0][:, halves[c]], grouped[c][:], E5M2)
+                quantize(dq_codes[g, h][:, halves[c]], dq_scales[g, h][:, halves[c]], grouped[c][:], E5M2)
 
-        def late_pair(a, n, w_grouped, grouped):
-            for b in range(PASSES):
-                interleave(nc.scalar.copy, w_grouped[:, b * P : (b + 1) * P, :], w_raw[n][:, b])
-            for c in range(2):
-                interleave(scalar_cast, grouped[c], dy_raw[a, 1][c])
-            quantize(w_codes[n][:], w_scales[n][:], w_grouped, E4M3)
-            for c in range(2):
-                quantize(dq_codes[a, 1][:, halves[c]], dq_scales[a, 1][:, halves[c]], grouped[c], E5M2)
-
-        def decode(u):
+        def decode(g, h):
             banks = []
             for t in range(PACK):
-                bank = dq_psum.tile([P, J_TILE], F32, name="dq_bank")
+                bank = decode_psum.tile([P, J_TILE], F32, name="decode_bank")
                 nc.tensor.matmul_mx(
                     out=bank[:],
                     lhsT=eye_codes[:, t * P : (t + 1) * P].bitcast(E4M3),
                     lhsT_scale=eye_scales[:, t * P : (t + 1) * P],
-                    rhs=dq_codes[u][:].bitcast(E5M2),
-                    rhs_scale=dq_scales[u][:],
+                    rhs=dq_codes[g, h][:].bitcast(E5M2),
+                    rhs_scale=dq_scales[g, h][:],
                     start=True,
                     stop=True,
                 )
                 banks.append(bank)
             return banks
 
-        def second_tier_early(a, whole_rows):
-            banks = decode((a, 0))
-            left = sb("left%d0" % a, [P, 2, PACK, HALF], BF16)
-            grouped = [sb("dr_grouped%d0%d" % (a, c), [P, HALF, PACK], BF16) for c in range(2)]
-            for t in range(whole_rows):
+        def residual_first_pass():
+            banks = decode(0, 0)
+            left = sb("left00", [P, 2, PACK, HALF], BF16)
+            grouped = [sb("dr_grouped00%d" % c, [P, HALF, PACK], BF16) for c in range(2)]
+            for t in range(WHOLE_ROWS):
                 bank = banks[t][:].rearrange("p (c j) -> p c j", c=2)
-                nc.vector.tensor_tensor(left[:, :, t, :], dy_early[a][:, :, t, :], bank, SUBTRACT)
+                nc.vector.tensor_tensor(left[:, :, t, :], dy_first[0][:, :, t, :], bank, SUBTRACT)
             for c in range(2):
-                for t in range(whole_rows, PACK):
-                    nc.vector.tensor_tensor(left[:, c, t, :], dy_early[a][:, c, t, :], banks[t][:, halves[c]], SUBTRACT)
+                for t in range(WHOLE_ROWS, PACK):
+                    nc.vector.tensor_tensor(left[:, c, t, :], dy_first[0][:, c, t, :], banks[t][:, halves[c]], SUBTRACT)
             for c in range(2):
-                interleave(nc.scalar.copy, grouped[c][:], left[:, c])
-            for c in range(2):
-                quantize(dr_codes[a, 0][:, halves[c]], dr_scales[a, 0][:, halves[c]], grouped[c][:], E4M3)
+                group(nc.scalar.copy, grouped[c][:], left[:, c])
+            return grouped
 
-        def second_tier_last_early():
-            banks = decode((1, 0))
-            pieces = [(0, 0, HALF), (1, 0, HALF // 2), (1, HALF // 2, HALF // 2)]
-            left = [sb("left10%d" % i, [P, PACK, width], BF16) for i, (c, first, width) in enumerate(pieces)]
-            grouped = [sb("dr_grouped10%d" % i, [P, width, PACK], BF16) for i, (c, first, width) in enumerate(pieces)]
-            cols = [slice(c * HALF + first, c * HALF + first + width) for c, first, width in pieces]
-            for i, (c, first, width) in enumerate(pieces):
+        pieces = [slice(0, HALF), slice(HALF, HALF + QUARTER), slice(HALF + QUARTER, J_TILE)]
+
+        def residual_second_pass(first_pass_grouped):
+            banks = decode(1, 0)
+            widths = [cols.stop - cols.start for cols in pieces]
+            left = [sb("left10%d" % i, [P, PACK, widths[i]], BF16, "slot%d" % i) for i in range(len(pieces))]
+            grouped = [sb("dr_grouped10%d" % i, [P, widths[i], PACK], BF16) for i in range(len(pieces))]
+            for i, cols in enumerate(pieces):
+                c, first = divmod(cols.start, HALF)
                 for t in range(PACK):
-                    raw = dy_early[1][:, c, t, first : first + width]
-                    nc.vector.tensor_tensor(left[i][:, t, :], raw, banks[t][:, cols[i]], SUBTRACT)
+                    rows = dy_first[1][:, c, t, first : first + widths[i]]
+                    nc.vector.tensor_tensor(left[i][:, t, :], rows, banks[t][:, cols], SUBTRACT)
             for i in range(len(pieces)):
-                interleave(nc.scalar.copy, grouped[i][:], left[i][:])
-            for i in range(len(pieces)):
-                quantize(dr_codes[1, 0][:, cols[i]], dr_scales[1, 0][:, cols[i]], grouped[i][:], E4M3)
+                group(nc.scalar.copy, grouped[i][:], left[i][:])
+            for c in range(2):
+                quantize(dr_codes[0, 0][:, halves[c]], dr_scales[0, 0][:, halves[c]], first_pass_grouped[c][:], E4M3)
+            for i, cols in enumerate(pieces):
+                quantize(dr_codes[1, 0][:, cols], dr_scales[1, 0][:, cols], grouped[i][:], E4M3)
 
-        def second_tier_late(a, left, on_gpsimd=0):
-            banks = decode((a, 1))
-            grouped = sb("dr_grouped%d1" % a, [P, J_TILE, PACK], BF16)
-            for t in range(on_gpsimd):
+        def residual_second_tile(g, left, gpsimd_rows):
+            banks = decode(g, 1)
+            grouped = sb("dr_grouped%d1" % g, [P, J_TILE, PACK], BF16)
+            for t in range(gpsimd_rows):
                 decoded = sb("decoded%d" % t, [P, J_TILE], F32)
                 nc.scalar.copy(out=decoded[:], in_=banks[t][:])
-                nc.gpsimd.tensor_tensor(left[:, t, :], dy_late[a][:, t, :], decoded[:], SUBTRACT)
-            for t in range(on_gpsimd, PACK):
-                nc.vector.tensor_tensor(left[:, t, :], dy_late[a][:, t, :], banks[t][:], SUBTRACT)
+                nc.gpsimd.tensor_tensor(left[:, t, :], dy_second[g][:, t, :], decoded[:], SUBTRACT)
+            for t in range(gpsimd_rows, PACK):
+                nc.vector.tensor_tensor(left[:, t, :], dy_second[g][:, t, :], banks[t][:], SUBTRACT)
             for cols in halves:
-                interleave(nc.scalar.copy, grouped[:, cols, :], left[:, :, cols])
-            quantize(dr_codes[a, 1][:], dr_scales[a, 1][:], grouped[:], E4M3)
+                group(nc.scalar.copy, grouped[:, cols, :], left[:, :, cols])
+            quantize(dr_codes[g, 1][:], dr_scales[g, 1][:], grouped[:], E4M3)
 
-        def weights(n, raw, copy, slot=None):
+        def weights(n, cast, slot=None):
             grouped = sb("w_grouped%d" % n, [P, PASSES * P, PACK], BF16, slot)
-            for a in range(PASSES):
-                interleave(copy, grouped[:, a * P : (a + 1) * P, :], raw[:, a])
+            for g in range(PASSES):
+                group(cast, grouped[:, g * P : (g + 1) * P, :], w_rows[n][:, g])
             quantize(w_codes[n][:], w_scales[n][:], grouped[:], E4M3)
 
-        def weights_by_pass(n, raw, slots):
-            grouped = [sb("w_grouped%d%d" % (n, a), [P, P, PACK], BF16, slots[a]) for a in range(PASSES)]
-            for a in range(PASSES):
-                interleave(nc.scalar.copy, grouped[a][:], raw[:, a])
-            for a in range(PASSES):
-                cols = slice(a * P, (a + 1) * P)
-                quantize(w_codes[n][:, cols], w_scales[n][:, cols], grouped[a][:], E4M3)
+        def weights_by_pass(n, slots):
+            grouped = [sb("w_grouped%d%d" % (n, g), [P, P, PACK], BF16, slots[g]) for g in range(PASSES)]
+            for g in range(PASSES):
+                group(nc.scalar.copy, grouped[g][:], w_rows[n][:, g])
+            for g in range(PASSES):
+                cols = slice(g * P, (g + 1) * P)
+                quantize(w_codes[n][:, cols], w_scales[n][:, cols], grouped[g][:], E4M3)
 
-        def product(n, h, slot=None):
+        whole = slice(0, J_TILE)
+
+        def product(n, h, slot=None, last_pass=(whole,)):
             dx_sb[n, h] = sb("dx%d%d" % (n, h), [P, J_TILE], F32, slot)
-            acc = dx_psum.tile([P, J_TILE], F32, name="acc")
-            passes = [(a, dq_codes, dq_scales, E5M2) for a in range(PASSES)]
-            passes += [(a, dr_codes, dr_scales, E4M3) for a in range(PASSES)]
-            for i, (a, codes, scales, fmt) in enumerate(passes):
+            acc = product_psum.tile([P, J_TILE], F32, name="acc")
+            steps = [(g, dq_codes, dq_scales, E5M2, whole) for g in range(PASSES)]
+            steps += [(0, dr_codes, dr_scales, E4M3, whole)]
+            steps += [(1, dr_codes, dr_scales, E4M3, cols) for cols in last_pass]
+            for i, (g, codes, scales, fmt, cols) in enumerate(steps):
                 nc.tensor.matmul_mx(
-                    out=acc[:],
-                    lhsT=w_codes[n][:, a * P : (a + 1) * P].bitcast(E4M3),
-                    lhsT_scale=w_scales[n][:, a * P : (a + 1) * P],
-                    rhs=codes[a, h][:].bitcast(fmt),
-                    rhs_scale=scales[a, h][:],
+                    out=acc[:, cols],
+                    lhsT=w_codes[n][:, g * P : (g + 1) * P].bitcast(E4M3),
+                    lhsT_scale=w_scales[n][:, g * P : (g + 1) * P],
+                    rhs=codes[g, h][:, cols].bitcast(fmt),
+                    rhs_scale=scales[g, h][:, cols],
                     start=(i == 0),
-                    stop=(i == len(passes) - 1),
+                    stop=(i == len(steps) - 1),
                 )
             nc.scalar.activation(out=dx_sb[n, h][:], in_=acc[:], func=COPY, scale=ls_sb[:, n : n + 1])
 
         def scatter(n, h):
-            cols = J_TILE // 16
+            cols = J_TILE // LIST_GROUP
             nc.vector.tensor_tensor(
                 windows[n][:].indirect(offsets[:, h * cols : (h + 1) * cols]), dx_sb[n, h][:], wgo_sb[h][:], MULT
             )
 
-        window(0, nc.gpsimd.memset)
-        first_tier_early(0, [scalar_cast, nc.vector.tensor_copy])
-        first_tier_early(1, [scalar_cast, scalar_cast])
-        second_tier_early(0, 2)
-        weights(0, w_raw[0], nc.vector.tensor_copy, "dy_grouped11")
-        second_tier_last_early()
-        nc.vector.transpose(ls_sb[:], ls_rows[:])
-        window(1, nc.vector.memset, "dr_grouped102")
-        weights_by_pass(1, w_raw[1], ["left101", "left102"])
-        product(0, 0)
+        on_scalar = [scalar_cast, scalar_cast]
+        first_halves = [[dy_first[g][:, c] for c in range(2)] for g in range(PASSES)]
+        second_halves = [[dy_second[g][:, :, cols] for cols in halves] for g in range(PASSES)]
+
+        window(0)
+        first_tier(0, 0, first_halves[0], [scalar_cast, nc.vector.tensor_copy], [None, None])
+        first_tier(1, 0, first_halves[1], on_scalar, [None, "slot3"])
+        first_pass_grouped = residual_first_pass()
+        weights(0, nc.vector.tensor_copy, "slot3")
+        window(1, "slot3")
+        residual_second_pass(first_pass_grouped)
+        weights_by_pass(1, ["slot1", "slot2"])
+        product(0, 0, None, pieces)
+        window(2, "slot2")
         scatter(0, 0)
-        late = [sb("late0%d" % i, [P, HALF, PACK], BF16, "left10%d" % i)[:] for i in range(3)]
-        late_pair(0, 2, late[0], late[1:])
+
+        first_tier(0, 1, second_halves[0], on_scalar, ["slot1", "slot0"])
         product(1, 0)
-        window(2, nc.gpsimd.memset, "left102")
         scatter(1, 0)
-        joint = sb("late10", [P, 2, HALF, PACK], BF16, "left100")
-        late_pair(1, 3, joint[:, 0], [joint[:, 1], sb("late11", [P, HALF, PACK], BF16, "left101")[:]])
-        left_late = sb("left_late", [P, PASSES, PACK, J_TILE], BF16, "left101")
-        second_tier_late(0, left_late[:, 0], 2)
-        product(2, 0, "left100")
-        second_tier_late(1, left_late[:, 1])
-        product(3, 0, "left101")
+        first_tier(1, 1, second_halves[1], on_scalar, ["slot1", "slot0"])
+        weights(2, nc.scalar.copy)
+        w_codes.append(sb("w_codes3", [P, PASSES * P], U32, "slot1"))
+        weights(3, nc.scalar.copy, "slot4")
+        left_second = sb("left_second", [P, PASSES, PACK, J_TILE], BF16, "slot0")
+        residual_second_tile(0, left_second[:, 0], GPSIMD_ROWS)
+        product(2, 0, "slot4")
+        residual_second_tile(1, left_second[:, 1], 0)
+        product(3, 0, "slot0")
         scatter(2, 0)
-        window(3, nc.gpsimd.memset, "dy_raw11")
+        window(3, "dy_second1")
         scatter(3, 0)
+
         for n in range(N_TILES):
             product(n, 1)
             scatter(n, 1)

@@ -70,25 +70,26 @@ def tile_list_embg_tgf32_ls_kernel(tc, dy, w, ls, wgo, offs, out):
         wgo_sb = [sb("wgo%d" % h, [P, J_TILE], F32) for h in range(J_TILES)]
         dy_first = [sb("dy_first%d" % g, [P, 2, PACK, HALF], F32) for g in range(PASSES)]
         dy_second = [sb("dy_second%d" % g, [P, PACK, J_TILE], F32) for g in range(PASSES)]
-        w_early = [sb("w_early%d" % n, [P, PASSES, PACK, P], F32) for n in range(2)]
-        w_late = sb("w_late", [P, PASSES, PACK, 2 * P], F32)
-        w_rows = [w_early[0][:], w_early[1][:], w_late[:, :, :, 0:P], w_late[:, :, :, P : 2 * P]]
+        w_first = sb("w_first", [P, PASSES, PACK, P], F32)
+        w_middle = sb("w_middle", [P, PASSES, PACK, 2 * P], F32)
+        w_last = sb("w_last", [P, PASSES, PACK, P], F32)
+        w_rows = [w_first[:], w_middle[:, :, :, 0:P], w_middle[:, :, :, P : 2 * P], w_last[:]]
 
         for g in range(PASSES):
             for c in range(2):
                 nc.sync.dma_start(out=dy_first[g][:, c], in_=k_rows(dy, g, halves[c]))
         for g in range(PASSES):
-            nc.sync.dma_start(out=w_early[0][:, g], in_=k_rows(w, g, slice(0, P)))
+            nc.sync.dma_start(out=w_first[:, g], in_=k_rows(w, g, slice(0, P)))
         nc.sync.dma_start(offsets[:], offs)
         nc.sync.dma_start(out=wgo_sb[0][:], in_=wgo[:, 0:J_TILE])
+        for g in range(PASSES):
+            nc.sync.dma_start(out=w_middle[:, g], in_=k_rows(w, g, slice(P, 3 * P)))
         with nc.allow_non_contiguous_dma(reason="one factor for each partition and n tile"):
             nc.sync.dma_start(out=ls_sb[:], in_=ls.rearrange("(c p) -> p c", p=P))
         for g in range(PASSES):
-            nc.sync.dma_start(out=w_early[1][:, g], in_=k_rows(w, g, slice(P, 2 * P)))
-        nc.sync.dma_start(out=dy_second[0][:], in_=k_rows(dy, 0, slice(J_TILE, J)))
+            nc.sync.dma_start(out=dy_second[g][:], in_=k_rows(dy, g, slice(J_TILE, J)))
         for g in range(PASSES):
-            nc.sync.dma_start(out=w_late[:, g], in_=k_rows(w, g, slice(2 * P, N)))
-        nc.sync.dma_start(out=dy_second[1][:], in_=k_rows(dy, 1, slice(J_TILE, J)))
+            nc.sync.dma_start(out=w_last[:, g], in_=k_rows(w, g, slice(3 * P, N)))
         nc.sync.dma_start(out=wgo_sb[1][:], in_=wgo[:, J_TILE:J])
 
         ones = sb("ones", [P, QUAD + 1], F32)
@@ -113,9 +114,9 @@ def tile_list_embg_tgf32_ls_kernel(tc, dy, w, ls, wgo, offs, out):
 
         dq_codes = {u: sb("dq_codes%d%d" % u, [P, J_TILE], U32) for u in units}
         dq_scales = {u: sb("dq_scales%d%d" % u, [P, J_TILE], U8) for u in units}
-        dr_codes = {u: sb("dr_codes%d%d" % u, [P, J_TILE], U32) for u in units}
+        dr_codes = {u: sb("dr_codes%d%d" % u, [P, J_TILE], U32) for u in units[1:]}
         dr_scales = {u: sb("dr_scales%d%d" % u, [P, J_TILE], U8) for u in units}
-        w_codes = [sb("w_codes%d" % n, [P, PASSES * P], U32) for n in range(N_TILES - 1)]
+        w_codes = {}
         w_scales = [sb("w_scales%d" % n, [P, PASSES * P], U8) for n in range(N_TILES)]
         dx_sb = {}
         windows = {}
@@ -163,10 +164,10 @@ def tile_list_embg_tgf32_ls_kernel(tc, dy, w, ls, wgo, offs, out):
 
         pieces = [slice(0, HALF), slice(HALF, HALF + QUARTER), slice(HALF + QUARTER, J_TILE)]
 
-        def residual_second_pass(first_pass_grouped):
+        def residual_second_pass():
             banks = decode(1, 0)
             widths = [cols.stop - cols.start for cols in pieces]
-            left = [sb("left10%d" % i, [P, PACK, widths[i]], BF16, "slot%d" % i) for i in range(len(pieces))]
+            left = [sb("left10%d" % i, [P, PACK, widths[i]], BF16) for i in range(len(pieces))]
             grouped = [sb("dr_grouped10%d" % i, [P, widths[i], PACK], BF16) for i in range(len(pieces))]
             for i, cols in enumerate(pieces):
                 c, first = divmod(cols.start, HALF)
@@ -175,37 +176,22 @@ def tile_list_embg_tgf32_ls_kernel(tc, dy, w, ls, wgo, offs, out):
                     nc.vector.tensor_tensor(left[i][:, t, :], rows, banks[t][:, cols], SUBTRACT)
             for i in range(len(pieces)):
                 group(nc.scalar.copy, grouped[i][:], left[i][:])
-            for c in range(2):
-                quantize(dr_codes[0, 0][:, halves[c]], dr_scales[0, 0][:, halves[c]], first_pass_grouped[c][:], E4M3)
-            for i, cols in enumerate(pieces):
-                quantize(dr_codes[1, 0][:, cols], dr_scales[1, 0][:, cols], grouped[i][:], E4M3)
+            return grouped
 
-        def residual_second_tile(g, left, gpsimd_rows):
-            banks = decode(g, 1)
-            grouped = sb("dr_grouped%d1" % g, [P, J_TILE, PACK], BF16)
-            for t in range(gpsimd_rows):
-                decoded = sb("decoded%d" % t, [P, J_TILE], F32)
-                nc.scalar.copy(out=decoded[:], in_=banks[t][:])
-                nc.gpsimd.tensor_tensor(left[:, t, :], dy_second[g][:, t, :], decoded[:], SUBTRACT)
-            for t in range(gpsimd_rows, PACK):
-                nc.vector.tensor_tensor(left[:, t, :], dy_second[g][:, t, :], banks[t][:], SUBTRACT)
-            for cols in halves:
-                group(nc.scalar.copy, grouped[:, cols, :], left[:, :, cols])
-            quantize(dr_codes[g, 1][:], dr_scales[g, 1][:], grouped[:], E4M3)
+        def first_tier_whole(g, slot=None):
+            grouped = sb("dy_grouped%d1" % g, [P, J_TILE, PACK], BF16, slot)
+            group(scalar_cast, grouped[:], dy_second[g][:])
+            quantize(dq_codes[g, 1][:], dq_scales[g, 1][:], grouped[:], E5M2)
 
-        def weights(n, cast, slot=None):
+        def group_weights(n, cast, slot=None):
             grouped = sb("w_grouped%d" % n, [P, PASSES * P, PACK], BF16, slot)
             for g in range(PASSES):
                 group(cast, grouped[:, g * P : (g + 1) * P, :], w_rows[n][:, g])
-            quantize(w_codes[n][:], w_scales[n][:], grouped[:], E4M3)
+            return grouped
 
-        def weights_by_pass(n, slots):
-            grouped = [sb("w_grouped%d%d" % (n, g), [P, P, PACK], BF16, slots[g]) for g in range(PASSES)]
-            for g in range(PASSES):
-                group(nc.scalar.copy, grouped[g][:], w_rows[n][:, g])
-            for g in range(PASSES):
-                cols = slice(g * P, (g + 1) * P)
-                quantize(w_codes[n][:, cols], w_scales[n][:, cols], grouped[g][:], E4M3)
+        def quantize_weights(n, grouped, slot=None):
+            w_codes[n] = sb("w_codes%d" % n, [P, PASSES * P], U32, slot)
+            quantize(w_codes[n][:], w_scales[n][:], grouped[:], E4M3)
 
         whole = slice(0, J_TILE)
 
@@ -235,34 +221,67 @@ def tile_list_embg_tgf32_ls_kernel(tc, dy, w, ls, wgo, offs, out):
 
         on_scalar = [scalar_cast, scalar_cast]
         first_halves = [[dy_first[g][:, c] for c in range(2)] for g in range(PASSES)]
-        second_halves = [[dy_second[g][:, :, cols] for cols in halves] for g in range(PASSES)]
 
         window(0)
         first_tier(0, 0, first_halves[0], [scalar_cast, nc.vector.tensor_copy], [None, None])
-        first_tier(1, 0, first_halves[1], on_scalar, [None, "slot3"])
+        first_tier(1, 0, first_halves[1], on_scalar, [None, "slot_w0"])
         first_pass_grouped = residual_first_pass()
-        weights(0, nc.vector.tensor_copy, "slot3")
-        window(1, "slot3")
-        residual_second_pass(first_pass_grouped)
-        weights_by_pass(1, ["slot1", "slot2"])
+        w0_grouped = sb("w_grouped0", [P, PASSES * P, PACK], BF16, "slot_w0")
+        nc.gpsimd.tensor_scalar(
+            w0_grouped[:].rearrange("p (g c) t -> p g c t", g=PASSES),
+            w_rows[0].rearrange("p g t c -> p g c t"),
+            1.0,
+            0.0,
+            MULT,
+            ADD,
+        )
+        second_pass_grouped = residual_second_pass()
+        quantize_weights(0, w0_grouped)
+        dr_codes[0, 0] = sb("dr_codes00", [P, J_TILE], U32, "slot_w0")
+        for c in range(2):
+            quantize(dr_codes[0, 0][:, halves[c]], dr_scales[0, 0][:, halves[c]], first_pass_grouped[c][:], E4M3)
+        for i, cols in enumerate(pieces):
+            quantize(dr_codes[1, 0][:, cols], dr_scales[1, 0][:, cols], second_pass_grouped[i][:], E4M3)
         product(0, 0, None, pieces)
-        window(2, "slot2")
+        w1_grouped = [sb("w_grouped1%d" % g, [P, P, PACK], BF16, ["dr_grouped102", "dr_grouped101"][g]) for g in range(PASSES)]
+        w_codes[1] = sb("w_codes1", [P, PASSES * P], U32)
+        for g in range(PASSES):
+            group(nc.vector.tensor_copy, w1_grouped[g][:], w_rows[1][:, g])
+        for g in range(PASSES):
+            cols = slice(g * P, (g + 1) * P)
+            quantize(w_codes[1][:, cols], w_scales[1][:, cols], w1_grouped[g][:], E4M3)
+        window(1, "dr_grouped101")
         scatter(0, 0)
 
-        first_tier(0, 1, second_halves[0], on_scalar, ["slot1", "slot0"])
+        quantize_weights(2, group_weights(2, nc.scalar.copy, "dr_grouped102"))
+        first_tier_whole(0)
         product(1, 0)
+        window(2, "dy_grouped01")
         scatter(1, 0)
-        first_tier(1, 1, second_halves[1], on_scalar, ["slot1", "slot0"])
-        weights(2, nc.scalar.copy)
-        w_codes.append(sb("w_codes3", [P, PASSES * P], U32, "slot1"))
-        weights(3, nc.scalar.copy, "slot4")
-        left_second = sb("left_second", [P, PASSES, PACK, J_TILE], BF16, "slot0")
-        residual_second_tile(0, left_second[:, 0], GPSIMD_ROWS)
-        product(2, 0, "slot4")
-        residual_second_tile(1, left_second[:, 1], 0)
-        product(3, 0, "slot0")
+
+        first_tier_whole(1)
+        banks = decode(0, 1)
+        decoded = sb("decoded", [P, GPSIMD_ROWS, J_TILE], F32)
+        for t in range(GPSIMD_ROWS):
+            nc.scalar.copy(out=decoded[:, t, :], in_=banks[t][:])
+        product(2, 0)
+        w3_grouped = group_weights(3, nc.scalar.copy)
+        left = sb("left_second", [P, PASSES, PACK, J_TILE], BF16, "dy_grouped11")
+        for t in range(GPSIMD_ROWS):
+            nc.gpsimd.tensor_tensor(left[:, 0, t, :], dy_second[0][:, t, :], decoded[:, t, :], SUBTRACT)
+        for t in range(GPSIMD_ROWS, PACK):
+            nc.vector.tensor_tensor(left[:, 0, t, :], dy_second[0][:, t, :], banks[t][:], SUBTRACT)
+        banks = decode(1, 1)
+        for t in range(PACK):
+            nc.vector.tensor_tensor(left[:, 1, t, :], dy_second[1][:, t, :], banks[t][:], SUBTRACT)
+        quantize_weights(3, w3_grouped, "decoded")
+        window(3, "w_grouped3")
         scatter(2, 0)
-        window(3, "dy_second1")
+        for g in range(PASSES):
+            grouped = sb("dr_grouped%d1" % g, [P, J_TILE, PACK], BF16)
+            group(nc.scalar.copy, grouped[:], left[:, g])
+            quantize(dr_codes[g, 1][:], dr_scales[g, 1][:], grouped[:], E4M3)
+        product(3, 0, "dy_grouped11")
         scatter(3, 0)
 
         for n in range(N_TILES):

@@ -35,6 +35,7 @@ DECODE_BANKS = 6
 PRODUCT_BANKS = 2
 WHOLE_ROWS = 2
 GPSIMD_ROWS = 2
+VECTOR_SHARE = 160
 
 
 def tile_list_embg_tgf32_ls_kernel(tc, dy, w, ls, wgo, offs, out):
@@ -80,10 +81,10 @@ def tile_list_embg_tgf32_ls_kernel(tc, dy, w, ls, wgo, offs, out):
                 nc.sync.dma_start(out=dy_first[g][:, c], in_=k_rows(dy, g, halves[c]))
         for g in range(PASSES):
             nc.sync.dma_start(out=w_first[:, g], in_=k_rows(w, g, slice(0, P)))
-        nc.sync.dma_start(offsets[:], offs)
-        nc.sync.dma_start(out=wgo_sb[0][:], in_=wgo[:, 0:J_TILE])
         for g in range(PASSES):
             nc.sync.dma_start(out=w_middle[:, g], in_=k_rows(w, g, slice(P, 3 * P)))
+        nc.sync.dma_start(offsets[:], offs)
+        nc.sync.dma_start(out=wgo_sb[0][:], in_=wgo[:, 0:J_TILE])
         with nc.allow_non_contiguous_dma(reason="one factor for each partition and n tile"):
             nc.sync.dma_start(out=ls_sb[:], in_=ls.rearrange("(c p) -> p c", p=P))
         for g in range(PASSES):
@@ -118,17 +119,18 @@ def tile_list_embg_tgf32_ls_kernel(tc, dy, w, ls, wgo, offs, out):
         dr_scales = {u: sb("dr_scales%d%d" % u, [P, J_TILE], U8) for u in units}
         w_codes = {}
         w_scales = [sb("w_scales%d" % n, [P, PASSES * P], U8) for n in range(N_TILES)]
-        dx_sb = {}
         windows = {}
 
         def window(n, slot=None):
             windows[n] = sb("window%d" % n, [P, T], F32, slot)
             nc.gpsimd.memset(windows[n][:].bitcast(U32), 0)
 
-        def first_tier(g, h, rows, casts, slots):
-            grouped = [sb("dy_grouped%d%d%d" % (g, h, c), [P, HALF, PACK], BF16, slots[c]) for c in range(2)]
-            for c in range(2):
-                group(casts[c], grouped[c][:], rows[c])
+        def first_tier(g, h, rows, vector_columns=0, slot=None):
+            grouped = [sb("dy_grouped%d%d%d" % (g, h, c), [P, HALF, PACK], BF16, [None, slot][c]) for c in range(2)]
+            group(scalar_cast, grouped[0][:], rows[0])
+            if vector_columns:
+                group(nc.vector.tensor_copy, grouped[1][:, 0:vector_columns, :], rows[1][:, :, 0:vector_columns])
+            group(scalar_cast, grouped[1][:, vector_columns:HALF, :], rows[1][:, :, vector_columns:HALF])
             for c in range(2):
                 quantize(dq_codes[g, h][:, halves[c]], dq_scales[g, h][:, halves[c]], grouped[c][:], E5M2)
 
@@ -178,15 +180,10 @@ def tile_list_embg_tgf32_ls_kernel(tc, dy, w, ls, wgo, offs, out):
                 group(nc.scalar.copy, grouped[i][:], left[i][:])
             return grouped
 
-        def first_tier_whole(g, slot=None):
-            grouped = sb("dy_grouped%d1" % g, [P, J_TILE, PACK], BF16, slot)
-            group(scalar_cast, grouped[:], dy_second[g][:])
-            quantize(dq_codes[g, 1][:], dq_scales[g, 1][:], grouped[:], E5M2)
-
-        def group_weights(n, cast, slot=None):
+        def group_weights(n, slot=None):
             grouped = sb("w_grouped%d" % n, [P, PASSES * P, PACK], BF16, slot)
             for g in range(PASSES):
-                group(cast, grouped[:, g * P : (g + 1) * P, :], w_rows[n][:, g])
+                group(nc.scalar.copy, grouped[:, g * P : (g + 1) * P, :], w_rows[n][:, g])
             return grouped
 
         def quantize_weights(n, grouped, slot=None):
@@ -195,8 +192,7 @@ def tile_list_embg_tgf32_ls_kernel(tc, dy, w, ls, wgo, offs, out):
 
         whole = slice(0, J_TILE)
 
-        def product(n, h, slot=None, last_pass=(whole,)):
-            dx_sb[n, h] = sb("dx%d%d" % (n, h), [P, J_TILE], F32, slot)
+        def accumulate(n, h, last_pass=(whole,)):
             acc = product_psum.tile([P, J_TILE], F32, name="acc")
             steps = [(g, dq_codes, dq_scales, E5M2, whole) for g in range(PASSES)]
             steps += [(0, dr_codes, dr_scales, E4M3, whole)]
@@ -211,22 +207,23 @@ def tile_list_embg_tgf32_ls_kernel(tc, dy, w, ls, wgo, offs, out):
                     start=(i == 0),
                     stop=(i == len(steps) - 1),
                 )
-            nc.scalar.activation(out=dx_sb[n, h][:], in_=acc[:], func=COPY, scale=ls_sb[:, n : n + 1])
+            return acc
 
-        def scatter(n, h):
-            cols = J_TILE // LIST_GROUP
-            nc.vector.tensor_tensor(
-                windows[n][:].indirect(offsets[:, h * cols : (h + 1) * cols]), dx_sb[n, h][:], wgo_sb[h][:], MULT
-            )
+        def scaled(acc, n, h, cols=whole, slot=None):
+            dx = sb("dx%d%d_%d" % (n, h, cols.start), [P, cols.stop - cols.start], F32, slot)
+            nc.scalar.activation(out=dx[:], in_=acc[:, cols], func=COPY, scale=ls_sb[:, n : n + 1])
+            return dx
 
-        on_scalar = [scalar_cast, scalar_cast]
-        first_halves = [[dy_first[g][:, c] for c in range(2)] for g in range(PASSES)]
+        def scatter(n, h, dx, cols=whole):
+            first = h * J_TILE
+            lists = offsets[:, (first + cols.start) // LIST_GROUP : (first + cols.stop) // LIST_GROUP]
+            nc.vector.tensor_tensor(windows[n][:].indirect(lists), dx[:], wgo_sb[h][:, cols], MULT)
 
         window(0)
-        first_tier(0, 0, first_halves[0], [scalar_cast, nc.vector.tensor_copy], [None, None])
-        first_tier(1, 0, first_halves[1], on_scalar, [None, "slot_w0"])
+        first_tier(0, 0, [dy_first[0][:, c] for c in range(2)], VECTOR_SHARE)
+        first_tier(1, 0, [dy_first[1][:, c] for c in range(2)], 0, "after_pass_1")
         first_pass_grouped = residual_first_pass()
-        w0_grouped = sb("w_grouped0", [P, PASSES * P, PACK], BF16, "slot_w0")
+        w0_grouped = sb("w_grouped0", [P, PASSES * P, PACK], BF16, "after_pass_1")
         nc.gpsimd.tensor_scalar(
             w0_grouped[:].rearrange("p (g c) t -> p g c t", g=PASSES),
             w_rows[0].rearrange("p g t c -> p g c t"),
@@ -237,36 +234,50 @@ def tile_list_embg_tgf32_ls_kernel(tc, dy, w, ls, wgo, offs, out):
         )
         second_pass_grouped = residual_second_pass()
         quantize_weights(0, w0_grouped)
-        dr_codes[0, 0] = sb("dr_codes00", [P, J_TILE], U32, "slot_w0")
+        dr_codes[0, 0] = sb("dr_codes00", [P, J_TILE], U32, "w_first")
         for c in range(2):
             quantize(dr_codes[0, 0][:, halves[c]], dr_scales[0, 0][:, halves[c]], first_pass_grouped[c][:], E4M3)
         for i, cols in enumerate(pieces):
             quantize(dr_codes[1, 0][:, cols], dr_scales[1, 0][:, cols], second_pass_grouped[i][:], E4M3)
-        product(0, 0, None, pieces)
-        w1_grouped = [sb("w_grouped1%d" % g, [P, P, PACK], BF16, ["dr_grouped102", "dr_grouped101"][g]) for g in range(PASSES)]
+        dx = scaled(accumulate(0, 0, pieces), 0, 0)
+        w1_grouped = [sb("w_grouped1%d" % g, [P, P, PACK], BF16, "left10%d" % (g + 1)) for g in range(PASSES)]
         w_codes[1] = sb("w_codes1", [P, PASSES * P], U32)
         for g in range(PASSES):
-            group(nc.vector.tensor_copy, w1_grouped[g][:], w_rows[1][:, g])
+            group(nc.scalar.copy, w1_grouped[g][:], w_rows[1][:, g])
         for g in range(PASSES):
             cols = slice(g * P, (g + 1) * P)
             quantize(w_codes[1][:, cols], w_scales[1][:, cols], w1_grouped[g][:], E4M3)
-        window(1, "dr_grouped101")
-        scatter(0, 0)
+        window(1, "left102")
+        scatter(0, 0, dx)
 
-        quantize_weights(2, group_weights(2, nc.scalar.copy, "dr_grouped102"))
-        first_tier_whole(0)
-        product(1, 0)
-        window(2, "dy_grouped01")
-        scatter(1, 0)
+        w2_grouped = group_weights(2, "left101")
+        parts = [slice(0, QUARTER), slice(QUARTER, HALF), halves[1]]
+        part_slots = [None, None, "w_middle"]
+        grouped = [
+            sb("dy_grouped01%d" % i, [P, cols.stop - cols.start, PACK], BF16, part_slots[i])
+            for i, cols in enumerate(parts)
+        ]
+        for i in (2, 0, 1):
+            group(scalar_cast, grouped[i][:], dy_second[0][:, :, parts[i]])
+        for i, cols in enumerate(parts):
+            quantize(dq_codes[0, 1][:, cols], dq_scales[0, 1][:, cols], grouped[i][:], E5M2)
+        quantize_weights(2, w2_grouped, "dy_grouped011")
+        acc = accumulate(1, 0)
+        window(2, "left101")
+        rest = slice(QUARTER, J_TILE)
+        dx_rest = scaled(acc, 1, 0, rest)
+        dx_quarter = scaled(acc, 1, 0, parts[0], "dy_grouped010")
+        scatter(1, 0, dx_quarter, parts[0])
+        scatter(1, 0, dx_rest, rest)
 
-        first_tier_whole(1)
+        first_tier(1, 1, [dy_second[1][:, :, cols] for cols in halves])
         banks = decode(0, 1)
         decoded = sb("decoded", [P, GPSIMD_ROWS, J_TILE], F32)
         for t in range(GPSIMD_ROWS):
             nc.scalar.copy(out=decoded[:, t, :], in_=banks[t][:])
-        product(2, 0)
-        w3_grouped = group_weights(3, nc.scalar.copy)
-        left = sb("left_second", [P, PASSES, PACK, J_TILE], BF16, "dy_grouped11")
+        dx = scaled(accumulate(2, 0), 2, 0)
+        w3_grouped = group_weights(3)
+        left = sb("left_second", [P, PASSES, PACK, J_TILE], BF16, "dy_grouped110")
         for t in range(GPSIMD_ROWS):
             nc.gpsimd.tensor_tensor(left[:, 0, t, :], dy_second[0][:, t, :], decoded[:, t, :], SUBTRACT)
         for t in range(GPSIMD_ROWS, PACK):
@@ -276,15 +287,13 @@ def tile_list_embg_tgf32_ls_kernel(tc, dy, w, ls, wgo, offs, out):
             nc.vector.tensor_tensor(left[:, 1, t, :], dy_second[1][:, t, :], banks[t][:], SUBTRACT)
         quantize_weights(3, w3_grouped, "decoded")
         window(3, "w_grouped3")
-        scatter(2, 0)
+        scatter(2, 0, dx)
         for g in range(PASSES):
             grouped = sb("dr_grouped%d1" % g, [P, J_TILE, PACK], BF16)
             group(nc.scalar.copy, grouped[:], left[:, g])
             quantize(dr_codes[g, 1][:], dr_scales[g, 1][:], grouped[:], E4M3)
-        product(3, 0, "dy_grouped11")
-        scatter(3, 0)
+        scatter(3, 0, scaled(accumulate(3, 0), 3, 0, whole, "dy_grouped110"))
 
         for n in range(N_TILES):
-            product(n, 1)
-            scatter(n, 1)
+            scatter(n, 1, scaled(accumulate(n, 1), n, 1))
             nc.sync.dma_start(out=out[n * P : (n + 1) * P, :], in_=windows[n][:])

@@ -30,7 +30,7 @@ N_TILES = N // P
 LIST_GROUP = 16
 RUN = 4
 QUAD = 32
-EYE_WIDTH = PACK * (K_PASS + P)
+STRIP = K_PASS + 1
 DECODE_BANKS = 6
 PRODUCT_BANKS = 2
 WHOLE_ROWS = 2
@@ -42,7 +42,7 @@ def tile_list_embg_tgf32_ls_kernel(tc, dy, w, ls, wgo, offs, out):
     nc = tc.nc
     with ExitStack() as ctx:
         keep = ctx.enter_context(tc.tile_pool(name="keep", bufs=1))
-        decode_psum = ctx.enter_context(tc.psum_pool(name="decode_psum", bufs=DECODE_BANKS))
+        decode_psum = ctx.enter_context(tc.psum_pool(name="decode_psum", bufs=1))
         product_psum = ctx.enter_context(tc.psum_pool(name="product_psum", bufs=PRODUCT_BANKS))
 
         def sb(name, shape, dtype, slot=None):
@@ -72,9 +72,8 @@ def tile_list_embg_tgf32_ls_kernel(tc, dy, w, ls, wgo, offs, out):
         dy_first = [sb("dy_first%d" % g, [P, 2, PACK, HALF], F32) for g in range(PASSES)]
         dy_second = [sb("dy_second%d" % g, [P, PACK, J_TILE], F32) for g in range(PASSES)]
         w_first = sb("w_first", [P, PASSES, PACK, P], F32)
-        w_middle = sb("w_middle", [P, PASSES, PACK, 2 * P], F32)
-        w_last = sb("w_last", [P, PASSES, PACK, P], F32)
-        w_rows = [w_first[:], w_middle[:, :, :, 0:P], w_middle[:, :, :, P : 2 * P], w_last[:]]
+        w_rest = sb("w_rest", [P, PASSES, PACK, N - P], F32)
+        w_rows = [w_first[:]] + [w_rest[:, :, :, n * P : (n + 1) * P] for n in range(N_TILES - 1)]
 
         for g in range(PASSES):
             for c in range(2):
@@ -82,36 +81,50 @@ def tile_list_embg_tgf32_ls_kernel(tc, dy, w, ls, wgo, offs, out):
         for g in range(PASSES):
             nc.sync.dma_start(out=w_first[:, g], in_=k_rows(w, g, slice(0, P)))
         for g in range(PASSES):
-            nc.sync.dma_start(out=w_middle[:, g], in_=k_rows(w, g, slice(P, 3 * P)))
+            nc.sync.dma_start(out=w_rest[:, g], in_=k_rows(w, g, slice(P, N)))
         nc.sync.dma_start(offsets[:], offs)
         nc.sync.dma_start(out=wgo_sb[0][:], in_=wgo[:, 0:J_TILE])
         with nc.allow_non_contiguous_dma(reason="one factor for each partition and n tile"):
             nc.sync.dma_start(out=ls_sb[:], in_=ls.rearrange("(c p) -> p c", p=P))
-        for g in range(PASSES):
-            nc.sync.dma_start(out=dy_second[g][:], in_=k_rows(dy, g, slice(J_TILE, J)))
-        for g in range(PASSES):
-            nc.sync.dma_start(out=w_last[:, g], in_=k_rows(w, g, slice(3 * P, N)))
+        nc.sync.dma_start(out=dy_second[0][:], in_=k_rows(dy, 0, slice(J_TILE, J)))
+        nc.sync.dma_start(out=dy_second[1][:], in_=k_rows(dy, 1, slice(J_TILE, J)))
         nc.sync.dma_start(out=wgo_sb[1][:], in_=wgo[:, J_TILE:J])
 
         ones = sb("ones", [P, QUAD + 1], F32)
         nc.vector.memset(ones[:], 1.0)
-        eye = sb("eye", [P, EYE_WIDTH], BF16)
-        nc.vector.memset(eye[:, 0 : PACK * K_PASS + 2].bitcast(U32), 0)
         column = sb("column", [P, QUAD], F32)
         nc.vector.tensor_tensor_scan(column[:], ones[:, 0:QUAD], ones[:, 0:QUAD], 0.0, MULT, ADD)
         row = sb("row", [P, QUAD], F32)
         nc.vector.transpose(row[:], column[:])
-        diagonal = sb("diagonal", [P, QUAD], BF16)
-        nc.vector.tensor_tensor(diagonal[:], column[:], row[:], IS_EQUAL)
+        strip = sb("strip", [P, STRIP + 1], BF16)
+        nc.vector.memset(strip[:].bitcast(U32), 0)
         for b in range(P // QUAD):
             parts = slice(b * QUAD, (b + 1) * QUAD)
-            run = eye[parts, b * P : b * P + PACK * (K_PASS + 1)].rearrange("p (t x) -> p t x", t=PACK)
-            nc.vector.tensor_copy(
-                out=run[:, :, 0:P:PACK], in_=diagonal[parts, :].unsqueeze(1).to_broadcast([QUAD, PACK, QUAD])
-            )
+            nc.vector.tensor_tensor(strip[parts, b * P : (b + 1) * P : PACK], column[parts, :], row[parts, :], IS_EQUAL)
+        eye = sb("eye", [P, PACK * STRIP], BF16)
         eye_codes = sb("eye_codes", [P, PACK * P], U32)
         eye_scales = sb("eye_scales", [P, PACK * P], U8)
-        nc.vector.quantize_mx(out=eye_codes[:].bitcast(E4M3), scales=eye_scales[:], in_=eye[:, 0 : PACK * K_PASS])
+        for c in range(2):
+            nc.vector.tensor_copy(
+                out=eye[:, 2 * c * STRIP : 2 * (c + 1) * STRIP].rearrange("p (t x) -> p t x", t=2),
+                in_=strip[:, 0:STRIP].unsqueeze(1).to_broadcast([P, 2, STRIP]),
+            )
+        for c in range(2):
+            words = slice(c * HALF, (c + 1) * HALF)
+            values = eye[:, PACK * words.start : PACK * words.stop]
+            nc.vector.quantize_mx(out=eye_codes[:, words].bitcast(E4M3), scales=eye_scales[:, words], in_=values)
+
+        for i in range(3):
+            idle = product_psum.tile([P, J_TILE], F32, name="acc")
+            nc.tensor.matmul_mx(
+                out=idle[:],
+                lhsT=eye_codes[:, 0:P].bitcast(E4M3),
+                lhsT_scale=eye_scales[:, 0:P],
+                rhs=eye_codes[:].bitcast(E4M3),
+                rhs_scale=eye_scales[:],
+                start=True,
+                stop=True,
+            )
 
         dq_codes = {u: sb("dq_codes%d%d" % u, [P, J_TILE], U32) for u in units}
         dq_scales = {u: sb("dq_scales%d%d" % u, [P, J_TILE], U8) for u in units}
@@ -137,7 +150,8 @@ def tile_list_embg_tgf32_ls_kernel(tc, dy, w, ls, wgo, offs, out):
         def decode(g, h):
             banks = []
             for t in range(PACK):
-                bank = decode_psum.tile([P, J_TILE], F32, name="decode_bank")
+                turn = PACK * units.index((g, h)) + t
+                bank = decode_psum.tile([P, J_TILE], F32, name="decode_bank", tag="bank%d" % (turn % DECODE_BANKS))
                 nc.tensor.matmul_mx(
                     out=bank[:],
                     lhsT=eye_codes[:, t * P : (t + 1) * P].bitcast(E4M3),
@@ -160,9 +174,8 @@ def tile_list_embg_tgf32_ls_kernel(tc, dy, w, ls, wgo, offs, out):
             for c in range(2):
                 for t in range(WHOLE_ROWS, PACK):
                     nc.vector.tensor_tensor(left[:, c, t, :], dy_first[0][:, c, t, :], banks[t][:, halves[c]], SUBTRACT)
-            for c in range(2):
-                group(nc.scalar.copy, grouped[c][:], left[:, c])
-            return grouped
+            group(nc.scalar.copy, grouped[0][:], left[:, 0])
+            return grouped, left
 
         pieces = [slice(0, HALF), slice(HALF, HALF + QUARTER), slice(HALF + QUARTER, J_TILE)]
 
@@ -222,7 +235,7 @@ def tile_list_embg_tgf32_ls_kernel(tc, dy, w, ls, wgo, offs, out):
         window(0)
         first_tier(0, 0, [dy_first[0][:, c] for c in range(2)], VECTOR_SHARE)
         first_tier(1, 0, [dy_first[1][:, c] for c in range(2)], 0, "after_pass_1")
-        first_pass_grouped = residual_first_pass()
+        first_pass_grouped, first_pass_left = residual_first_pass()
         w0_grouped = sb("w_grouped0", [P, PASSES * P, PACK], BF16, "after_pass_1")
         nc.gpsimd.tensor_scalar(
             w0_grouped[:].rearrange("p (g c) t -> p g c t", g=PASSES),
@@ -231,6 +244,9 @@ def tile_list_embg_tgf32_ls_kernel(tc, dy, w, ls, wgo, offs, out):
             0.0,
             MULT,
             ADD,
+        )
+        nc.gpsimd.tensor_scalar(
+            first_pass_grouped[1][:], first_pass_left[:, 1].rearrange("p t c -> p c t"), 1.0, 0.0, MULT, ADD
         )
         second_pass_grouped = residual_second_pass()
         quantize_weights(0, w0_grouped)
@@ -252,7 +268,7 @@ def tile_list_embg_tgf32_ls_kernel(tc, dy, w, ls, wgo, offs, out):
 
         w2_grouped = group_weights(2, "left101")
         parts = [slice(0, QUARTER), slice(QUARTER, HALF), halves[1]]
-        part_slots = [None, None, "w_middle"]
+        part_slots = [None, None, "left100"]
         grouped = [
             sb("dy_grouped01%d" % i, [P, cols.stop - cols.start, PACK], BF16, part_slots[i])
             for i, cols in enumerate(parts)
@@ -264,35 +280,45 @@ def tile_list_embg_tgf32_ls_kernel(tc, dy, w, ls, wgo, offs, out):
         quantize_weights(2, w2_grouped, "dy_grouped011")
         acc = accumulate(1, 0)
         window(2, "left101")
-        rest = slice(QUARTER, J_TILE)
-        dx_rest = scaled(acc, 1, 0, rest)
-        dx_quarter = scaled(acc, 1, 0, parts[0], "dy_grouped010")
-        scatter(1, 0, dx_quarter, parts[0])
-        scatter(1, 0, dx_rest, rest)
+        scatter(1, 0, scaled(acc, 1, 0, whole, "dy_grouped010"))
 
-        first_tier(1, 1, [dy_second[1][:, :, cols] for cols in halves])
+        w3_grouped = [sb("w_grouped3%d" % g, [P, P, PACK], BF16) for g in range(PASSES)]
+        for g in range(PASSES):
+            group(nc.scalar.copy, w3_grouped[g][:], w_rows[3][:, g])
+        grouped = sb("dy_grouped11", [P, J_TILE, PACK], BF16)
+        for cols in halves:
+            group(scalar_cast, grouped[:, cols, :], dy_second[1][:, :, cols])
+        quantize(dq_codes[1, 1][:], dq_scales[1, 1][:], grouped[:], E5M2)
+        w_codes[3] = sb("w_codes3", [P, PASSES * P], U32, "dy_grouped11")
+        for g in range(PASSES):
+            cols = slice(g * P, (g + 1) * P)
+            quantize(w_codes[3][:, cols], w_scales[3][:, cols], w3_grouped[g][:], E4M3)
         banks = decode(0, 1)
-        decoded = sb("decoded", [P, GPSIMD_ROWS, J_TILE], F32)
-        for t in range(GPSIMD_ROWS):
+        decoded = sb("decoded", [P, 2, J_TILE], F32)
+        decoded_half = sb("decoded_half", [P, HALF], F32)
+        left = [sb("left%d1" % g, [P, PACK, J_TILE], BF16, ["w_grouped30", None][g]) for g in range(PASSES)]
+        for t in range(2):
             nc.scalar.copy(out=decoded[:, t, :], in_=banks[t][:])
         dx = scaled(accumulate(2, 0), 2, 0)
-        w3_grouped = group_weights(3)
-        left = sb("left_second", [P, PASSES, PACK, J_TILE], BF16, "dy_grouped110")
-        for t in range(GPSIMD_ROWS):
-            nc.gpsimd.tensor_tensor(left[:, 0, t, :], dy_second[0][:, t, :], decoded[:, t, :], SUBTRACT)
-        for t in range(GPSIMD_ROWS, PACK):
-            nc.vector.tensor_tensor(left[:, 0, t, :], dy_second[0][:, t, :], banks[t][:], SUBTRACT)
+        for t in range(2):
+            nc.gpsimd.tensor_tensor(left[0][:, t, :], dy_second[0][:, t, :], decoded[:, t, :], SUBTRACT)
+        for t in range(2, PACK):
+            nc.vector.tensor_tensor(left[0][:, t, :], dy_second[0][:, t, :], banks[t][:], SUBTRACT)
         banks = decode(1, 1)
-        for t in range(PACK):
-            nc.vector.tensor_tensor(left[:, 1, t, :], dy_second[1][:, t, :], banks[t][:], SUBTRACT)
-        quantize_weights(3, w3_grouped, "decoded")
-        window(3, "w_grouped3")
+        nc.scalar.copy(out=decoded_half[:], in_=banks[0][:, halves[0]])
+        nc.vector.tensor_tensor(left[1][:, 0, halves[1]], dy_second[1][:, 0, halves[1]], banks[0][:, halves[1]], SUBTRACT)
+        nc.gpsimd.tensor_tensor(left[1][:, 0, halves[0]], dy_second[1][:, 0, halves[0]], decoded_half[:], SUBTRACT)
+        for t in range(1, PACK):
+            nc.vector.tensor_tensor(left[1][:, t, :], dy_second[1][:, t, :], banks[t][:], SUBTRACT)
+        window(3, "dy_second1")
         scatter(2, 0, dx)
+        acc = accumulate(3, 0)
         for g in range(PASSES):
             grouped = sb("dr_grouped%d1" % g, [P, J_TILE, PACK], BF16)
-            group(nc.scalar.copy, grouped[:], left[:, g])
+            group(nc.scalar.copy, grouped[:], left[g][:])
             quantize(dr_codes[g, 1][:], dr_scales[g, 1][:], grouped[:], E4M3)
-        scatter(3, 0, scaled(accumulate(3, 0), 3, 0, whole, "dy_grouped110"))
+            cols = [slice(0, 192), slice(192, J_TILE)][g]
+            scatter(3, 0, scaled(acc, 3, 0, cols, ["decoded", "left11"][g]), cols)
 
         for n in range(N_TILES):
             scatter(n, 1, scaled(accumulate(n, 1), n, 1))

@@ -35,6 +35,7 @@ DECODE_BANKS = 6
 PRODUCT_BANKS = 2
 WHOLE_ROWS = 2
 GPSIMD_ROWS = 2
+EARLY_PLACES = 192
 VECTOR_SHARE = 160
 
 
@@ -54,6 +55,9 @@ def tile_list_embg_tgf32_ls_kernel(tc, dy, w, ls, wgo, offs, out):
                 in_=rows.rearrange("p t (c i) -> p c t i", i=RUN),
             )
 
+        def gpsimd_group(grouped, rows):
+            nc.gpsimd.tensor_scalar(grouped, rows.rearrange("p t c -> p c t"), 1.0, 0.0, MULT, ADD)
+
         def scalar_cast(out, in_):
             nc.scalar.activation(out=out, in_=in_, func=COPY)
 
@@ -72,8 +76,12 @@ def tile_list_embg_tgf32_ls_kernel(tc, dy, w, ls, wgo, offs, out):
         dy_first = [sb("dy_first%d" % g, [P, 2, PACK, HALF], F32) for g in range(PASSES)]
         dy_second = [sb("dy_second%d" % g, [P, PACK, J_TILE], F32) for g in range(PASSES)]
         w_first = sb("w_first", [P, PASSES, PACK, P], F32)
-        w_rest = sb("w_rest", [P, PASSES, PACK, N - P], F32)
-        w_rows = [w_first[:]] + [w_rest[:, :, :, n * P : (n + 1) * P] for n in range(N_TILES - 1)]
+        w_middle = [sb("w_middle%d" % g, [P, PACK, 2 * P], F32) for g in range(PASSES)]
+        w_last = sb("w_last", [P, PASSES, PACK, P], F32)
+        w_rows = {}
+        for g in range(PASSES):
+            w_rows[0, g], w_rows[3, g] = w_first[:, g], w_last[:, g]
+            w_rows[1, g], w_rows[2, g] = w_middle[g][:, :, 0:P], w_middle[g][:, :, P : 2 * P]
 
         for g in range(PASSES):
             for c in range(2):
@@ -81,12 +89,14 @@ def tile_list_embg_tgf32_ls_kernel(tc, dy, w, ls, wgo, offs, out):
         for g in range(PASSES):
             nc.sync.dma_start(out=w_first[:, g], in_=k_rows(w, g, slice(0, P)))
         for g in range(PASSES):
-            nc.sync.dma_start(out=w_rest[:, g], in_=k_rows(w, g, slice(P, N)))
+            nc.sync.dma_start(out=w_middle[g][:], in_=k_rows(w, g, slice(P, 3 * P)))
         nc.sync.dma_start(offsets[:], offs)
         nc.sync.dma_start(out=wgo_sb[0][:], in_=wgo[:, 0:J_TILE])
         with nc.allow_non_contiguous_dma(reason="one factor for each partition and n tile"):
             nc.sync.dma_start(out=ls_sb[:], in_=ls.rearrange("(c p) -> p c", p=P))
         nc.sync.dma_start(out=dy_second[0][:], in_=k_rows(dy, 0, slice(J_TILE, J)))
+        for g in range(PASSES):
+            nc.sync.dma_start(out=w_last[:, g], in_=k_rows(w, g, slice(3 * P, N)))
         nc.sync.dma_start(out=dy_second[1][:], in_=k_rows(dy, 1, slice(J_TILE, J)))
         nc.sync.dma_start(out=wgo_sb[1][:], in_=wgo[:, J_TILE:J])
 
@@ -99,8 +109,8 @@ def tile_list_embg_tgf32_ls_kernel(tc, dy, w, ls, wgo, offs, out):
         strip = sb("strip", [P, STRIP + 1], BF16)
         nc.vector.memset(strip[:].bitcast(U32), 0)
         for b in range(P // QUAD):
-            parts = slice(b * QUAD, (b + 1) * QUAD)
-            nc.vector.tensor_tensor(strip[parts, b * P : (b + 1) * P : PACK], column[parts, :], row[parts, :], IS_EQUAL)
+            lanes = slice(b * QUAD, (b + 1) * QUAD)
+            nc.vector.tensor_tensor(strip[lanes, b * P : (b + 1) * P : PACK], column[lanes, :], row[lanes, :], IS_EQUAL)
         eye = sb("eye", [P, PACK * STRIP], BF16)
         eye_codes = sb("eye_codes", [P, PACK * P], U32)
         eye_scales = sb("eye_scales", [P, PACK * P], U8)
@@ -114,18 +124,6 @@ def tile_list_embg_tgf32_ls_kernel(tc, dy, w, ls, wgo, offs, out):
             values = eye[:, PACK * words.start : PACK * words.stop]
             nc.vector.quantize_mx(out=eye_codes[:, words].bitcast(E4M3), scales=eye_scales[:, words], in_=values)
 
-        for i in range(3):
-            idle = product_psum.tile([P, J_TILE], F32, name="acc")
-            nc.tensor.matmul_mx(
-                out=idle[:],
-                lhsT=eye_codes[:, 0:P].bitcast(E4M3),
-                lhsT_scale=eye_scales[:, 0:P],
-                rhs=eye_codes[:].bitcast(E4M3),
-                rhs_scale=eye_scales[:],
-                start=True,
-                stop=True,
-            )
-
         dq_codes = {u: sb("dq_codes%d%d" % u, [P, J_TILE], U32) for u in units}
         dq_scales = {u: sb("dq_scales%d%d" % u, [P, J_TILE], U8) for u in units}
         dr_codes = {u: sb("dr_codes%d%d" % u, [P, J_TILE], U32) for u in units[1:]}
@@ -138,14 +136,21 @@ def tile_list_embg_tgf32_ls_kernel(tc, dy, w, ls, wgo, offs, out):
             windows[n] = sb("window%d" % n, [P, T], F32, slot)
             nc.gpsimd.memset(windows[n][:].bitcast(U32), 0)
 
-        def first_tier(g, h, rows, vector_columns=0, slot=None):
-            grouped = [sb("dy_grouped%d%d%d" % (g, h, c), [P, HALF, PACK], BF16, [None, slot][c]) for c in range(2)]
-            group(scalar_cast, grouped[0][:], rows[0])
+        def first_tier_in_halves(g, vector_columns):
+            grouped = [sb("dy_grouped%d0%d" % (g, c), [P, HALF, PACK], BF16) for c in range(2)]
+            last = dy_first[g][:, 1]
+            group(scalar_cast, grouped[0][:], dy_first[g][:, 0])
             if vector_columns:
-                group(nc.vector.tensor_copy, grouped[1][:, 0:vector_columns, :], rows[1][:, :, 0:vector_columns])
-            group(scalar_cast, grouped[1][:, vector_columns:HALF, :], rows[1][:, :, vector_columns:HALF])
+                group(nc.vector.tensor_copy, grouped[1][:, 0:vector_columns, :], last[:, :, 0:vector_columns])
+            group(scalar_cast, grouped[1][:, vector_columns:HALF, :], last[:, :, vector_columns:HALF])
             for c in range(2):
-                quantize(dq_codes[g, h][:, halves[c]], dq_scales[g, h][:, halves[c]], grouped[c][:], E5M2)
+                quantize(dq_codes[g, 0][:, halves[c]], dq_scales[g, 0][:, halves[c]], grouped[c][:], E5M2)
+
+        def first_tier_whole(g, slot=None):
+            grouped = sb("dy_grouped%d1" % g, [P, J_TILE, PACK], BF16, slot)
+            for cols in halves:
+                group(scalar_cast, grouped[:, cols, :], dy_second[g][:, :, cols])
+            quantize(dq_codes[g, 1][:], dq_scales[g, 1][:], grouped[:], E5M2)
 
         def decode(g, h):
             banks = []
@@ -175,16 +180,19 @@ def tile_list_embg_tgf32_ls_kernel(tc, dy, w, ls, wgo, offs, out):
                 for t in range(WHOLE_ROWS, PACK):
                     nc.vector.tensor_tensor(left[:, c, t, :], dy_first[0][:, c, t, :], banks[t][:, halves[c]], SUBTRACT)
             group(nc.scalar.copy, grouped[0][:], left[:, 0])
-            return grouped, left
+            gpsimd_group(grouped[1][:], left[:, 1])
+            return grouped
 
         pieces = [slice(0, HALF), slice(HALF, HALF + QUARTER), slice(HALF + QUARTER, J_TILE)]
 
-        def residual_second_pass():
+        def residual_second_pass(w0_grouped):
             banks = decode(1, 0)
             widths = [cols.stop - cols.start for cols in pieces]
             left = [sb("left10%d" % i, [P, PACK, widths[i]], BF16) for i in range(len(pieces))]
             grouped = [sb("dr_grouped10%d" % i, [P, widths[i], PACK], BF16) for i in range(len(pieces))]
             for i, cols in enumerate(pieces):
+                if i == len(pieces) - 1:
+                    quantize_weights(0, w0_grouped, "left00")
                 c, first = divmod(cols.start, HALF)
                 for t in range(PACK):
                     rows = dy_first[1][:, c, t, first : first + widths[i]]
@@ -196,12 +204,24 @@ def tile_list_embg_tgf32_ls_kernel(tc, dy, w, ls, wgo, offs, out):
         def group_weights(n, slot=None):
             grouped = sb("w_grouped%d" % n, [P, PASSES * P, PACK], BF16, slot)
             for g in range(PASSES):
-                group(nc.scalar.copy, grouped[:, g * P : (g + 1) * P, :], w_rows[n][:, g])
+                group(nc.scalar.copy, grouped[:, g * P : (g + 1) * P, :], w_rows[n, g])
             return grouped
 
         def quantize_weights(n, grouped, slot=None):
             w_codes[n] = sb("w_codes%d" % n, [P, PASSES * P], U32, slot)
             quantize(w_codes[n][:], w_scales[n][:], grouped[:], E4M3)
+
+        def group_weights_by_pass(n, slots):
+            grouped = [sb("w_grouped%d%d" % (n, g), [P, P, PACK], BF16, slots[g]) for g in range(PASSES)]
+            for g in range(PASSES):
+                group(nc.scalar.copy, grouped[g][:], w_rows[n, g])
+            return grouped
+
+        def quantize_weights_by_pass(n, grouped, slot=None):
+            w_codes[n] = sb("w_codes%d" % n, [P, PASSES * P], U32, slot)
+            for g in range(PASSES):
+                cols = slice(g * P, (g + 1) * P)
+                quantize(w_codes[n][:, cols], w_scales[n][:, cols], grouped[g][:], E4M3)
 
         whole = slice(0, J_TILE)
 
@@ -233,92 +253,59 @@ def tile_list_embg_tgf32_ls_kernel(tc, dy, w, ls, wgo, offs, out):
             nc.vector.tensor_tensor(windows[n][:].indirect(lists), dx[:], wgo_sb[h][:, cols], MULT)
 
         window(0)
-        first_tier(0, 0, [dy_first[0][:, c] for c in range(2)], VECTOR_SHARE)
-        first_tier(1, 0, [dy_first[1][:, c] for c in range(2)], 0, "after_pass_1")
-        first_pass_grouped, first_pass_left = residual_first_pass()
-        w0_grouped = sb("w_grouped0", [P, PASSES * P, PACK], BF16, "after_pass_1")
-        nc.gpsimd.tensor_scalar(
-            w0_grouped[:].rearrange("p (g c) t -> p g c t", g=PASSES),
-            w_rows[0].rearrange("p g t c -> p g c t"),
-            1.0,
-            0.0,
-            MULT,
-            ADD,
-        )
-        nc.gpsimd.tensor_scalar(
-            first_pass_grouped[1][:], first_pass_left[:, 1].rearrange("p t c -> p c t"), 1.0, 0.0, MULT, ADD
-        )
-        second_pass_grouped = residual_second_pass()
-        quantize_weights(0, w0_grouped)
-        dr_codes[0, 0] = sb("dr_codes00", [P, J_TILE], U32, "w_first")
+        first_tier_in_halves(0, VECTOR_SHARE)
+        first_tier_in_halves(1, 0)
+        w0_grouped = sb("w_grouped0", [P, PASSES * P, PACK], BF16, "dy_grouped101")
+        group(nc.scalar.copy, w0_grouped[:, 0:P, :], w_rows[0, 0])
+        gpsimd_group(w0_grouped[:, P : 2 * P, :], w_rows[0, 1])
+        first_pass_grouped = residual_first_pass()
+        second_pass_grouped = residual_second_pass(w0_grouped)
+        dr_codes[0, 0] = sb("dr_codes00", [P, J_TILE], U32, "dy_grouped101")
         for c in range(2):
             quantize(dr_codes[0, 0][:, halves[c]], dr_scales[0, 0][:, halves[c]], first_pass_grouped[c][:], E4M3)
         for i, cols in enumerate(pieces):
             quantize(dr_codes[1, 0][:, cols], dr_scales[1, 0][:, cols], second_pass_grouped[i][:], E4M3)
         dx = scaled(accumulate(0, 0, pieces), 0, 0)
-        w1_grouped = [sb("w_grouped1%d" % g, [P, P, PACK], BF16, "left10%d" % (g + 1)) for g in range(PASSES)]
-        w_codes[1] = sb("w_codes1", [P, PASSES * P], U32)
-        for g in range(PASSES):
-            group(nc.scalar.copy, w1_grouped[g][:], w_rows[1][:, g])
-        for g in range(PASSES):
-            cols = slice(g * P, (g + 1) * P)
-            quantize(w_codes[1][:, cols], w_scales[1][:, cols], w1_grouped[g][:], E4M3)
+        quantize_weights_by_pass(1, group_weights_by_pass(1, ["left101", "left102"]))
         window(1, "left102")
         scatter(0, 0, dx)
 
-        w2_grouped = group_weights(2, "left101")
-        parts = [slice(0, QUARTER), slice(QUARTER, HALF), halves[1]]
-        part_slots = [None, None, "left100"]
-        grouped = [
-            sb("dy_grouped01%d" % i, [P, cols.stop - cols.start, PACK], BF16, part_slots[i])
-            for i, cols in enumerate(parts)
-        ]
-        for i in (2, 0, 1):
-            group(scalar_cast, grouped[i][:], dy_second[0][:, :, parts[i]])
-        for i, cols in enumerate(parts):
-            quantize(dq_codes[0, 1][:, cols], dq_scales[0, 1][:, cols], grouped[i][:], E5M2)
-        quantize_weights(2, w2_grouped, "dy_grouped011")
-        acc = accumulate(1, 0)
+        first_tier_whole(0, "left100")
+        quantize_weights(2, group_weights(2, "left101"))
         window(2, "left101")
-        scatter(1, 0, scaled(acc, 1, 0, whole, "dy_grouped010"))
+        scatter(1, 0, scaled(accumulate(1, 0), 1, 0, whole, "w_middle0"))
 
-        w3_grouped = [sb("w_grouped3%d" % g, [P, P, PACK], BF16) for g in range(PASSES)]
-        for g in range(PASSES):
-            group(nc.scalar.copy, w3_grouped[g][:], w_rows[3][:, g])
-        grouped = sb("dy_grouped11", [P, J_TILE, PACK], BF16)
-        for cols in halves:
-            group(scalar_cast, grouped[:, cols, :], dy_second[1][:, :, cols])
-        quantize(dq_codes[1, 1][:], dq_scales[1, 1][:], grouped[:], E5M2)
-        w_codes[3] = sb("w_codes3", [P, PASSES * P], U32, "dy_grouped11")
-        for g in range(PASSES):
-            cols = slice(g * P, (g + 1) * P)
-            quantize(w_codes[3][:, cols], w_scales[3][:, cols], w3_grouped[g][:], E4M3)
+        w3_grouped = group_weights_by_pass(3, [None, None])
+        first_tier_whole(1)
+        quantize_weights_by_pass(3, w3_grouped, "dy_grouped11")
         banks = decode(0, 1)
-        decoded = sb("decoded", [P, 2, J_TILE], F32)
+        decoded = sb("decoded", [P, GPSIMD_ROWS, J_TILE], F32, "w_middle0")
         decoded_half = sb("decoded_half", [P, HALF], F32)
         left = [sb("left%d1" % g, [P, PACK, J_TILE], BF16, ["w_grouped30", None][g]) for g in range(PASSES)]
-        for t in range(2):
+        for t in range(GPSIMD_ROWS):
             nc.scalar.copy(out=decoded[:, t, :], in_=banks[t][:])
         dx = scaled(accumulate(2, 0), 2, 0)
-        for t in range(2):
+        for t in range(GPSIMD_ROWS):
             nc.gpsimd.tensor_tensor(left[0][:, t, :], dy_second[0][:, t, :], decoded[:, t, :], SUBTRACT)
-        for t in range(2, PACK):
+        for t in range(GPSIMD_ROWS, PACK):
             nc.vector.tensor_tensor(left[0][:, t, :], dy_second[0][:, t, :], banks[t][:], SUBTRACT)
         banks = decode(1, 1)
-        nc.scalar.copy(out=decoded_half[:], in_=banks[0][:, halves[0]])
-        nc.vector.tensor_tensor(left[1][:, 0, halves[1]], dy_second[1][:, 0, halves[1]], banks[0][:, halves[1]], SUBTRACT)
-        nc.gpsimd.tensor_tensor(left[1][:, 0, halves[0]], dy_second[1][:, 0, halves[0]], decoded_half[:], SUBTRACT)
+        shared, kept = halves
+        nc.scalar.copy(out=decoded_half[:], in_=banks[0][:, shared])
+        nc.vector.tensor_tensor(left[1][:, 0, kept], dy_second[1][:, 0, kept], banks[0][:, kept], SUBTRACT)
+        nc.gpsimd.tensor_tensor(left[1][:, 0, shared], dy_second[1][:, 0, shared], decoded_half[:], SUBTRACT)
         for t in range(1, PACK):
             nc.vector.tensor_tensor(left[1][:, t, :], dy_second[1][:, t, :], banks[t][:], SUBTRACT)
         window(3, "dy_second1")
         scatter(2, 0, dx)
+
         acc = accumulate(3, 0)
+        parts = [slice(0, EARLY_PLACES), slice(EARLY_PLACES, J_TILE)]
         for g in range(PASSES):
             grouped = sb("dr_grouped%d1" % g, [P, J_TILE, PACK], BF16)
             group(nc.scalar.copy, grouped[:], left[g][:])
             quantize(dr_codes[g, 1][:], dr_scales[g, 1][:], grouped[:], E4M3)
-            cols = [slice(0, 192), slice(192, J_TILE)][g]
-            scatter(3, 0, scaled(acc, 3, 0, cols, ["decoded", "left11"][g]), cols)
+            scatter(3, 0, scaled(acc, 3, 0, parts[g], ["w_middle0", "left11"][g]), parts[g])
 
         for n in range(N_TILES):
             scatter(n, 1, scaled(accumulate(n, 1), n, 1))

@@ -169,6 +169,19 @@ def tile_list_embg_tgf32_ls_kernel(tc, dy, w, ls, wgo, offs, out):
                 banks.append(bank)
             return banks
 
+        def keep_clock():
+            for t in range(WHOLE_ROWS, PACK):
+                idle = decode_psum.tile([P, J_TILE], F32, name="idle", tag="bank%d" % t)
+                nc.tensor.matmul_mx(
+                    out=idle[:],
+                    lhsT=eye_codes[:, 0:P].bitcast(E4M3),
+                    lhsT_scale=eye_scales[:, 0:P],
+                    rhs=eye_codes[:].bitcast(E4M3),
+                    rhs_scale=eye_scales[:],
+                    start=True,
+                    stop=True,
+                )
+
         def residual_first_pass():
             banks = decode(0, 0)
             left = sb("left00", [P, 2, PACK, HALF], BF16)
@@ -187,6 +200,7 @@ def tile_list_embg_tgf32_ls_kernel(tc, dy, w, ls, wgo, offs, out):
 
         def residual_second_pass(w0_grouped):
             banks = decode(1, 0)
+            keep_clock()
             widths = [cols.stop - cols.start for cols in pieces]
             left = [sb("left10%d" % i, [P, PACK, widths[i]], BF16) for i in range(len(pieces))]
             grouped = [sb("dr_grouped10%d" % i, [P, widths[i], PACK], BF16) for i in range(len(pieces))]

@@ -8,6 +8,7 @@ FLOPS = 2 * (2 * K * N * J) + 2 * K * 512 * J
 F32 = mybir.dt.float32
 BF16 = mybir.dt.bfloat16
 U32 = mybir.dt.uint32
+I32 = mybir.dt.int32
 U16 = mybir.dt.uint16
 U8 = mybir.dt.uint8
 E4M3 = mybir.dt.float8_e4m3fn_x4
@@ -25,7 +26,7 @@ PASSES = K // K_PASS
 J_TILE = 512
 J_TILES = J // J_TILE
 HALF = J_TILE // 2
-QUARTER = J_TILE // 4
+LINE = [(1, 0), (0, 0), (0, 1), (1, 1)]
 N_TILES = N // P
 LIST_GROUP = 16
 RUN = 4
@@ -33,7 +34,9 @@ QUAD = 32
 STRIP = K_PASS + 1
 DECODE_BANKS = 6
 PRODUCT_BANKS = 2
-WHOLE_ROWS = 2
+GPSIMD_FIRST = 192
+GPSIMD_SECOND = 160
+EARLY = 320
 GPSIMD_ROWS = 2
 EARLY_PLACES = 192
 VECTOR_SHARE = 160
@@ -43,10 +46,13 @@ def tile_list_embg_tgf32_ls_kernel(tc, dy, w, ls, wgo, offs, out):
     nc = tc.nc
     with ExitStack() as ctx:
         keep = ctx.enter_context(tc.tile_pool(name="keep", bufs=1))
+        turns = ctx.enter_context(tc.tile_pool(name="turns", bufs=1))
         decode_psum = ctx.enter_context(tc.psum_pool(name="decode_psum", bufs=1))
-        product_psum = ctx.enter_context(tc.psum_pool(name="product_psum", bufs=PRODUCT_BANKS))
+        product_psum = ctx.enter_context(tc.psum_pool(name="product_psum", bufs=1))
 
         def sb(name, shape, dtype, slot=None):
+            if isinstance(slot, int):
+                return turns.tile(shape, dtype, name=name, tag=name, align_bytes=64, offset=slot)
             return keep.tile(shape, dtype, name=name, tag=slot or name, align_bytes=64)
 
         def group(copy, grouped, rows):
@@ -67,37 +73,35 @@ def tile_list_embg_tgf32_ls_kernel(tc, dy, w, ls, wgo, offs, out):
         def k_rows(x, g, cols):
             return x[g * K_PASS : (g + 1) * K_PASS, cols].rearrange("(p t) c -> p t c", t=PACK)
 
-        units = [(g, h) for h in range(J_TILES) for g in range(PASSES)]
         halves = [slice(c * HALF, (c + 1) * HALF) for c in range(2)]
+        whole = slice(0, J_TILE)
 
         offsets = keep.tile([P, J // LIST_GROUP], U16, name="offsets")
         ls_sb = sb("ls_sb", [P, N_TILES], F32)
         wgo_sb = [sb("wgo%d" % h, [P, J_TILE], F32) for h in range(J_TILES)]
-        dy_first = [sb("dy_first%d" % g, [P, 2, PACK, HALF], F32) for g in range(PASSES)]
+        dy_first = [sb("dy_first%d" % c, [P, PACK, J_TILE], F32, [None, 20480][c]) for c in range(2)]
         dy_second = [sb("dy_second%d" % g, [P, PACK, J_TILE], F32) for g in range(PASSES)]
-        w_first = sb("w_first", [P, PASSES, PACK, P], F32)
-        w_middle = [sb("w_middle%d" % g, [P, PACK, 2 * P], F32) for g in range(PASSES)]
-        w_last = sb("w_last", [P, PASSES, PACK, P], F32)
+        w_early = [sb("w_early%d" % g, [P, PACK, 2 * P], F32) for g in range(PASSES)]
+        w_late = {(n, g): sb("w_late%d%d" % (n, g), [P, PACK, P], F32) for n in (2, 3) for g in range(PASSES)}
         w_rows = {}
         for g in range(PASSES):
-            w_rows[0, g], w_rows[3, g] = w_first[:, g], w_last[:, g]
-            w_rows[1, g], w_rows[2, g] = w_middle[g][:, :, 0:P], w_middle[g][:, :, P : 2 * P]
+            w_rows[0, g], w_rows[1, g] = w_early[g][:, :, 0:P], w_early[g][:, :, P : 2 * P]
+            w_rows[2, g], w_rows[3, g] = w_late[2, g][:], w_late[3, g][:]
 
+        for place, (g, c) in enumerate(LINE):
+            nc.sync.dma_start(out=dy_first[c][:, :, halves[place % 2]], in_=k_rows(dy, g, halves[c]))
         for g in range(PASSES):
-            for c in range(2):
-                nc.sync.dma_start(out=dy_first[g][:, c], in_=k_rows(dy, g, halves[c]))
-        for g in range(PASSES):
-            nc.sync.dma_start(out=w_first[:, g], in_=k_rows(w, g, slice(0, P)))
-        for g in range(PASSES):
-            nc.sync.dma_start(out=w_middle[g][:], in_=k_rows(w, g, slice(P, 3 * P)))
-        nc.sync.dma_start(offsets[:], offs)
-        nc.sync.dma_start(out=wgo_sb[0][:], in_=wgo[:, 0:J_TILE])
+            nc.sync.dma_start(out=w_early[g][:], in_=k_rows(w, g, slice(0, 2 * P)))
         with nc.allow_non_contiguous_dma(reason="one factor for each partition and n tile"):
             nc.sync.dma_start(out=ls_sb[:], in_=ls.rearrange("(c p) -> p c", p=P))
-        nc.sync.dma_start(out=dy_second[0][:], in_=k_rows(dy, 0, slice(J_TILE, J)))
+        nc.sync.dma_start(offsets[:], offs)
+        nc.sync.dma_start(out=wgo_sb[0][:], in_=wgo[:, 0:J_TILE])
         for g in range(PASSES):
-            nc.sync.dma_start(out=w_last[:, g], in_=k_rows(w, g, slice(3 * P, N)))
+            nc.sync.dma_start(out=w_late[2, g][:], in_=k_rows(w, g, slice(2 * P, 3 * P)))
+        nc.sync.dma_start(out=dy_second[0][:], in_=k_rows(dy, 0, slice(J_TILE, J)))
         nc.sync.dma_start(out=dy_second[1][:], in_=k_rows(dy, 1, slice(J_TILE, J)))
+        for g in range(PASSES):
+            nc.sync.dma_start(out=w_late[3, g][:], in_=k_rows(w, g, slice(3 * P, N)))
         nc.sync.dma_start(out=wgo_sb[1][:], in_=wgo[:, J_TILE:J])
 
         ones = sb("ones", [P, QUAD + 1], F32)
@@ -124,10 +128,15 @@ def tile_list_embg_tgf32_ls_kernel(tc, dy, w, ls, wgo, offs, out):
             values = eye[:, PACK * words.start : PACK * words.stop]
             nc.vector.quantize_mx(out=eye_codes[:, words].bitcast(E4M3), scales=eye_scales[:, words], in_=values)
 
-        dq_codes = {u: sb("dq_codes%d%d" % u, [P, J_TILE], U32) for u in units}
-        dq_scales = {u: sb("dq_scales%d%d" % u, [P, J_TILE], U8) for u in units}
-        dr_codes = {u: sb("dr_codes%d%d" % u, [P, J_TILE], U32) for u in units[1:]}
-        dr_scales = {u: sb("dr_scales%d%d" % u, [P, J_TILE], U8) for u in units}
+        dq_line = sb("dq_line", [P, 2 * J_TILE], U32)
+        dq_line_scales = sb("dq_line_scales", [P, 2 * J_TILE + 4], U8)
+        nc.vector.memset(dq_line_scales[:].bitcast(U32), 0)
+        dq_joined = sb("dq_joined", [P, J_TILE], U32)
+        dq_joined_scales = sb("dq_joined_scales", [P, J_TILE], U8)
+        dr_line = sb("dr_line", [P, 2 * J_TILE], U32)
+        dr_line_scales = sb("dr_line_scales", [P, 2 * J_TILE], U8)
+        dq_second = [(sb("dq_codes%d" % g, [P, J_TILE], U32), sb("dq_scales%d" % g, [P, J_TILE], U8)) for g in range(PASSES)]
+        dr_second = [(sb("dr_codes%d" % g, [P, J_TILE], U32), sb("dr_scales%d" % g, [P, J_TILE], U8)) for g in range(PASSES)]
         w_codes = {}
         w_scales = [sb("w_scales%d" % n, [P, PASSES * P], U8) for n in range(N_TILES)]
         windows = {}
@@ -136,84 +145,31 @@ def tile_list_embg_tgf32_ls_kernel(tc, dy, w, ls, wgo, offs, out):
             windows[n] = sb("window%d" % n, [P, T], F32, slot)
             nc.gpsimd.memset(windows[n][:].bitcast(U32), 0)
 
-        def first_tier_in_halves(g, vector_columns):
-            grouped = [sb("dy_grouped%d0%d" % (g, c), [P, HALF, PACK], BF16) for c in range(2)]
-            last = dy_first[g][:, 1]
-            group(scalar_cast, grouped[0][:], dy_first[g][:, 0])
-            if vector_columns:
-                group(nc.vector.tensor_copy, grouped[1][:, 0:vector_columns, :], last[:, :, 0:vector_columns])
-            group(scalar_cast, grouped[1][:, vector_columns:HALF, :], last[:, :, vector_columns:HALF])
-            for c in range(2):
-                quantize(dq_codes[g, 0][:, halves[c]], dq_scales[g, 0][:, halves[c]], grouped[c][:], E5M2)
+        def places(first, count):
+            return slice(first * HALF, (first + count) * HALF)
 
         def first_tier_whole(g, slot=None):
-            grouped = sb("dy_grouped%d1" % g, [P, J_TILE, PACK], BF16, slot)
+            grouped = sb("dy_whole%d" % g, [P, J_TILE, PACK], BF16, slot)
             for cols in halves:
                 group(scalar_cast, grouped[:, cols, :], dy_second[g][:, :, cols])
-            quantize(dq_codes[g, 1][:], dq_scales[g, 1][:], grouped[:], E5M2)
+            quantize(dq_second[g][0][:], dq_second[g][1][:], grouped[:], E5M2)
 
-        def decode(g, h):
+        def decode(codes, scales, step):
             banks = []
             for t in range(PACK):
-                turn = PACK * units.index((g, h)) + t
+                turn = PACK * step + t
                 bank = decode_psum.tile([P, J_TILE], F32, name="decode_bank", tag="bank%d" % (turn % DECODE_BANKS))
                 nc.tensor.matmul_mx(
                     out=bank[:],
                     lhsT=eye_codes[:, t * P : (t + 1) * P].bitcast(E4M3),
                     lhsT_scale=eye_scales[:, t * P : (t + 1) * P],
-                    rhs=dq_codes[g, h][:].bitcast(E5M2),
-                    rhs_scale=dq_scales[g, h][:],
+                    rhs=codes.bitcast(E5M2),
+                    rhs_scale=scales,
                     start=True,
                     stop=True,
                 )
                 banks.append(bank)
             return banks
-
-        def keep_clock():
-            for t in range(WHOLE_ROWS, PACK):
-                idle = decode_psum.tile([P, J_TILE], F32, name="idle", tag="bank%d" % t)
-                nc.tensor.matmul_mx(
-                    out=idle[:],
-                    lhsT=eye_codes[:, 0:P].bitcast(E4M3),
-                    lhsT_scale=eye_scales[:, 0:P],
-                    rhs=eye_codes[:].bitcast(E4M3),
-                    rhs_scale=eye_scales[:],
-                    start=True,
-                    stop=True,
-                )
-
-        def residual_first_pass():
-            banks = decode(0, 0)
-            left = sb("left00", [P, 2, PACK, HALF], BF16)
-            grouped = [sb("dr_grouped00%d" % c, [P, HALF, PACK], BF16) for c in range(2)]
-            for t in range(WHOLE_ROWS):
-                bank = banks[t][:].rearrange("p (c j) -> p c j", c=2)
-                nc.vector.tensor_tensor(left[:, :, t, :], dy_first[0][:, :, t, :], bank, SUBTRACT)
-            for c in range(2):
-                for t in range(WHOLE_ROWS, PACK):
-                    nc.vector.tensor_tensor(left[:, c, t, :], dy_first[0][:, c, t, :], banks[t][:, halves[c]], SUBTRACT)
-            group(nc.scalar.copy, grouped[0][:], left[:, 0])
-            gpsimd_group(grouped[1][:], left[:, 1])
-            return grouped
-
-        pieces = [slice(0, HALF), slice(HALF, HALF + QUARTER), slice(HALF + QUARTER, J_TILE)]
-
-        def residual_second_pass(w0_grouped):
-            banks = decode(1, 0)
-            keep_clock()
-            widths = [cols.stop - cols.start for cols in pieces]
-            left = [sb("left10%d" % i, [P, PACK, widths[i]], BF16) for i in range(len(pieces))]
-            grouped = [sb("dr_grouped10%d" % i, [P, widths[i], PACK], BF16) for i in range(len(pieces))]
-            for i, cols in enumerate(pieces):
-                if i == len(pieces) - 1:
-                    quantize_weights(0, w0_grouped, "left00")
-                c, first = divmod(cols.start, HALF)
-                for t in range(PACK):
-                    rows = dy_first[1][:, c, t, first : first + widths[i]]
-                    nc.vector.tensor_tensor(left[i][:, t, :], rows, banks[t][:, cols], SUBTRACT)
-            for i in range(len(pieces)):
-                group(nc.scalar.copy, grouped[i][:], left[i][:])
-            return grouped
 
         def group_weights(n, slot=None):
             grouped = sb("w_grouped%d" % n, [P, PASSES * P, PACK], BF16, slot)
@@ -237,24 +193,34 @@ def tile_list_embg_tgf32_ls_kernel(tc, dy, w, ls, wgo, offs, out):
                 cols = slice(g * P, (g + 1) * P)
                 quantize(w_codes[n][:, cols], w_scales[n][:, cols], grouped[g][:], E4M3)
 
-        whole = slice(0, J_TILE)
-
-        def accumulate(n, h, last_pass=(whole,)):
-            acc = product_psum.tile([P, J_TILE], F32, name="acc")
-            steps = [(g, dq_codes, dq_scales, E5M2, whole) for g in range(PASSES)]
-            steps += [(0, dr_codes, dr_scales, E4M3, whole)]
-            steps += [(1, dr_codes, dr_scales, E4M3, cols) for cols in last_pass]
+        def accumulate(n, steps):
+            acc = product_psum.tile([P, J_TILE], F32, name="acc", tag="acc%d" % (n % PRODUCT_BANKS))
             for i, (g, codes, scales, fmt, cols) in enumerate(steps):
                 nc.tensor.matmul_mx(
                     out=acc[:, cols],
                     lhsT=w_codes[n][:, g * P : (g + 1) * P].bitcast(E4M3),
                     lhsT_scale=w_scales[n][:, g * P : (g + 1) * P],
-                    rhs=codes[g, h][:, cols].bitcast(fmt),
-                    rhs_scale=scales[g, h][:, cols],
+                    rhs=codes.bitcast(fmt),
+                    rhs_scale=scales,
                     start=(i == 0),
                     stop=(i == len(steps) - 1),
                 )
             return acc
+
+        def dq_step(g, at):
+            return (g, dq_line[:, at], dq_line_scales[:, at], E5M2, whole)
+
+        def dr_step(g, c):
+            at = places(LINE.index((g, c)), 1)
+            return (g, dr_line[:, at], dr_line_scales[:, at], E4M3, halves[c])
+
+        def half_steps(c):
+            return [dq_step(0, places(1, 2)), dq_step(1, places(2 * c, 2)), dr_step(0, c), dr_step(1, c)]
+
+        first_steps = [dq_step(0, places(1, 2)), (1, dq_joined[:], dq_joined_scales[:], E5M2, whole)]
+        first_steps = first_steps + [dr_step(g, c) for c in range(2) for g in range(PASSES)]
+        second_steps = [(g, dq_second[g][0][:], dq_second[g][1][:], E5M2, whole) for g in range(PASSES)]
+        second_steps = second_steps + [(g, dr_second[g][0][:], dr_second[g][1][:], E4M3, whole) for g in range(PASSES)]
 
         def scaled(acc, n, h, cols=whole, slot=None):
             dx = sb("dx%d%d_%d" % (n, h, cols.start), [P, cols.stop - cols.start], F32, slot)
@@ -267,60 +233,90 @@ def tile_list_embg_tgf32_ls_kernel(tc, dy, w, ls, wgo, offs, out):
             nc.vector.tensor_tensor(windows[n][:].indirect(lists), dx[:], wgo_sb[h][:, cols], MULT)
 
         window(0)
-        first_tier_in_halves(0, VECTOR_SHARE)
-        first_tier_in_halves(1, 0)
-        w0_grouped = sb("w_grouped0", [P, PASSES * P, PACK], BF16, "dy_grouped101")
-        group(nc.scalar.copy, w0_grouped[:, 0:P, :], w_rows[0, 0])
-        gpsimd_group(w0_grouped[:, P : 2 * P, :], w_rows[0, 1])
-        first_pass_grouped = residual_first_pass()
-        second_pass_grouped = residual_second_pass(w0_grouped)
-        dr_codes[0, 0] = sb("dr_codes00", [P, J_TILE], U32, "dy_grouped101")
-        for c in range(2):
-            quantize(dr_codes[0, 0][:, halves[c]], dr_scales[0, 0][:, halves[c]], first_pass_grouped[c][:], E4M3)
-        for i, cols in enumerate(pieces):
-            quantize(dr_codes[1, 0][:, cols], dr_scales[1, 0][:, cols], second_pass_grouped[i][:], E4M3)
-        dx = scaled(accumulate(0, 0, pieces), 0, 0)
-        quantize_weights_by_pass(1, group_weights_by_pass(1, ["left101", "left102"]))
-        window(1, "left102")
-        scatter(0, 0, dx)
+        grouped = [sb("dy_grouped0%d" % s, [P, HALF, PACK], BF16) for s in range(2)]
+        group(scalar_cast, grouped[0][:], dy_first[0][:, :, halves[0]])
+        last = dy_first[0][:, :, halves[1]]
+        group(nc.vector.tensor_copy, grouped[1][:, 0:VECTOR_SHARE, :], last[:, :, 0:VECTOR_SHARE])
+        group(scalar_cast, grouped[1][:, VECTOR_SHARE:HALF, :], last[:, :, VECTOR_SHARE:HALF])
+        for s in range(2):
+            quantize(dq_line[:, places(s, 1)], dq_line_scales[:, places(s, 1)], grouped[s][:], E5M2)
+        window(1, "dy_grouped01")
+        banks = decode(dq_line[:, places(0, 2)], dq_line_scales[:, places(0, 2)], 0)
+        left_first = sb("left_first", [P, PACK, J_TILE], BF16)
 
-        first_tier_whole(0, "left100")
-        quantize_weights(2, group_weights(2, "left101"))
-        window(2, "left101")
-        scatter(1, 0, scaled(accumulate(1, 0), 1, 0, whole, "w_middle0"))
+        def subtract_first(t):
+            nc.vector.tensor_tensor(left_first[:, t, :], dy_first[0][:, t, :], banks[t][:], SUBTRACT)
 
-        w3_grouped = group_weights_by_pass(3, [None, None])
-        first_tier_whole(1)
-        quantize_weights_by_pass(3, w3_grouped, "dy_grouped11")
-        banks = decode(0, 1)
-        decoded = sb("decoded", [P, GPSIMD_ROWS, J_TILE], F32, "w_middle0")
+        for t in range(PACK - 1):
+            subtract_first(t)
+
+        grouped = sb("dy_grouped1", [P, J_TILE, PACK], BF16)
+        for s in range(2):
+            group(scalar_cast, grouped[:, halves[s], :], dy_first[1][:, :, halves[s]])
+        quantize(dq_line[:, places(2, 2)], dq_line_scales[:, places(2, 2)], grouped[:], E5M2)
+        subtract_first(PACK - 1)
+        ends = dq_line[:].bitcast(I32).rearrange("p (a j) -> p a j", a=4)[:, 0:4:3, :]
+        nc.sync.dma_start(out=dq_joined[:].bitcast(I32).rearrange("p (a j) -> p a j", a=2), in_=ends)
+        ends = dq_line_scales[:, 0 : 2 * J_TILE].bitcast(I32).rearrange("p (a j) -> p a j", a=4)[:, 0:4:3, :]
+        nc.sync.dma_start(out=dq_joined_scales[:].bitcast(I32).rearrange("p (a j) -> p a j", a=2), in_=ends)
+        banks = decode(dq_line[:, places(2, 2)], dq_line_scales[:, places(2, 2)], 1)
+        dr_grouped0 = sb("dr_grouped0", [P, J_TILE, PACK], BF16, "dy_grouped1")
+        split = J_TILE - GPSIMD_FIRST
+        gpsimd_group(dr_grouped0[:, split:J_TILE, :], left_first[:, :, split:J_TILE])
+        group(nc.scalar.copy, dr_grouped0[:, 0:split, :], left_first[:, :, 0:split])
+        w_grouped = [group_weights(0), group_weights(1, "dy_first0")]
+        early = sb("left_early", [P, PACK, EARLY], BF16, 0)
+        late = sb("left_late", [P, PACK, J_TILE - EARLY], BF16, "dy_grouped1")
+        for t in range(PACK):
+            nc.vector.tensor_tensor(early[:, t, :], dy_first[1][:, t, 0:EARLY], banks[t][:, 0:EARLY], SUBTRACT)
+        quantize_weights(0, w_grouped[0], "left_first")
+        quantize(dr_line[:, places(0, 2)], dr_line_scales[:, places(0, 2)], dr_grouped0[:], E4M3)
+        quantize_weights(1, w_grouped[1], "w_grouped0")
+        for t in range(PACK):
+            nc.vector.tensor_tensor(late[:, t, :], dy_first[1][:, t, EARLY:J_TILE], banks[t][:, EARLY:J_TILE], SUBTRACT)
+        dr_grouped1 = sb("dr_grouped1", [P, J_TILE, PACK], BF16, "dy_first0")
+        gpsimd_group(dr_grouped1[:, 0:GPSIMD_SECOND, :], early[:, :, 0:GPSIMD_SECOND])
+        scatter(0, 0, scaled(accumulate(0, half_steps(0)), 0, 0, halves[0]), halves[0])
+        group(nc.scalar.copy, dr_grouped1[:, GPSIMD_SECOND:EARLY, :], early[:, :, GPSIMD_SECOND:EARLY])
+        group(nc.scalar.copy, dr_grouped1[:, EARLY:J_TILE, :], late[:])
+        quantize(dr_line[:, places(2, 2)], dr_line_scales[:, places(2, 2)], dr_grouped1[:], E4M3)
+        scatter(1, 0, scaled(accumulate(1, half_steps(0)), 1, 0, halves[0], 0), halves[0])
+        first_tier_whole(0, 1024)
+        window(2, 4096)
+        scatter(0, 0, scaled(accumulate(0, half_steps(1)), 0, 0, halves[1]), halves[1])
+        scatter(1, 0, scaled(accumulate(1, half_steps(1)), 1, 0, halves[1], 12288), halves[1])
+
+        first_tier_whole(1, 0)
+        quantize_weights_by_pass(2, group_weights_by_pass(2, [None, 20480]), 0)
+        banks = decode(dq_second[0][0][:], dq_second[0][1][:], 2)
+        decoded = sb("decoded", [P, GPSIMD_ROWS, J_TILE], F32, 12288)
         decoded_half = sb("decoded_half", [P, HALF], F32)
-        left = [sb("left%d1" % g, [P, PACK, J_TILE], BF16, ["w_grouped30", None][g]) for g in range(PASSES)]
+        left = [sb("left%d1" % g, [P, PACK, J_TILE], BF16, ["w_grouped20", None][g]) for g in range(PASSES)]
         for t in range(GPSIMD_ROWS):
             nc.scalar.copy(out=decoded[:, t, :], in_=banks[t][:])
-        dx = scaled(accumulate(2, 0), 2, 0)
         for t in range(GPSIMD_ROWS):
             nc.gpsimd.tensor_tensor(left[0][:, t, :], dy_second[0][:, t, :], decoded[:, t, :], SUBTRACT)
         for t in range(GPSIMD_ROWS, PACK):
             nc.vector.tensor_tensor(left[0][:, t, :], dy_second[0][:, t, :], banks[t][:], SUBTRACT)
-        banks = decode(1, 1)
+        banks = decode(dq_second[1][0][:], dq_second[1][1][:], 3)
         shared, kept = halves
         nc.scalar.copy(out=decoded_half[:], in_=banks[0][:, shared])
         nc.vector.tensor_tensor(left[1][:, 0, kept], dy_second[1][:, 0, kept], banks[0][:, kept], SUBTRACT)
         nc.gpsimd.tensor_tensor(left[1][:, 0, shared], dy_second[1][:, 0, shared], decoded_half[:], SUBTRACT)
         for t in range(1, PACK):
             nc.vector.tensor_tensor(left[1][:, t, :], dy_second[1][:, t, :], banks[t][:], SUBTRACT)
-        window(3, "dy_second1")
-        scatter(2, 0, dx)
+        quantize_weights(3, group_weights(3, 20480), "dy_second0")
+        window(3, 21504)
+        scatter(2, 0, scaled(accumulate(2, first_steps), 2, 0, whole, 12288))
 
-        acc = accumulate(3, 0)
+        acc = accumulate(3, first_steps)
         parts = [slice(0, EARLY_PLACES), slice(EARLY_PLACES, J_TILE)]
         for g in range(PASSES):
-            grouped = sb("dr_grouped%d1" % g, [P, J_TILE, PACK], BF16)
+            grouped = sb("dr_whole%d" % g, [P, J_TILE, PACK], BF16, [17408, "w_grouped20"][g])
             group(nc.scalar.copy, grouped[:], left[g][:])
-            quantize(dr_codes[g, 1][:], dr_scales[g, 1][:], grouped[:], E4M3)
-            scatter(3, 0, scaled(acc, 3, 0, parts[g], ["w_middle0", "left11"][g]), parts[g])
+            quantize(dr_second[g][0][:], dr_second[g][1][:], grouped[:], E4M3)
+            scatter(3, 0, scaled(acc, 3, 0, parts[g], ["decoded_half", "left11"][g]), parts[g])
 
         for n in range(N_TILES):
-            scatter(n, 1, scaled(accumulate(n, 1), n, 1))
+            scatter(n, 1, scaled(accumulate(n, second_steps), n, 1))
             nc.sync.dma_start(out=out[n * P : (n + 1) * P, :], in_=windows[n][:])

@@ -82,11 +82,11 @@ def tile_list_embg_tgf32_ls_kernel(tc, dy, w, ls, wgo, offs, out):
         dy_first = [sb("dy_first%d" % c, [P, PACK, J_TILE], F32, [None, 20480][c]) for c in range(2)]
         dy_second = [sb("dy_second%d" % g, [P, PACK, J_TILE], F32) for g in range(PASSES)]
         w_early = [sb("w_early%d" % g, [P, PACK, 2 * P], F32) for g in range(PASSES)]
-        w_late = {(n, g): sb("w_late%d%d" % (n, g), [P, PACK, P], F32) for n in (2, 3) for g in range(PASSES)}
+        w_late = [sb("w_late%d" % g, [P, PACK, 2 * P], F32) for g in range(PASSES)]
         w_rows = {}
         for g in range(PASSES):
             w_rows[0, g], w_rows[1, g] = w_early[g][:, :, 0:P], w_early[g][:, :, P : 2 * P]
-            w_rows[2, g], w_rows[3, g] = w_late[2, g][:], w_late[3, g][:]
+            w_rows[2, g], w_rows[3, g] = w_late[g][:, :, 0:P], w_late[g][:, :, P : 2 * P]
 
         for place, (g, c) in enumerate(LINE):
             nc.sync.dma_start(out=dy_first[c][:, :, halves[place % 2]], in_=k_rows(dy, g, halves[c]))
@@ -96,12 +96,10 @@ def tile_list_embg_tgf32_ls_kernel(tc, dy, w, ls, wgo, offs, out):
             nc.sync.dma_start(out=ls_sb[:], in_=ls.rearrange("(c p) -> p c", p=P))
         nc.sync.dma_start(offsets[:], offs)
         nc.sync.dma_start(out=wgo_sb[0][:], in_=wgo[:, 0:J_TILE])
-        for g in range(PASSES):
-            nc.sync.dma_start(out=w_late[2, g][:], in_=k_rows(w, g, slice(2 * P, 3 * P)))
+        nc.sync.dma_start(out=w_late[0][:], in_=k_rows(w, 0, slice(2 * P, N)))
         nc.sync.dma_start(out=dy_second[0][:], in_=k_rows(dy, 0, slice(J_TILE, J)))
         nc.sync.dma_start(out=dy_second[1][:], in_=k_rows(dy, 1, slice(J_TILE, J)))
-        for g in range(PASSES):
-            nc.sync.dma_start(out=w_late[3, g][:], in_=k_rows(w, g, slice(3 * P, N)))
+        nc.sync.dma_start(out=w_late[1][:], in_=k_rows(w, 1, slice(2 * P, N)))
         nc.sync.dma_start(out=wgo_sb[1][:], in_=wgo[:, J_TILE:J])
 
         ones = sb("ones", [P, QUAD + 1], F32)
@@ -251,8 +249,8 @@ def tile_list_embg_tgf32_ls_kernel(tc, dy, w, ls, wgo, offs, out):
             subtract_first(t)
 
         grouped = sb("dy_grouped1", [P, J_TILE, PACK], BF16)
-        for s in range(2):
-            group(scalar_cast, grouped[:, halves[s], :], dy_first[1][:, :, halves[s]])
+        for cols in halves:
+            group(scalar_cast, grouped[:, cols, :], dy_first[1][:, :, cols])
         quantize(dq_line[:, places(2, 2)], dq_line_scales[:, places(2, 2)], grouped[:], E5M2)
         subtract_first(PACK - 1)
         ends = dq_line[:].bitcast(I32).rearrange("p (a j) -> p a j", a=4)[:, 0:4:3, :]
@@ -290,20 +288,14 @@ def tile_list_embg_tgf32_ls_kernel(tc, dy, w, ls, wgo, offs, out):
         quantize_weights_by_pass(2, group_weights_by_pass(2, [None, 20480]), 0)
         banks = decode(dq_second[0][0][:], dq_second[0][1][:], 2)
         decoded = sb("decoded", [P, GPSIMD_ROWS, J_TILE], F32, 12288)
-        decoded_half = sb("decoded_half", [P, HALF], F32)
         left = [sb("left%d1" % g, [P, PACK, J_TILE], BF16, ["w_grouped20", None][g]) for g in range(PASSES)]
         for t in range(GPSIMD_ROWS):
             nc.scalar.copy(out=decoded[:, t, :], in_=banks[t][:])
-        for t in range(GPSIMD_ROWS):
-            nc.gpsimd.tensor_tensor(left[0][:, t, :], dy_second[0][:, t, :], decoded[:, t, :], SUBTRACT)
+        nc.gpsimd.tensor_tensor(left[0][:, 0:GPSIMD_ROWS, :], dy_second[0][:, 0:GPSIMD_ROWS, :], decoded[:], SUBTRACT)
         for t in range(GPSIMD_ROWS, PACK):
             nc.vector.tensor_tensor(left[0][:, t, :], dy_second[0][:, t, :], banks[t][:], SUBTRACT)
         banks = decode(dq_second[1][0][:], dq_second[1][1][:], 3)
-        shared, kept = halves
-        nc.scalar.copy(out=decoded_half[:], in_=banks[0][:, shared])
-        nc.vector.tensor_tensor(left[1][:, 0, kept], dy_second[1][:, 0, kept], banks[0][:, kept], SUBTRACT)
-        nc.gpsimd.tensor_tensor(left[1][:, 0, shared], dy_second[1][:, 0, shared], decoded_half[:], SUBTRACT)
-        for t in range(1, PACK):
+        for t in range(PACK):
             nc.vector.tensor_tensor(left[1][:, t, :], dy_second[1][:, t, :], banks[t][:], SUBTRACT)
         quantize_weights(3, group_weights(3, 20480), "dy_second0")
         window(3, 21504)
@@ -315,7 +307,7 @@ def tile_list_embg_tgf32_ls_kernel(tc, dy, w, ls, wgo, offs, out):
             grouped = sb("dr_whole%d" % g, [P, J_TILE, PACK], BF16, [17408, "w_grouped20"][g])
             group(nc.scalar.copy, grouped[:], left[g][:])
             quantize(dr_second[g][0][:], dr_second[g][1][:], grouped[:], E4M3)
-            scatter(3, 0, scaled(acc, 3, 0, parts[g], ["decoded_half", "left11"][g]), parts[g])
+            scatter(3, 0, scaled(acc, 3, 0, parts[g], [None, "left11"][g]), parts[g])
 
         for n in range(N_TILES):
             scatter(n, 1, scaled(accumulate(n, second_steps), n, 1))

@@ -8,7 +8,6 @@ FLOPS = 2 * (2 * K * N * J) + 2 * K * 512 * J
 F32 = mybir.dt.float32
 BF16 = mybir.dt.bfloat16
 U32 = mybir.dt.uint32
-I32 = mybir.dt.int32
 U16 = mybir.dt.uint16
 U8 = mybir.dt.uint8
 E4M3 = mybir.dt.float8_e4m3fn_x4
@@ -24,21 +23,14 @@ PACK = 4
 K_PASS = P * PACK
 PASSES = K // K_PASS
 J_TILE = 512
-J_TILES = J // J_TILE
 HALF = J_TILE // 2
-LINE = [(1, 0), (0, 0), (0, 1), (1, 1)]
+BANK = J_TILE // PACK
 N_TILES = N // P
 LIST_GROUP = 16
 RUN = 4
+PAIR = 2
 QUAD = 32
 STRIP = K_PASS + 1
-DECODE_BANKS = 6
-PRODUCT_BANKS = 2
-GPSIMD_FIRST = 192
-GPSIMD_SECOND = 160
-EARLY = 320
-GPSIMD_ROWS = 2
-EARLY_PLACES = 192
 VECTOR_SHARE = 160
 
 
@@ -47,13 +39,15 @@ def tile_list_embg_tgf32_ls_kernel(tc, dy, w, ls, wgo, offs, out):
     with ExitStack() as ctx:
         keep = ctx.enter_context(tc.tile_pool(name="keep", bufs=1))
         turns = ctx.enter_context(tc.tile_pool(name="turns", bufs=1))
-        decode_psum = ctx.enter_context(tc.psum_pool(name="decode_psum", bufs=1))
-        product_psum = ctx.enter_context(tc.psum_pool(name="product_psum", bufs=1))
+        psum = ctx.enter_context(tc.psum_pool(name="psum", bufs=1))
 
-        def sb(name, shape, dtype, slot=None):
-            if isinstance(slot, int):
-                return turns.tile(shape, dtype, name=name, tag=name, align_bytes=64, offset=slot)
-            return keep.tile(shape, dtype, name=name, tag=slot or name, align_bytes=64)
+        def sb(name, shape, dtype, at=None):
+            if at is None:
+                return keep.tile(shape, dtype, name=name, tag=name, align_bytes=64)
+            return turns.tile(shape, dtype, name=name, tag=name, align_bytes=64, offset=at)
+
+        def mx(name, width, at=None):
+            return sb(name + "_codes", [P, width], U32, at), sb(name + "_scales", [P, width], U8)
 
         def group(copy, grouped, rows):
             copy(
@@ -61,46 +55,118 @@ def tile_list_embg_tgf32_ls_kernel(tc, dy, w, ls, wgo, offs, out):
                 in_=rows.rearrange("p t (c i) -> p c t i", i=RUN),
             )
 
-        def gpsimd_group(grouped, rows):
-            nc.gpsimd.tensor_scalar(grouped, rows.rearrange("p t c -> p c t"), 1.0, 0.0, MULT, ADD)
-
         def scalar_cast(out, in_):
             nc.scalar.activation(out=out, in_=in_, func=COPY)
 
-        def quantize(codes, scales, grouped, fmt):
-            nc.vector.quantize_mx(out=codes.bitcast(fmt), scales=scales, in_=grouped.rearrange("p c t -> p (c t)"))
+        def quantize(operand, cols, grouped, fmt):
+            codes, scales = operand
+            nc.vector.quantize_mx(out=codes[:, cols].bitcast(fmt), scales=scales[:, cols], in_=grouped.rearrange("p c t -> p (c t)"))
 
         def k_rows(x, g, cols):
             return x[g * K_PASS : (g + 1) * K_PASS, cols].rearrange("(p t) c -> p t c", t=PACK)
 
-        halves = [slice(c * HALF, (c + 1) * HALF) for c in range(2)]
-        whole = slice(0, J_TILE)
+        def span(first, count):
+            return slice(first, first + count)
+
+        halves = [span(h * HALF, HALF) for h in range(2)]
+        whole = span(0, J_TILE)
 
         offsets = keep.tile([P, J // LIST_GROUP], U16, name="offsets")
         ls_sb = sb("ls_sb", [P, N_TILES], F32)
-        wgo_sb = [sb("wgo%d" % h, [P, J_TILE], F32) for h in range(J_TILES)]
-        dy_first = [sb("dy_first%d" % c, [P, PACK, J_TILE], F32, [None, 20480][c]) for c in range(2)]
-        dy_second = [sb("dy_second%d" % g, [P, PACK, J_TILE], F32) for g in range(PASSES)]
+        wgo_sb = [sb("wgo%d" % s, [P, J_TILE], F32) for s in range(2)]
+        dy_first = {(g, h): sb("dy_first%d%d" % (g, h), [P, PACK, HALF], F32) for h in range(2) for g in range(PASSES)}
+        dy_second = [sb("dy_second%d" % g, [P, PACK, J_TILE], F32, [44032, 54272][g]) for g in range(PASSES)]
         w_early = [sb("w_early%d" % g, [P, PACK, 2 * P], F32) for g in range(PASSES)]
-        w_late = [sb("w_late%d" % g, [P, PACK, 2 * P], F32) for g in range(PASSES)]
-        w_rows = {}
-        for g in range(PASSES):
-            w_rows[0, g], w_rows[1, g] = w_early[g][:, :, 0:P], w_early[g][:, :, P : 2 * P]
-            w_rows[2, g], w_rows[3, g] = w_late[g][:, :, 0:P], w_late[g][:, :, P : 2 * P]
+        w_third = [sb("w_third%d" % g, [P, PACK, P], F32, [None, 26624][g]) for g in range(PASSES)]
+        w_last = [sb("w_last%d" % g, [P, PACK, P], F32, [41984, 52224][g]) for g in range(PASSES)]
 
-        for place, (g, c) in enumerate(LINE):
-            nc.sync.dma_start(out=dy_first[c][:, :, halves[place % 2]], in_=k_rows(dy, g, halves[c]))
+        for h in range(2):
+            for g in range(PASSES):
+                nc.sync.dma_start(out=dy_first[g, h][:], in_=k_rows(dy, g, halves[h]))
         for g in range(PASSES):
-            nc.sync.dma_start(out=w_early[g][:], in_=k_rows(w, g, slice(0, 2 * P)))
+            nc.sync.dma_start(out=w_early[g][:], in_=k_rows(w, g, span(0, 2 * P)))
         with nc.allow_non_contiguous_dma(reason="one factor for each partition and n tile"):
             nc.sync.dma_start(out=ls_sb[:], in_=ls.rearrange("(c p) -> p c", p=P))
         nc.sync.dma_start(offsets[:], offs)
         nc.sync.dma_start(out=wgo_sb[0][:], in_=wgo[:, 0:J_TILE])
-        nc.sync.dma_start(out=w_late[0][:], in_=k_rows(w, 0, slice(2 * P, N)))
-        nc.sync.dma_start(out=dy_second[0][:], in_=k_rows(dy, 0, slice(J_TILE, J)))
-        nc.sync.dma_start(out=dy_second[1][:], in_=k_rows(dy, 1, slice(J_TILE, J)))
-        nc.sync.dma_start(out=w_late[1][:], in_=k_rows(w, 1, slice(2 * P, N)))
+        for h in range(2):
+            nc.sync.dma_start(out=dy_second[0][:, :, halves[h]], in_=k_rows(dy, 0, span(J_TILE + h * HALF, HALF)))
+        for g in range(PASSES):
+            nc.sync.dma_start(out=w_third[g][:], in_=k_rows(w, g, span(2 * P, P)))
+        nc.sync.dma_start(out=dy_second[1][:], in_=k_rows(dy, 1, span(J_TILE, J_TILE)))
+        for g in range(PASSES):
+            nc.sync.dma_start(out=w_last[g][:], in_=k_rows(w, g, span(3 * P, P)))
         nc.sync.dma_start(out=wgo_sb[1][:], in_=wgo[:, J_TILE:J])
+
+
+        windows = {}
+
+        def window(n, memset, at=None):
+            windows[n] = sb("window%d" % n, [P, T], F32, at)
+            memset(windows[n][:].bitcast(U32), 0)
+
+        def decode(operand, first, tag):
+            codes, scales = operand
+            bank = psum.tile([P, PACK, BANK], F32, name="decoded", tag="decode%d" % tag)
+            for t in range(PACK):
+                nc.tensor.matmul_mx(
+                    out=bank[:, t, :],
+                    lhsT=eye_codes[:, span(t * P, P)].bitcast(E4M3),
+                    lhsT_scale=eye_scales[:, span(t * P, P)],
+                    rhs=codes[:, span(first, BANK)].bitcast(E5M2),
+                    rhs_scale=scales[:, span(first, BANK)],
+                    start=True,
+                    stop=True,
+                )
+            return bank
+
+        def subtract(left, rows, bank):
+            nc.vector.tensor_tensor(
+                left.rearrange("p (c i) t -> p c t i", i=PAIR),
+                rows.rearrange("p t (c i) -> p c t i", i=PAIR),
+                bank[:].rearrange("p t (c i) -> p c t i", i=PAIR),
+                SUBTRACT,
+            )
+
+        def unload(values, bank):
+            nc.scalar.copy(out=values, in_=bank[:].rearrange("p t c -> p c t"))
+
+        def gpsimd_subtract(left, rows, values):
+            nc.gpsimd.tensor_tensor(left, rows.rearrange("p t c -> p c t"), values, SUBTRACT)
+
+        def accumulate(weights, width, steps, tag):
+            acc = psum.tile([P, width], F32, name="acc", tag="acc%d" % tag)
+            for i, (g, (codes, scales), first, count, fmt, col) in enumerate(steps):
+                (w_codes, w_scales), w_first = weights(g)
+                nc.tensor.matmul_mx(
+                    out=acc[:, span(col, count)],
+                    lhsT=w_codes[:, span(w_first, P)].bitcast(E4M3),
+                    lhsT_scale=w_scales[:, span(w_first, P)],
+                    rhs=codes[:, span(first, count)].bitcast(fmt),
+                    rhs_scale=scales[:, span(first, count)],
+                    start=(i == 0),
+                    stop=(i == len(steps) - 1),
+                )
+            return acc
+
+        def lists(first, count):
+            return offsets[:, span(first // LIST_GROUP, count // LIST_GROUP)]
+
+        def weigh(name, acc_cols, n, wgo_cols, count, at=None):
+            dx = sb(name, [P, count], F32, at)
+            nc.vector.scalar_tensor_tensor(dx[:], acc_cols, ls_sb[:, n : n + 1], wgo_cols, MULT, MULT)
+            return dx
+
+        def place(n, first, count, dx):
+            nc.vector.tensor_copy(windows[n][:].indirect(lists(first, count)), dx[:])
+
+        def scaled(name, acc_cols, n, count, at=None):
+            dx = sb(name, [P, count], F32, at)
+            nc.scalar.activation(out=dx[:], in_=acc_cols, func=COPY, scale=ls_sb[:, n : n + 1])
+            return dx
+
+        def weigh_and_place(n, first, count, dx, wgo_cols):
+            nc.vector.tensor_tensor(windows[n][:].indirect(lists(first, count)), dx[:], wgo_cols, MULT)
 
         ones = sb("ones", [P, QUAD + 1], F32)
         nc.vector.memset(ones[:], 1.0)
@@ -126,189 +192,112 @@ def tile_list_embg_tgf32_ls_kernel(tc, dy, w, ls, wgo, offs, out):
             values = eye[:, PACK * words.start : PACK * words.stop]
             nc.vector.quantize_mx(out=eye_codes[:, words].bitcast(E4M3), scales=eye_scales[:, words], in_=values)
 
-        dq_line = sb("dq_line", [P, 2 * J_TILE], U32)
-        dq_line_scales = sb("dq_line_scales", [P, 2 * J_TILE + 4], U8)
-        nc.vector.memset(dq_line_scales[:].bitcast(U32), 0)
-        dq_joined = sb("dq_joined", [P, J_TILE], U32)
-        dq_joined_scales = sb("dq_joined_scales", [P, J_TILE], U8)
-        dr_line = sb("dr_line", [P, 2 * J_TILE], U32)
-        dr_line_scales = sb("dr_line_scales", [P, 2 * J_TILE], U8)
-        dq_second = [(sb("dq_codes%d" % g, [P, J_TILE], U32), sb("dq_scales%d" % g, [P, J_TILE], U8)) for g in range(PASSES)]
-        dr_second = [(sb("dr_codes%d" % g, [P, J_TILE], U32), sb("dr_scales%d" % g, [P, J_TILE], U8)) for g in range(PASSES)]
-        w_codes = {}
-        w_scales = [sb("w_scales%d" % n, [P, PASSES * P], U8) for n in range(N_TILES)]
-        windows = {}
+        window(0, nc.gpsimd.memset)
 
-        def window(n, slot=None):
-            windows[n] = sb("window%d" % n, [P, T], F32, slot)
-            nc.gpsimd.memset(windows[n][:].bitcast(U32), 0)
 
-        def places(first, count):
-            return slice(first * HALF, (first + count) * HALF)
+        dq_first = [mx("dq_first%d" % h, PASSES * HALF) for h in range(2)]
+        dr_first = [mx("dr_first%d" % h, PASSES * HALF) for h in range(2)]
+        grouped = [sb("grouped0%d" % g, [P, HALF, PACK], BF16, [0, None][g]) for g in range(PASSES)]
+        left = [sb("left0%d" % g, [P, HALF, PACK], BF16, [None, 8192][g]) for g in range(PASSES)]
+        group(nc.vector.tensor_copy, grouped[0][:, 0:VECTOR_SHARE, :], dy_first[0, 0][:, :, 0:VECTOR_SHARE])
+        group(scalar_cast, grouped[0][:, VECTOR_SHARE:HALF, :], dy_first[0, 0][:, :, VECTOR_SHARE:HALF])
+        quantize(dq_first[0], halves[0], grouped[0][:], E5M2)
+        window(1, nc.vector.memset, 0)
+        group(scalar_cast, grouped[1][:], dy_first[1, 0][:])
+        banks = [decode(dq_first[0], b * BANK, b) for b in range(2)]
+        for b in range(2):
+            subtract(left[0][:, span(b * BANK, BANK), :], dy_first[0, 0][:, :, span(b * BANK, BANK)], banks[b])
+        quantize(dq_first[0], halves[1], grouped[1][:], E5M2)
+        quantize(dr_first[0], halves[0], left[0][:], E4M3)
+        banks = [decode(dq_first[0], HALF + b * BANK, 2 + b) for b in range(2)]
+        for b in range(2):
+            subtract(left[1][:, span(b * BANK, BANK), :], dy_first[1, 0][:, :, span(b * BANK, BANK)], banks[b])
 
-        def first_tier_whole(g, slot=None):
-            grouped = sb("dy_whole%d" % g, [P, J_TILE, PACK], BF16, slot)
-            for cols in halves:
-                group(scalar_cast, grouped[:, cols, :], dy_second[g][:, :, cols])
-            quantize(dq_second[g][0][:], dq_second[g][1][:], grouped[:], E5M2)
-
-        def decode(codes, scales, step):
-            banks = []
-            for t in range(PACK):
-                turn = PACK * step + t
-                bank = decode_psum.tile([P, J_TILE], F32, name="decode_bank", tag="bank%d" % (turn % DECODE_BANKS))
-                nc.tensor.matmul_mx(
-                    out=bank[:],
-                    lhsT=eye_codes[:, t * P : (t + 1) * P].bitcast(E4M3),
-                    lhsT_scale=eye_scales[:, t * P : (t + 1) * P],
-                    rhs=codes.bitcast(E5M2),
-                    rhs_scale=scales,
-                    start=True,
-                    stop=True,
-                )
-                banks.append(bank)
-            return banks
-
-        def group_weights(n, slot=None):
-            grouped = sb("w_grouped%d" % n, [P, PASSES * P, PACK], BF16, slot)
-            for g in range(PASSES):
-                group(nc.scalar.copy, grouped[:, g * P : (g + 1) * P, :], w_rows[n, g])
-            return grouped
-
-        def quantize_weights(n, grouped, slot=None):
-            w_codes[n] = sb("w_codes%d" % n, [P, PASSES * P], U32, slot)
-            quantize(w_codes[n][:], w_scales[n][:], grouped[:], E4M3)
-
-        def group_weights_by_pass(n, slots):
-            grouped = [sb("w_grouped%d%d" % (n, g), [P, P, PACK], BF16, slots[g]) for g in range(PASSES)]
-            for g in range(PASSES):
-                group(nc.scalar.copy, grouped[g][:], w_rows[n, g])
-            return grouped
-
-        def quantize_weights_by_pass(n, grouped, slot=None):
-            w_codes[n] = sb("w_codes%d" % n, [P, PASSES * P], U32, slot)
-            for g in range(PASSES):
-                cols = slice(g * P, (g + 1) * P)
-                quantize(w_codes[n][:, cols], w_scales[n][:, cols], grouped[g][:], E4M3)
-
-        def accumulate(n, steps):
-            acc = product_psum.tile([P, J_TILE], F32, name="acc", tag="acc%d" % (n % PRODUCT_BANKS))
-            for i, (g, codes, scales, fmt, cols) in enumerate(steps):
-                nc.tensor.matmul_mx(
-                    out=acc[:, cols],
-                    lhsT=w_codes[n][:, g * P : (g + 1) * P].bitcast(E4M3),
-                    lhsT_scale=w_scales[n][:, g * P : (g + 1) * P],
-                    rhs=codes.bitcast(fmt),
-                    rhs_scale=scales,
-                    start=(i == 0),
-                    stop=(i == len(steps) - 1),
-                )
-            return acc
-
-        def dq_step(g, at):
-            return (g, dq_line[:, at], dq_line_scales[:, at], E5M2, whole)
-
-        def dr_step(g, c):
-            at = places(LINE.index((g, c)), 1)
-            return (g, dr_line[:, at], dr_line_scales[:, at], E4M3, halves[c])
-
-        def half_steps(c):
-            return [dq_step(0, places(1, 2)), dq_step(1, places(2 * c, 2)), dr_step(0, c), dr_step(1, c)]
-
-        first_steps = [dq_step(0, places(1, 2)), (1, dq_joined[:], dq_joined_scales[:], E5M2, whole)]
-        first_steps = first_steps + [dr_step(g, c) for c in range(2) for g in range(PASSES)]
-        second_steps = [(g, dq_second[g][0][:], dq_second[g][1][:], E5M2, whole) for g in range(PASSES)]
-        second_steps = second_steps + [(g, dr_second[g][0][:], dr_second[g][1][:], E4M3, whole) for g in range(PASSES)]
-
-        def scaled(acc, n, h, cols=whole, slot=None):
-            dx = sb("dx%d%d_%d" % (n, h, cols.start), [P, cols.stop - cols.start], F32, slot)
-            nc.scalar.activation(out=dx[:], in_=acc[:, cols], func=COPY, scale=ls_sb[:, n : n + 1])
-            return dx
-
-        def scatter(n, h, dx, cols=whole):
-            first = h * J_TILE
-            lists = offsets[:, (first + cols.start) // LIST_GROUP : (first + cols.stop) // LIST_GROUP]
-            nc.vector.tensor_tensor(windows[n][:].indirect(lists), dx[:], wgo_sb[h][:, cols], MULT)
-
-        window(0)
-        grouped = [sb("dy_grouped0%d" % s, [P, HALF, PACK], BF16) for s in range(2)]
-        group(scalar_cast, grouped[0][:], dy_first[0][:, :, halves[0]])
-        last = dy_first[0][:, :, halves[1]]
-        group(nc.vector.tensor_copy, grouped[1][:, 0:VECTOR_SHARE, :], last[:, :, 0:VECTOR_SHARE])
-        group(scalar_cast, grouped[1][:, VECTOR_SHARE:HALF, :], last[:, :, VECTOR_SHARE:HALF])
-        for s in range(2):
-            quantize(dq_line[:, places(s, 1)], dq_line_scales[:, places(s, 1)], grouped[s][:], E5M2)
-        window(1, "dy_grouped01")
-        banks = decode(dq_line[:, places(0, 2)], dq_line_scales[:, places(0, 2)], 0)
-        left_first = sb("left_first", [P, PACK, J_TILE], BF16)
-
-        def subtract_first(t):
-            nc.vector.tensor_tensor(left_first[:, t, :], dy_first[0][:, t, :], banks[t][:], SUBTRACT)
-
-        for t in range(PACK - 1):
-            subtract_first(t)
-
-        grouped = sb("dy_grouped1", [P, J_TILE, PACK], BF16)
-        for cols in halves:
-            group(scalar_cast, grouped[:, cols, :], dy_first[1][:, :, cols])
-        quantize(dq_line[:, places(2, 2)], dq_line_scales[:, places(2, 2)], grouped[:], E5M2)
-        subtract_first(PACK - 1)
-        ends = dq_line[:].bitcast(I32).rearrange("p (a j) -> p a j", a=4)[:, 0:4:3, :]
-        nc.sync.dma_start(out=dq_joined[:].bitcast(I32).rearrange("p (a j) -> p a j", a=2), in_=ends)
-        ends = dq_line_scales[:, 0 : 2 * J_TILE].bitcast(I32).rearrange("p (a j) -> p a j", a=4)[:, 0:4:3, :]
-        nc.sync.dma_start(out=dq_joined_scales[:].bitcast(I32).rearrange("p (a j) -> p a j", a=2), in_=ends)
-        banks = decode(dq_line[:, places(2, 2)], dq_line_scales[:, places(2, 2)], 1)
-        dr_grouped0 = sb("dr_grouped0", [P, J_TILE, PACK], BF16, "dy_grouped1")
-        split = J_TILE - GPSIMD_FIRST
-        gpsimd_group(dr_grouped0[:, split:J_TILE, :], left_first[:, :, split:J_TILE])
-        group(nc.scalar.copy, dr_grouped0[:, 0:split, :], left_first[:, :, 0:split])
-        w_grouped = [group_weights(0), group_weights(1, "dy_first0")]
-        early = sb("left_early", [P, PACK, EARLY], BF16, 0)
-        late = sb("left_late", [P, PACK, J_TILE - EARLY], BF16, "dy_grouped1")
-        for t in range(PACK):
-            nc.vector.tensor_tensor(early[:, t, :], dy_first[1][:, t, 0:EARLY], banks[t][:, 0:EARLY], SUBTRACT)
-        quantize_weights(0, w_grouped[0], "left_first")
-        quantize(dr_line[:, places(0, 2)], dr_line_scales[:, places(0, 2)], dr_grouped0[:], E4M3)
-        quantize_weights(1, w_grouped[1], "w_grouped0")
-        for t in range(PACK):
-            nc.vector.tensor_tensor(late[:, t, :], dy_first[1][:, t, EARLY:J_TILE], banks[t][:, EARLY:J_TILE], SUBTRACT)
-        dr_grouped1 = sb("dr_grouped1", [P, J_TILE, PACK], BF16, "dy_first0")
-        gpsimd_group(dr_grouped1[:, 0:GPSIMD_SECOND, :], early[:, :, 0:GPSIMD_SECOND])
-        scatter(0, 0, scaled(accumulate(0, half_steps(0)), 0, 0, halves[0]), halves[0])
-        group(nc.scalar.copy, dr_grouped1[:, GPSIMD_SECOND:EARLY, :], early[:, :, GPSIMD_SECOND:EARLY])
-        group(nc.scalar.copy, dr_grouped1[:, EARLY:J_TILE, :], late[:])
-        quantize(dr_line[:, places(2, 2)], dr_line_scales[:, places(2, 2)], dr_grouped1[:], E4M3)
-        scatter(1, 0, scaled(accumulate(1, half_steps(0)), 1, 0, halves[0], 0), halves[0])
-        first_tier_whole(0, 1024)
-        window(2, 4096)
-        scatter(0, 0, scaled(accumulate(0, half_steps(1)), 0, 0, halves[1]), halves[1])
-        scatter(1, 0, scaled(accumulate(1, half_steps(1)), 1, 0, halves[1], 12288), halves[1])
-
-        first_tier_whole(1, 0)
-        quantize_weights_by_pass(2, group_weights_by_pass(2, [None, 20480]), 0)
-        banks = decode(dq_second[0][0][:], dq_second[0][1][:], 2)
-        decoded = sb("decoded", [P, GPSIMD_ROWS, J_TILE], F32, 12288)
-        left = [sb("left%d1" % g, [P, PACK, J_TILE], BF16, ["w_grouped20", None][g]) for g in range(PASSES)]
-        for t in range(GPSIMD_ROWS):
-            nc.scalar.copy(out=decoded[:, t, :], in_=banks[t][:])
-        nc.gpsimd.tensor_tensor(left[0][:, 0:GPSIMD_ROWS, :], dy_second[0][:, 0:GPSIMD_ROWS, :], decoded[:], SUBTRACT)
-        for t in range(GPSIMD_ROWS, PACK):
-            nc.vector.tensor_tensor(left[0][:, t, :], dy_second[0][:, t, :], banks[t][:], SUBTRACT)
-        banks = decode(dq_second[1][0][:], dq_second[1][1][:], 3)
-        for t in range(PACK):
-            nc.vector.tensor_tensor(left[1][:, t, :], dy_second[1][:, t, :], banks[t][:], SUBTRACT)
-        quantize_weights(3, group_weights(3, 20480), "dy_second0")
-        window(3, 21504)
-        scatter(2, 0, scaled(accumulate(2, first_steps), 2, 0, whole, 12288))
-
-        acc = accumulate(3, first_steps)
-        parts = [slice(0, EARLY_PLACES), slice(EARLY_PLACES, J_TILE)]
+        grouped = sb("grouped1", [P, PASSES * HALF, PACK], BF16, 10240)
         for g in range(PASSES):
-            grouped = sb("dr_whole%d" % g, [P, J_TILE, PACK], BF16, [17408, "w_grouped20"][g])
-            group(nc.scalar.copy, grouped[:], left[g][:])
-            quantize(dr_second[g][0][:], dr_second[g][1][:], grouped[:], E4M3)
-            scatter(3, 0, scaled(acc, 3, 0, parts[g], [None, "left11"][g]), parts[g])
+            group(scalar_cast, grouped[:, halves[g], :], dy_first[g, 1][:])
+        quantize(dq_first[1], whole, grouped[:], E5M2)
+        quantize(dr_first[0], halves[1], left[1][:], E4M3)
+        window(2, nc.gpsimd.memset, 8192)
+        left = sb("left1", [P, PASSES * HALF, PACK], BF16, 16384)
+        for b in range(4):
+            bank = decode(dq_first[1], b * BANK, b)
+            subtract(left[:, span(b * BANK, BANK), :], dy_first[b // 2, 1][:, :, span(b % 2 * BANK, BANK)], bank)
+        w_mx = {n: mx("w%d" % n, PASSES * P) for n in range(N_TILES)}
+        w_grouped = [sb("w_grouped%d" % n, [P, PASSES * P, PACK], BF16, [None, 16384 + 4096][n]) for n in range(2)]
+        for g in range(PASSES):
+            for n in range(2):
+                group(nc.scalar.copy, w_grouped[n][:, span(g * P, P), :], w_early[g][:, :, span(n * P, P)])
+        quantize(w_mx[0], span(0, PASSES * P), w_grouped[0][:], E4M3)
+        quantize(dr_first[1], whole, left[:], E4M3)
 
+        def weights(n):
+            return lambda g: (w_mx[n], g * P)
+
+        def first_steps(h, col):
+            steps = [(g, dq_first[h], g * HALF, HALF, E5M2, col) for g in range(PASSES)]
+            return steps + [(g, dr_first[h], g * HALF, HALF, E4M3, col) for g in range(PASSES)]
+
+        accs = {(0, 0): accumulate(weights(0), HALF, first_steps(0, 0), 0)}
+        dx = weigh("dx00", accs[0, 0][:], 0, wgo_sb[0][:, halves[0]], HALF, 24576)
+        quantize(w_mx[1], span(0, PASSES * P), w_grouped[1][:], E4M3)
+        window(3, nc.gpsimd.memset, 16384)
+        place(0, 0, HALF, dx)
+        for n, h in [(1, 0), (0, 1), (1, 1)]:
+            accs[n, h] = accumulate(weights(n), HALF, first_steps(h, 0), 2 * h + n)
+        weigh_and_place(1, 0, HALF, scaled("dx10", accs[1, 0][:], 1, HALF), wgo_sb[0][:, halves[0]])
+
+        dq_second = [mx("dq_second%d" % g, J_TILE, [24576, None][g]) for g in range(PASSES)]
+        grouped = sb("grouped20", [P, J_TILE, PACK], BF16)
+        for h in range(2):
+            group(scalar_cast, grouped[:, halves[h], :], dy_second[0][:, :, halves[h]])
+        quantize(dq_second[0], whole, grouped[:], E5M2)
+        grouped = sb("w_grouped2", [P, PASSES * P, PACK], BF16, 32768)
+        for g in range(PASSES):
+            group(nc.scalar.copy, grouped[:, span(g * P, P), :], w_third[g][:])
+        quantize(w_mx[2], span(0, PASSES * P), grouped[:], E4M3)
+        dx = [weigh("dx%d1" % n, accs[n, 1][:], n, wgo_sb[0][:, halves[1]], HALF, 26624 + 1024 * n) for n in range(2)]
+        for n in range(2):
+            place(n, HALF, HALF, dx[n])
+        banks = [decode(dq_second[0], b * BANK, b) for b in range(4)]
+        left = sb("left20", [P, J_TILE, PACK], BF16, 64512)
+        values = [sb("values00", [P, BANK, PACK], F32), sb("values01", [P, 2 * BANK, PACK], F32)]
+        unload(values[0][:], banks[0])
+        for b in range(2):
+            unload(values[1][:, span(b * BANK, BANK), :], banks[1 + b])
+        gpsimd_subtract(left[:, 0:BANK, :], dy_second[0][:, :, 0:BANK], values[0][:])
+        gpsimd_subtract(left[:, BANK : 3 * BANK, :], dy_second[0][:, :, BANK : 3 * BANK], values[1][:])
+        subtract(left[:, 3 * BANK : J_TILE, :], dy_second[0][:, :, 3 * BANK : J_TILE], banks[3])
+        acc = accumulate(weights(2), J_TILE, first_steps(0, 0) + first_steps(1, HALF), 0)
+
+        grouped = sb("grouped21", [P, J_TILE, PACK], BF16, 29696)
+        for h in range(2):
+            group(scalar_cast, grouped[:, halves[h], :], dy_second[1][:, :, halves[h]])
+        quantize(dq_second[1], whole, grouped[:], E5M2)
+        grouped = sb("w_grouped3", [P, PASSES * P, PACK], BF16, 33792)
+        for g in range(PASSES):
+            group(nc.scalar.copy, grouped[:, span(g * P, P), :], w_last[g][:])
+        quantize(w_mx[3], span(0, PASSES * P), grouped[:], E4M3)
+        dx = weigh("dx2", acc[:], 2, wgo_sb[0][:], J_TILE, 51200)
+        dr_second = [mx("dr_second%d" % g, J_TILE, [43008, None][g]) for g in range(PASSES)]
+        quantize(dr_second[0], whole, left[:], E4M3)
+        place(2, 0, J_TILE, dx)
+        banks = [decode(dq_second[1], b * BANK, b) for b in range(4)]
+        left = sb("left21", [P, J_TILE, PACK], BF16, 64512 + 2048)
+        values = [sb("values10", [P, BANK, PACK], F32), sb("values11", [P, 3 * BANK, PACK], F32)]
+        unload(values[0][:], banks[0])
+        for b in range(3):
+            unload(values[1][:, span(b * BANK, BANK), :], banks[1 + b])
+        gpsimd_subtract(left[:, 0:BANK, :], dy_second[1][:, :, 0:BANK], values[0][:])
+        gpsimd_subtract(left[:, BANK:J_TILE, :], dy_second[1][:, :, BANK:J_TILE], values[1][:])
+        acc = accumulate(weights(3), J_TILE, first_steps(0, 0) + first_steps(1, HALF), 1)
+        place(3, 0, HALF, weigh("dx30", acc[:, halves[0]], 3, wgo_sb[0][:, halves[0]], HALF, 64512))
+        quantize(dr_second[1], whole, left[:], E4M3)
+        weigh_and_place(3, HALF, HALF, scaled("dx31", acc[:, halves[1]], 3, HALF, 54272), wgo_sb[0][:, halves[1]])
+
+        second_steps = [(g, dq_second[g], 0, J_TILE, E5M2, 0) for g in range(PASSES)]
+        second_steps = second_steps + [(g, dr_second[g], 0, J_TILE, E4M3, 0) for g in range(PASSES)]
         for n in range(N_TILES):
-            scatter(n, 1, scaled(accumulate(n, second_steps), n, 1))
+            acc = accumulate(weights(n), J_TILE, second_steps, (2 + n) % 4)
+            weigh_and_place(n, J_TILE, J_TILE, scaled("dx_second%d" % n, acc[:], n, J_TILE), wgo_sb[1][:])
             nc.sync.dma_start(out=out[n * P : (n + 1) * P, :], in_=windows[n][:])

@@ -32,6 +32,7 @@ PAIR = 2
 QUAD = 32
 STRIP = K_PASS + 1
 VECTOR_SHARE = 160
+GPSIMD_PIECES = [slice(0, 128), slice(128, 512)]
 
 
 def tile_list_embg_tgf32_ls_kernel(tc, dy, w, ls, wgo, offs, out):
@@ -75,10 +76,10 @@ def tile_list_embg_tgf32_ls_kernel(tc, dy, w, ls, wgo, offs, out):
         ls_sb = sb("ls_sb", [P, N_TILES], F32)
         wgo_sb = [sb("wgo%d" % s, [P, J_TILE], F32) for s in range(2)]
         dy_first = {(g, h): sb("dy_first%d%d" % (g, h), [P, PACK, HALF], F32) for h in range(2) for g in range(PASSES)}
-        dy_second = [sb("dy_second%d" % g, [P, PACK, J_TILE], F32, [44032, 54272][g]) for g in range(PASSES)]
+        dy_second = [sb("dy_second%d" % g, [P, PACK, J_TILE], F32, [49152, None][g]) for g in range(PASSES)]
         w_early = [sb("w_early%d" % g, [P, PACK, 2 * P], F32) for g in range(PASSES)]
-        w_third = [sb("w_third%d" % g, [P, PACK, P], F32, [None, 26624][g]) for g in range(PASSES)]
-        w_last = [sb("w_last%d" % g, [P, PACK, P], F32, [41984, 52224][g]) for g in range(PASSES)]
+        w_third = [sb("w_third%d" % g, [P, PACK, P], F32, [8192, 40960][g]) for g in range(PASSES)]
+        w_last = [sb("w_last%d" % g, [P, PACK, P], F32, [None, 12288][g]) for g in range(PASSES)]
 
         for h in range(2):
             for g in range(PASSES):
@@ -89,13 +90,11 @@ def tile_list_embg_tgf32_ls_kernel(tc, dy, w, ls, wgo, offs, out):
             nc.sync.dma_start(out=ls_sb[:], in_=ls.rearrange("(c p) -> p c", p=P))
         nc.sync.dma_start(offsets[:], offs)
         nc.sync.dma_start(out=wgo_sb[0][:], in_=wgo[:, 0:J_TILE])
-        for h in range(2):
-            nc.sync.dma_start(out=dy_second[0][:, :, halves[h]], in_=k_rows(dy, 0, span(J_TILE + h * HALF, HALF)))
-        for g in range(PASSES):
-            nc.sync.dma_start(out=w_third[g][:], in_=k_rows(w, g, span(2 * P, P)))
-        nc.sync.dma_start(out=dy_second[1][:], in_=k_rows(dy, 1, span(J_TILE, J_TILE)))
-        for g in range(PASSES):
-            nc.sync.dma_start(out=w_last[g][:], in_=k_rows(w, g, span(3 * P, P)))
+        for s, w_tile in enumerate([w_third, w_last]):
+            for h in range(2):
+                nc.sync.dma_start(out=dy_second[s][:, :, halves[h]], in_=k_rows(dy, s, span(J_TILE + h * HALF, HALF)))
+            for g in range(PASSES):
+                nc.sync.dma_start(out=w_tile[g][:], in_=k_rows(w, g, span((2 + s) * P, P)))
         nc.sync.dma_start(out=wgo_sb[1][:], in_=wgo[:, J_TILE:J])
 
 
@@ -194,42 +193,45 @@ def tile_list_embg_tgf32_ls_kernel(tc, dy, w, ls, wgo, offs, out):
 
         window(0, nc.gpsimd.memset)
 
-
         dq_first = [mx("dq_first%d" % h, PASSES * HALF) for h in range(2)]
         dr_first = [mx("dr_first%d" % h, PASSES * HALF) for h in range(2)]
         grouped = [sb("grouped0%d" % g, [P, HALF, PACK], BF16, [0, None][g]) for g in range(PASSES)]
-        left = [sb("left0%d" % g, [P, HALF, PACK], BF16, [None, 8192][g]) for g in range(PASSES)]
+        left = sb("left0", [P, PASSES * HALF, PACK], BF16)
         group(nc.vector.tensor_copy, grouped[0][:, 0:VECTOR_SHARE, :], dy_first[0, 0][:, :, 0:VECTOR_SHARE])
         group(scalar_cast, grouped[0][:, VECTOR_SHARE:HALF, :], dy_first[0, 0][:, :, VECTOR_SHARE:HALF])
         quantize(dq_first[0], halves[0], grouped[0][:], E5M2)
         window(1, nc.vector.memset, 0)
         group(scalar_cast, grouped[1][:], dy_first[1, 0][:])
         banks = [decode(dq_first[0], b * BANK, b) for b in range(2)]
-        for b in range(2):
-            subtract(left[0][:, span(b * BANK, BANK), :], dy_first[0, 0][:, :, span(b * BANK, BANK)], banks[b])
+        subtract(left[:, 0:BANK, :], dy_first[0, 0][:, :, 0:BANK], banks[0])
         quantize(dq_first[0], halves[1], grouped[1][:], E5M2)
-        quantize(dr_first[0], halves[0], left[0][:], E4M3)
-        banks = [decode(dq_first[0], HALF + b * BANK, 2 + b) for b in range(2)]
+        subtract(left[:, BANK:HALF, :], dy_first[0, 0][:, :, BANK:HALF], banks[1])
         for b in range(2):
-            subtract(left[1][:, span(b * BANK, BANK), :], dy_first[1, 0][:, :, span(b * BANK, BANK)], banks[b])
+            bank = decode(dq_first[0], HALF + b * BANK, 2 + b)
+            subtract(left[:, span(HALF + b * BANK, BANK), :], dy_first[1, 0][:, :, span(b * BANK, BANK)], bank)
 
-        grouped = sb("grouped1", [P, PASSES * HALF, PACK], BF16, 10240)
+        grouped = [sb("grouped1%d" % g, [P, HALF, PACK], BF16) for g in range(PASSES)]
         for g in range(PASSES):
-            group(scalar_cast, grouped[:, halves[g], :], dy_first[g, 1][:])
-        quantize(dq_first[1], whole, grouped[:], E5M2)
-        quantize(dr_first[0], halves[1], left[1][:], E4M3)
-        window(2, nc.gpsimd.memset, 8192)
-        left = sb("left1", [P, PASSES * HALF, PACK], BF16, 16384)
-        for b in range(4):
-            bank = decode(dq_first[1], b * BANK, b)
-            subtract(left[:, span(b * BANK, BANK), :], dy_first[b // 2, 1][:, :, span(b % 2 * BANK, BANK)], bank)
-        w_mx = {n: mx("w%d" % n, PASSES * P) for n in range(N_TILES)}
-        w_grouped = [sb("w_grouped%d" % n, [P, PASSES * P, PACK], BF16, [None, 16384 + 4096][n]) for n in range(2)]
+            group(scalar_cast, grouped[g][:], dy_first[g, 1][:])
+        quantize(dq_first[1], halves[0], grouped[0][:], E5M2)
+        quantize(dr_first[0], whole, left[:], E4M3)
+        left = sb("left1", [P, PASSES * HALF, PACK], BF16)
+        banks = [decode(dq_first[1], b * BANK, b) for b in range(2)]
+        subtract(left[:, 0:BANK, :], dy_first[0, 1][:, :, 0:BANK], banks[0])
+        quantize(dq_first[1], halves[1], grouped[1][:], E5M2)
+        subtract(left[:, BANK:HALF, :], dy_first[0, 1][:, :, BANK:HALF], banks[1])
+        for b in range(2):
+            bank = decode(dq_first[1], HALF + b * BANK, 2 + b)
+            subtract(left[:, span(HALF + b * BANK, BANK), :], dy_first[1, 1][:, :, span(b * BANK, BANK)], bank)
+        w_mx = {n: mx("w%d" % n, PASSES * P, [None, None, None, 12288][n]) for n in range(N_TILES)}
+        w_grouped = [sb("w_grouped%d" % n, [P, PASSES * P, PACK], BF16, [None, 26624][n]) for n in range(2)]
         for g in range(PASSES):
             for n in range(2):
                 group(nc.scalar.copy, w_grouped[n][:, span(g * P, P), :], w_early[g][:, :, span(n * P, P)])
         quantize(w_mx[0], span(0, PASSES * P), w_grouped[0][:], E4M3)
         quantize(dr_first[1], whole, left[:], E4M3)
+        quantize(w_mx[1], span(0, PASSES * P), w_grouped[1][:], E4M3)
+        window(2, nc.gpsimd.memset, 19456)
 
         def weights(n):
             return lambda g: (w_mx[n], g * P)
@@ -238,66 +240,63 @@ def tile_list_embg_tgf32_ls_kernel(tc, dy, w, ls, wgo, offs, out):
             steps = [(g, dq_first[h], g * HALF, HALF, E5M2, col) for g in range(PASSES)]
             return steps + [(g, dr_first[h], g * HALF, HALF, E4M3, col) for g in range(PASSES)]
 
-        accs = {(0, 0): accumulate(weights(0), HALF, first_steps(0, 0), 0)}
-        dx = weigh("dx00", accs[0, 0][:], 0, wgo_sb[0][:, halves[0]], HALF, 24576)
-        quantize(w_mx[1], span(0, PASSES * P), w_grouped[1][:], E4M3)
-        window(3, nc.gpsimd.memset, 16384)
-        place(0, 0, HALF, dx)
-        for n, h in [(1, 0), (0, 1), (1, 1)]:
-            accs[n, h] = accumulate(weights(n), HALF, first_steps(h, 0), 2 * h + n)
-        weigh_and_place(1, 0, HALF, scaled("dx10", accs[1, 0][:], 1, HALF), wgo_sb[0][:, halves[0]])
-
-        dq_second = [mx("dq_second%d" % g, J_TILE, [24576, None][g]) for g in range(PASSES)]
-        grouped = sb("grouped20", [P, J_TILE, PACK], BF16)
-        for h in range(2):
-            group(scalar_cast, grouped[:, halves[h], :], dy_second[0][:, :, halves[h]])
-        quantize(dq_second[0], whole, grouped[:], E5M2)
-        grouped = sb("w_grouped2", [P, PASSES * P, PACK], BF16, 32768)
-        for g in range(PASSES):
-            group(nc.scalar.copy, grouped[:, span(g * P, P), :], w_third[g][:])
-        quantize(w_mx[2], span(0, PASSES * P), grouped[:], E4M3)
-        dx = [weigh("dx%d1" % n, accs[n, 1][:], n, wgo_sb[0][:, halves[1]], HALF, 26624 + 1024 * n) for n in range(2)]
+        accs = {(n, h): accumulate(weights(n), HALF, first_steps(h, 0), 2 * h + n) for h in range(2) for n in range(2)}
         for n in range(2):
-            place(n, HALF, HALF, dx[n])
-        banks = [decode(dq_second[0], b * BANK, b) for b in range(4)]
-        left = sb("left20", [P, J_TILE, PACK], BF16, 64512)
-        values = [sb("values00", [P, BANK, PACK], F32), sb("values01", [P, 2 * BANK, PACK], F32)]
-        unload(values[0][:], banks[0])
-        for b in range(2):
-            unload(values[1][:, span(b * BANK, BANK), :], banks[1 + b])
-        gpsimd_subtract(left[:, 0:BANK, :], dy_second[0][:, :, 0:BANK], values[0][:])
-        gpsimd_subtract(left[:, BANK : 3 * BANK, :], dy_second[0][:, :, BANK : 3 * BANK], values[1][:])
-        subtract(left[:, 3 * BANK : J_TILE, :], dy_second[0][:, :, 3 * BANK : J_TILE], banks[3])
+            dx = scaled("dx%d0" % n, accs[n, 0][:], n, HALF, [57344, None][n])
+            weigh_and_place(n, 0, HALF, dx, wgo_sb[0][:, halves[0]])
+
+        def stage(s, w_tile, at):
+            grouped = sb("stage%d" % s, [P, J_TILE + PASSES * P, PACK], BF16, at)
+            for h in range(2):
+                group(scalar_cast, grouped[:, halves[h], :], dy_second[s][:, :, halves[h]])
+            for g in range(PASSES):
+                group(nc.scalar.copy, grouped[:, span(J_TILE + g * P, P), :], w_tile[g][:])
+            return grouped[:, 0:J_TILE, :], grouped[:, span(J_TILE, PASSES * P), :]
+
+        dq_second = [mx("dq_second%d" % g, J_TILE, [57344, None][g]) for g in range(PASSES)]
+        dy_grouped, w_grouped = stage(0, w_third, 27648)
+        quantize(dq_second[0], whole, dy_grouped, E5M2)
+        quantize(w_mx[2], span(0, PASSES * P), w_grouped, E4M3)
+        window(3, nc.gpsimd.memset, 32768)
+        for n in range(2):
+            dx = scaled("dx%d1" % n, accs[n, 1][:], n, HALF, 8192 + 1024 * n)
+            weigh_and_place(n, HALF, HALF, dx, wgo_sb[0][:, halves[1]])
         acc = accumulate(weights(2), J_TILE, first_steps(0, 0) + first_steps(1, HALF), 0)
 
-        grouped = sb("grouped21", [P, J_TILE, PACK], BF16, 29696)
-        for h in range(2):
-            group(scalar_cast, grouped[:, halves[h], :], dy_second[1][:, :, halves[h]])
-        quantize(dq_second[1], whole, grouped[:], E5M2)
-        grouped = sb("w_grouped3", [P, PASSES * P, PACK], BF16, 33792)
-        for g in range(PASSES):
-            group(nc.scalar.copy, grouped[:, span(g * P, P), :], w_last[g][:])
-        quantize(w_mx[3], span(0, PASSES * P), grouped[:], E4M3)
-        dx = weigh("dx2", acc[:], 2, wgo_sb[0][:], J_TILE, 51200)
-        dr_second = [mx("dr_second%d" % g, J_TILE, [43008, None][g]) for g in range(PASSES)]
-        quantize(dr_second[0], whole, left[:], E4M3)
+        dy_grouped, w_grouped = stage(1, w_last, 40960)
+        values = sb("values0", [P, J_TILE, PACK], F32)
+        for b in range(4):
+            unload(values[:, span(b * BANK, BANK), :], decode(dq_second[0], b * BANK, b))
+        quantize(dq_second[1], whole, dy_grouped, E5M2)
+        dx = weigh("dx2", acc[:], 2, wgo_sb[0][:], J_TILE, 13312)
+        quantize(w_mx[3], span(0, PASSES * P), w_grouped, E4M3)
         place(2, 0, J_TILE, dx)
+        left = sb("left20", [P, J_TILE, PACK], BF16, 43008)
+        for cols in GPSIMD_PIECES:
+            gpsimd_subtract(left[:, cols, :], dy_second[0][:, :, cols], values[:, cols, :])
+        most, rest = span(0, 3 * BANK), span(3 * BANK, BANK)
+        left_most = sb("left_most", [P, 3 * BANK, PACK], BF16, 59392)
         banks = [decode(dq_second[1], b * BANK, b) for b in range(4)]
-        left = sb("left21", [P, J_TILE, PACK], BF16, 64512 + 2048)
-        values = [sb("values10", [P, BANK, PACK], F32), sb("values11", [P, 3 * BANK, PACK], F32)]
-        unload(values[0][:], banks[0])
+        values = sb("values1", [P, BANK, PACK], F32, 63488)
+        unload(values[:], banks[3])
         for b in range(3):
-            unload(values[1][:, span(b * BANK, BANK), :], banks[1 + b])
-        gpsimd_subtract(left[:, 0:BANK, :], dy_second[1][:, :, 0:BANK], values[0][:])
-        gpsimd_subtract(left[:, BANK:J_TILE, :], dy_second[1][:, :, BANK:J_TILE], values[1][:])
+            subtract(left_most[:, span(b * BANK, BANK), :], dy_second[1][:, :, span(b * BANK, BANK)], banks[b])
         acc = accumulate(weights(3), J_TILE, first_steps(0, 0) + first_steps(1, HALF), 1)
-        place(3, 0, HALF, weigh("dx30", acc[:, halves[0]], 3, wgo_sb[0][:, halves[0]], HALF, 64512))
-        quantize(dr_second[1], whole, left[:], E4M3)
-        weigh_and_place(3, HALF, HALF, scaled("dx31", acc[:, halves[1]], 3, HALF, 54272), wgo_sb[0][:, halves[1]])
+        dx = weigh("dx30", acc[:, halves[0]], 3, wgo_sb[0][:, halves[0]], HALF, 49152)
+        dr_second = [mx("dr_second%d" % g, J_TILE, [50176, 52224][g]) for g in range(PASSES)]
+        quantize(dr_second[0], whole, left[:], E4M3)
+        quantize(dr_second[1], most, left_most[:], E4M3)
+        place(3, 0, HALF, dx)
+        left_rest = sb("left_rest", [P, BANK, PACK], BF16, 59392)
+        gpsimd_subtract(left_rest[:], dy_second[1][:, :, rest], values[:])
+        quantize(dr_second[1], rest, left_rest[:], E4M3)
+        weigh_and_place(3, HALF, HALF, scaled("dx31", acc[:, halves[1]], 3, HALF, 63488), wgo_sb[0][:, halves[1]])
 
         second_steps = [(g, dq_second[g], 0, J_TILE, E5M2, 0) for g in range(PASSES)]
-        second_steps = second_steps + [(g, dr_second[g], 0, J_TILE, E4M3, 0) for g in range(PASSES)]
+        second_steps = second_steps + [(0, dr_second[0], 0, J_TILE, E4M3, 0)]
+        cut = [(1, dr_second[1], first, count, E4M3, first) for first, count in [(0, HALF), (HALF, BANK), (3 * BANK, BANK)]]
         for n in range(N_TILES):
-            acc = accumulate(weights(n), J_TILE, second_steps, (2 + n) % 4)
+            last = cut if n == 0 else [(1, dr_second[1], 0, J_TILE, E4M3, 0)]
+            acc = accumulate(weights(n), J_TILE, second_steps + last, (2 + n) % 4)
             weigh_and_place(n, J_TILE, J_TILE, scaled("dx_second%d" % n, acc[:], n, J_TILE), wgo_sb[1][:])
             nc.sync.dma_start(out=out[n * P : (n + 1) * P, :], in_=windows[n][:])

@@ -75,17 +75,25 @@ def tile_list_embg_tgf32_ls_kernel(tc, dy, w, ls, wgo, offs, out):
         offsets = keep.tile([P, J // LIST_GROUP], U16, name="offsets")
         ls_sb = sb("ls_sb", [P, N_TILES], F32)
         wgo_sb = [sb("wgo%d" % s, [P, J_TILE], F32) for s in range(2)]
-        dy_first = {(g, h): sb("dy_first%d%d" % (g, h), [P, PACK, HALF], F32) for h in range(2) for g in range(PASSES)}
-        dy_second = [sb("dy_second%d" % g, [P, PACK, J_TILE], F32, [49152, None][g]) for g in range(PASSES)]
-        w_early = [sb("w_early%d" % g, [P, PACK, 2 * P], F32) for g in range(PASSES)]
+        dy_first = {(g, h): sb("dy_first%d%d" % (g, h), [P, PACK, HALF], F32, {(0, 1): 71680, (1, 1): 57344}.get((g, h))) for h in range(2) for g in range(PASSES)}
+        dy_second = [sb("dy_second%d" % g, [P, PACK, J_TILE], F32) for g in range(PASSES)]
+        w_early = {(n, g): sb("w_early%d%d" % (n, g), [P, PACK, P], F32) for n in range(2) for g in range(PASSES)}
         w_third = [sb("w_third%d" % g, [P, PACK, P], F32, [8192, 40960][g]) for g in range(PASSES)]
         w_last = [sb("w_last%d" % g, [P, PACK, P], F32, [None, 12288][g]) for g in range(PASSES)]
 
-        for h in range(2):
+        def load_dy(g, h):
+            nc.sync.dma_start(out=dy_first[g, h][:], in_=k_rows(dy, g, halves[h]))
+
+        def load_w(n):
             for g in range(PASSES):
-                nc.sync.dma_start(out=dy_first[g, h][:], in_=k_rows(dy, g, halves[h]))
-        for g in range(PASSES):
-            nc.sync.dma_start(out=w_early[g][:], in_=k_rows(w, g, span(0, 2 * P)))
+                nc.sync.dma_start(out=w_early[n, g][:], in_=k_rows(w, g, span(n * P, P)))
+
+        load_dy(0, 0)
+        load_dy(1, 0)
+        load_dy(0, 1)
+        load_w(0)
+        load_dy(1, 1)
+        load_w(1)
         with nc.allow_non_contiguous_dma(reason="one factor for each partition and n tile"):
             nc.sync.dma_start(out=ls_sb[:], in_=ls.rearrange("(c p) -> p c", p=P))
         nc.sync.dma_start(offsets[:], offs)
@@ -134,7 +142,7 @@ def tile_list_embg_tgf32_ls_kernel(tc, dy, w, ls, wgo, offs, out):
             nc.gpsimd.tensor_tensor(left, rows.rearrange("p t c -> p c t"), values, SUBTRACT)
 
         def accumulate(weights, width, steps, tag):
-            acc = psum.tile([P, width], F32, name="acc", tag="acc%d" % tag)
+            acc = psum.tile([P, width], F32, name="acc", tag=tag if isinstance(tag, str) else "acc%d" % tag)
             for i, (g, (codes, scales), first, count, fmt, col) in enumerate(steps):
                 (w_codes, w_scales), w_first = weights(g)
                 nc.tensor.matmul_mx(
@@ -210,12 +218,20 @@ def tile_list_embg_tgf32_ls_kernel(tc, dy, w, ls, wgo, offs, out):
             bank = decode(dq_first[0], HALF + b * BANK, 2 + b)
             subtract(left[:, span(HALF + b * BANK, BANK), :], dy_first[1, 0][:, :, span(b * BANK, BANK)], bank)
 
+        def group_weights(n, at=None):
+            grouped = sb("w_grouped%d" % n, [P, PASSES * P, PACK], BF16, at)
+            for g in range(PASSES):
+                group(nc.scalar.copy, grouped[:, span(g * P, P), :], w_early[n, g][:])
+            return grouped
+
+        w_mx = {n: mx("w%d" % n, PASSES * P, [None, 71680, None, 12288][n]) for n in range(N_TILES)}
         grouped = [sb("grouped1%d" % g, [P, HALF, PACK], BF16) for g in range(PASSES)]
-        for g in range(PASSES):
-            group(scalar_cast, grouped[g][:], dy_first[g, 1][:])
+        group(scalar_cast, grouped[0][:], dy_first[0, 1][:])
         quantize(dq_first[1], halves[0], grouped[0][:], E5M2)
         quantize(dr_first[0], whole, left[:], E4M3)
-        left = sb("left1", [P, PASSES * HALF, PACK], BF16)
+        quantize(w_mx[0], span(0, PASSES * P), group_weights(0)[:], E4M3)
+        group(scalar_cast, grouped[1][:], dy_first[1, 1][:])
+        left = sb("left1", [P, PASSES * HALF, PACK], BF16, 19456)
         banks = [decode(dq_first[1], b * BANK, b) for b in range(2)]
         subtract(left[:, 0:BANK, :], dy_first[0, 1][:, :, 0:BANK], banks[0])
         quantize(dq_first[1], halves[1], grouped[1][:], E5M2)
@@ -223,14 +239,8 @@ def tile_list_embg_tgf32_ls_kernel(tc, dy, w, ls, wgo, offs, out):
         for b in range(2):
             bank = decode(dq_first[1], HALF + b * BANK, 2 + b)
             subtract(left[:, span(HALF + b * BANK, BANK), :], dy_first[1, 1][:, :, span(b * BANK, BANK)], bank)
-        w_mx = {n: mx("w%d" % n, PASSES * P, [None, None, None, 12288][n]) for n in range(N_TILES)}
-        w_grouped = [sb("w_grouped%d" % n, [P, PASSES * P, PACK], BF16, [None, 26624][n]) for n in range(2)]
-        for g in range(PASSES):
-            for n in range(2):
-                group(nc.scalar.copy, w_grouped[n][:, span(g * P, P), :], w_early[g][:, :, span(n * P, P)])
-        quantize(w_mx[0], span(0, PASSES * P), w_grouped[0][:], E4M3)
+        quantize(w_mx[1], span(0, PASSES * P), group_weights(1, 26624)[:], E4M3)
         quantize(dr_first[1], whole, left[:], E4M3)
-        quantize(w_mx[1], span(0, PASSES * P), w_grouped[1][:], E4M3)
         window(2, nc.gpsimd.memset, 19456)
 
         def weights(n):
@@ -275,28 +285,27 @@ def tile_list_embg_tgf32_ls_kernel(tc, dy, w, ls, wgo, offs, out):
         for cols in GPSIMD_PIECES:
             gpsimd_subtract(left[:, cols, :], dy_second[0][:, :, cols], values[:, cols, :])
         most, rest = span(0, 3 * BANK), span(3 * BANK, BANK)
-        left_most = sb("left_most", [P, 3 * BANK, PACK], BF16, 59392)
+        left_last = sb("left21", [P, J_TILE, PACK], BF16)
         banks = [decode(dq_second[1], b * BANK, b) for b in range(4)]
         values = sb("values1", [P, BANK, PACK], F32, 63488)
         unload(values[:], banks[3])
-        for b in range(3):
-            subtract(left_most[:, span(b * BANK, BANK), :], dy_second[1][:, :, span(b * BANK, BANK)], banks[b])
+        gpsimd_subtract(left_last[:, rest, :], dy_second[1][:, :, rest], values[:])
         acc = accumulate(weights(3), J_TILE, first_steps(0, 0) + first_steps(1, HALF), 1)
-        dx = weigh("dx30", acc[:, halves[0]], 3, wgo_sb[0][:, halves[0]], HALF, 49152)
-        dr_second = [mx("dr_second%d" % g, J_TILE, [50176, 52224][g]) for g in range(PASSES)]
-        quantize(dr_second[0], whole, left[:], E4M3)
-        quantize(dr_second[1], most, left_most[:], E4M3)
+        dx = weigh("dx30", acc[:, halves[0]], 3, wgo_sb[0][:, halves[0]], HALF)
+        for b in range(3):
+            subtract(left_last[:, span(b * BANK, BANK), :], dy_second[1][:, :, span(b * BANK, BANK)], banks[b])
         place(3, 0, HALF, dx)
-        left_rest = sb("left_rest", [P, BANK, PACK], BF16, 59392)
-        gpsimd_subtract(left_rest[:], dy_second[1][:, :, rest], values[:])
-        quantize(dr_second[1], rest, left_rest[:], E4M3)
+        dr_line = mx("dr_second", PASSES * J_TILE, 63488 + 1024)
+        quantize(dr_line, whole, left[:], E4M3)
+        quantize(dr_line, span(J_TILE, 3 * BANK), left_last[:, most, :], E4M3)
+        quantize(dr_line, span(J_TILE + 3 * BANK, BANK), left_last[:, rest, :], E4M3)
         weigh_and_place(3, HALF, HALF, scaled("dx31", acc[:, halves[1]], 3, HALF, 63488), wgo_sb[0][:, halves[1]])
 
         second_steps = [(g, dq_second[g], 0, J_TILE, E5M2, 0) for g in range(PASSES)]
-        second_steps = second_steps + [(0, dr_second[0], 0, J_TILE, E4M3, 0)]
-        cut = [(1, dr_second[1], first, count, E4M3, first) for first, count in [(0, HALF), (HALF, BANK), (3 * BANK, BANK)]]
+        second_steps = second_steps + [(0, dr_line, 0, J_TILE, E4M3, 0)]
+        cut = [(1, dr_line, J_TILE + first, count, E4M3, first) for first, count in [(0, HALF), (HALF, BANK), (3 * BANK, BANK)]]
         for n in range(N_TILES):
-            last = cut if n == 0 else [(1, dr_second[1], 0, J_TILE, E4M3, 0)]
-            acc = accumulate(weights(n), J_TILE, second_steps + last, (2 + n) % 4)
+            last = cut if n == 0 else [(1, dr_line, J_TILE, J_TILE, E4M3, 0)]
+            acc = accumulate(weights(n), J_TILE, second_steps + last, [2, "decode2"][n % 2])
             weigh_and_place(n, J_TILE, J_TILE, scaled("dx_second%d" % n, acc[:], n, J_TILE), wgo_sb[1][:])
             nc.sync.dma_start(out=out[n * P : (n + 1) * P, :], in_=windows[n][:])

@@ -31,8 +31,9 @@ RUN = 4
 PAIR = 2
 QUAD = 32
 STRIP = K_PASS + 1
-VECTOR_SHARE = 160
-GPSIMD_PIECES = [slice(0, 128), slice(128, 512)]
+GPSIMD_PIECES = [slice(0, 128), slice(128, 256), slice(256, 512)]
+TURNED = 2
+GPSIMD_REST = 32
 
 
 def tile_list_embg_tgf32_ls_kernel(tc, dy, w, ls, wgo, offs, out):
@@ -88,11 +89,13 @@ def tile_list_embg_tgf32_ls_kernel(tc, dy, w, ls, wgo, offs, out):
             for g in range(PASSES):
                 nc.sync.dma_start(out=w_early[n, g][:], in_=k_rows(w, g, span(n * P, P)))
 
-        load_dy(0, 0)
+        for b in range(2):
+            cols = span(b * BANK, BANK)
+            nc.sync.dma_start(out=dy_first[0, 0][:, :, cols], in_=k_rows(dy, 0, cols))
         load_dy(1, 0)
         load_dy(0, 1)
-        load_w(0)
         load_dy(1, 1)
+        load_w(0)
         load_w(1)
         with nc.allow_non_contiguous_dma(reason="one factor for each partition and n tile"):
             nc.sync.dma_start(out=ls_sb[:], in_=ls.rearrange("(c p) -> p c", p=P))
@@ -131,7 +134,7 @@ def tile_list_embg_tgf32_ls_kernel(tc, dy, w, ls, wgo, offs, out):
             nc.vector.tensor_tensor(
                 left.rearrange("p (c i) t -> p c t i", i=PAIR),
                 rows.rearrange("p t (c i) -> p c t i", i=PAIR),
-                bank[:].rearrange("p t (c i) -> p c t i", i=PAIR),
+                bank[:, :, :].rearrange("p t (c i) -> p c t i", i=PAIR),
                 SUBTRACT,
             )
 
@@ -201,44 +204,52 @@ def tile_list_embg_tgf32_ls_kernel(tc, dy, w, ls, wgo, offs, out):
 
         window(0, nc.gpsimd.memset)
 
-        dq_first = [mx("dq_first%d" % h, PASSES * HALF) for h in range(2)]
-        dr_first = [mx("dr_first%d" % h, PASSES * HALF) for h in range(2)]
-        grouped = [sb("grouped0%d" % g, [P, HALF, PACK], BF16, [0, None][g]) for g in range(PASSES)]
-        left = sb("left0", [P, PASSES * HALF, PACK], BF16)
-        group(nc.vector.tensor_copy, grouped[0][:, 0:VECTOR_SHARE, :], dy_first[0, 0][:, :, 0:VECTOR_SHARE])
-        group(scalar_cast, grouped[0][:, VECTOR_SHARE:HALF, :], dy_first[0, 0][:, :, VECTOR_SHARE:HALF])
-        quantize(dq_first[0], halves[0], grouped[0][:], E5M2)
-        window(1, nc.vector.memset, 0)
-        group(scalar_cast, grouped[1][:], dy_first[1, 0][:])
-        banks = [decode(dq_first[0], b * BANK, b) for b in range(2)]
-        subtract(left[:, 0:BANK, :], dy_first[0, 0][:, :, 0:BANK], banks[0])
-        quantize(dq_first[0], halves[1], grouped[1][:], E5M2)
-        subtract(left[:, BANK:HALF, :], dy_first[0, 0][:, :, BANK:HALF], banks[1])
-        for b in range(2):
-            bank = decode(dq_first[0], HALF + b * BANK, 2 + b)
-            subtract(left[:, span(HALF + b * BANK, BANK), :], dy_first[1, 0][:, :, span(b * BANK, BANK)], bank)
-
         def group_weights(n, at=None):
             grouped = sb("w_grouped%d" % n, [P, PASSES * P, PACK], BF16, at)
             for g in range(PASSES):
                 group(nc.scalar.copy, grouped[:, span(g * P, P), :], w_early[n, g][:])
             return grouped
 
-        w_mx = {n: mx("w%d" % n, PASSES * P, [None, 71680, None, 12288][n]) for n in range(N_TILES)}
-        grouped = [sb("grouped1%d" % g, [P, HALF, PACK], BF16) for g in range(PASSES)]
-        group(scalar_cast, grouped[0][:], dy_first[0, 1][:])
-        quantize(dq_first[1], halves[0], grouped[0][:], E5M2)
-        quantize(dr_first[0], whole, left[:], E4M3)
-        quantize(w_mx[0], span(0, PASSES * P), group_weights(0)[:], E4M3)
-        group(scalar_cast, grouped[1][:], dy_first[1, 1][:])
-        left = sb("left1", [P, PASSES * HALF, PACK], BF16, 19456)
-        banks = [decode(dq_first[1], b * BANK, b) for b in range(2)]
-        subtract(left[:, 0:BANK, :], dy_first[0, 1][:, :, 0:BANK], banks[0])
-        quantize(dq_first[1], halves[1], grouped[1][:], E5M2)
-        subtract(left[:, BANK:HALF, :], dy_first[0, 1][:, :, BANK:HALF], banks[1])
+        w_mx = {n: mx("w%d" % n, PASSES * P, [0 + 75776, 71680, None, 12288][n]) for n in range(N_TILES)}
+        dq_first = [mx("dq_first%d" % h, PASSES * HALF) for h in range(2)]
+        dr_first = [mx("dr_first%d" % h, PASSES * HALF) for h in range(2)]
+        grouped = {(g, h): sb("grouped%d%d" % (g, h), [P, HALF, PACK], BF16, {(1, 1): 75776}.get((g, h))) for g, h in [(1, 0), (0, 1), (1, 1)]}
+        first = [sb("first%d" % b, [P, BANK, PACK], BF16, [0, None][b]) for b in range(2)]
+        lefts = [sb("left%d" % h, [P, PASSES * HALF, PACK], BF16, [None, 19456][h]) for h in range(2)]
+        banks = {}
+
+        def first_tier(g, h):
+            quantize(dq_first[h], halves[g], grouped[g, h][:], E5M2)
+            for b in range(2):
+                banks[g, h, b] = decode(dq_first[h], g * HALF + b * BANK, 2 * g + b)
+
+        def residual(g, h, b):
+            subtract(lefts[h][:, span(g * HALF + b * BANK, BANK), :], dy_first[g, h][:, :, span(b * BANK, BANK)], banks[g, h, b])
+
         for b in range(2):
-            bank = decode(dq_first[1], HALF + b * BANK, 2 + b)
-            subtract(left[:, span(HALF + b * BANK, BANK), :], dy_first[1, 1][:, :, span(b * BANK, BANK)], bank)
+            cols = span(b * BANK, BANK)
+            group(scalar_cast, first[b][:], dy_first[0, 0][:, :, cols])
+        for g, h in [(1, 0), (0, 1), (1, 1)]:
+            group(scalar_cast, grouped[g, h][:], dy_first[g, h][:])
+        quantize(dq_first[0], span(0, BANK), first[0][:], E5M2)
+        banks[0, 0, 0] = decode(dq_first[0], 0, 0)
+        window(1, nc.vector.memset, 0)
+        quantize(dq_first[0], span(BANK, BANK), first[1][:], E5M2)
+        banks[0, 0, 1] = decode(dq_first[0], BANK, 1)
+        residual(0, 0, 0)
+        first_tier(1, 0)
+        residual(0, 0, 1)
+        first_tier(0, 1)
+        residual(1, 0, 0)
+        residual(1, 0, 1)
+        residual(0, 1, 0)
+        quantize(dr_first[0], whole, lefts[0][:], E4M3)
+        first_tier(1, 1)
+        residual(0, 1, 1)
+        quantize(w_mx[0], span(0, PASSES * P), group_weights(0)[:], E4M3)
+        residual(1, 1, 0)
+        residual(1, 1, 1)
+        left = lefts[1]
         quantize(w_mx[1], span(0, PASSES * P), group_weights(1, 26624)[:], E4M3)
         quantize(dr_first[1], whole, left[:], E4M3)
         window(2, nc.gpsimd.memset, 19456)
@@ -263,6 +274,9 @@ def tile_list_embg_tgf32_ls_kernel(tc, dy, w, ls, wgo, offs, out):
                 group(nc.scalar.copy, grouped[:, span(J_TILE + g * P, P), :], w_tile[g][:])
             return grouped[:, 0:J_TILE, :], grouped[:, span(J_TILE, PASSES * P), :]
 
+        identity = sb("identity", [P, P], F32)
+        nc.scalar.copy(out=identity[:], in_=strip[:, 0:K_PASS:PACK])
+
         dq_second = [mx("dq_second%d" % g, J_TILE, [57344, None][g]) for g in range(PASSES)]
         dy_grouped, w_grouped = stage(0, w_third, 27648)
         quantize(dq_second[0], whole, dy_grouped, E5M2)
@@ -274,38 +288,60 @@ def tile_list_embg_tgf32_ls_kernel(tc, dy, w, ls, wgo, offs, out):
         acc = accumulate(weights(2), J_TILE, first_steps(0, 0) + first_steps(1, HALF), 0)
 
         dy_grouped, w_grouped = stage(1, w_last, 40960)
-        values = sb("values0", [P, J_TILE, PACK], F32)
-        for b in range(4):
-            unload(values[:, span(b * BANK, BANK), :], decode(dq_second[0], b * BANK, b))
+        values = sb("values0", [P, J_TILE + GPSIMD_REST, PACK], F32, 79872)
+        early = [decode(dq_second[0], b * BANK, b) for b in range(4)]
+        for b in range(2):
+            unload(values[:, span(b * BANK, BANK), :], early[b])
         quantize(dq_second[1], whole, dy_grouped, E5M2)
         dx = weigh("dx2", acc[:], 2, wgo_sb[0][:], J_TILE, 13312)
         quantize(w_mx[3], span(0, PASSES * P), w_grouped, E4M3)
         place(2, 0, J_TILE, dx)
+        acc = accumulate(weights(3), J_TILE, first_steps(0, 0) + first_steps(1, HALF), 1)
         left = sb("left20", [P, J_TILE, PACK], BF16, 43008)
+        left_last = sb("left21", [P, J_TILE, PACK], BF16)
+
+        negated = [sb("negated%d" % b, [P, PACK, BANK], F32) for b in range(TURNED)]
+        rounded = [sb("rounded%d" % b, [P, 2, P, 2], BF16) for b in range(TURNED)]
+        for b in range(TURNED):
+            nc.scalar.activation(out=negated[b][:], in_=decode(dq_second[1], b * BANK, b)[:], func=COPY, scale=-1.0)
+        for b in range(TURNED):
+            unload(values[:, span((2 + b) * BANK, BANK), :], early[2 + b])
+            sums = psum.tile([P, PACK, P], F32, name="sums", tag=["acc3", "decode0"][b])
+            terms = [dy_second[1][:, t, span(b * BANK, BANK)] for t in range(PACK)] + [negated[b][:, t, :] for t in range(PACK)]
+            for i, term in enumerate(terms):
+                nc.tensor.matmul(sums[:, i % PACK, :], term, identity[:], start=(i == 0), stop=(i == len(terms) - 1), is_transpose=True)
+            nc.scalar.copy(out=rounded[b][:], in_=sums[:].rearrange("j (u e) p -> j u p e", e=2))
+        words = psum.tile([P, TURNED, 2, BANK], F32, name="words", tag="decode1")
+        for b in range(TURNED):
+            pairs = rounded[b][:].rearrange("j u p e -> j (u p e)").bitcast(F32)
+            for u in range(2):
+                nc.tensor.transpose(words[:, b, u, :], pairs[:, span(u * P, P)], identity[:])
+        nc.scalar.copy(
+            out=left_last[:, 0 : TURNED * BANK, :].rearrange("p c t -> p (c t)").bitcast(F32).rearrange("p (b j u) -> p b j u", b=TURNED, u=2),
+            in_=words[:].rearrange("p b u j -> p b j u"),
+        )
         for cols in GPSIMD_PIECES:
             gpsimd_subtract(left[:, cols, :], dy_second[0][:, :, cols], values[:, cols, :])
-        most, rest = span(0, 3 * BANK), span(3 * BANK, BANK)
-        left_last = sb("left21", [P, J_TILE, PACK], BF16)
-        banks = [decode(dq_second[1], b * BANK, b) for b in range(4)]
-        values = sb("values1", [P, BANK, PACK], F32, 63488)
-        unload(values[:], banks[3])
-        gpsimd_subtract(left_last[:, rest, :], dy_second[1][:, :, rest], values[:])
-        acc = accumulate(weights(3), J_TILE, first_steps(0, 0) + first_steps(1, HALF), 1)
+        banks = {b: decode(dq_second[1], b * BANK, b) for b in range(TURNED, 4)}
         dx = weigh("dx30", acc[:, halves[0]], 3, wgo_sb[0][:, halves[0]], HALF)
-        for b in range(3):
-            subtract(left_last[:, span(b * BANK, BANK), :], dy_second[1][:, :, span(b * BANK, BANK)], banks[b])
+        mine = BANK - GPSIMD_REST
+        theirs = span(J_TILE - GPSIMD_REST, GPSIMD_REST)
+        nc.scalar.copy(out=values[:, span(J_TILE, GPSIMD_REST), :], in_=banks[3][:, :, mine:BANK].rearrange("p t c -> p c t"))
+        gpsimd_subtract(left_last[:, theirs, :], dy_second[1][:, :, theirs], values[:, span(J_TILE, GPSIMD_REST), :])
+        subtract(left_last[:, span(2 * BANK, BANK), :], dy_second[1][:, :, span(2 * BANK, BANK)], banks[2])
+        subtract(left_last[:, span(3 * BANK, mine), :], dy_second[1][:, :, span(3 * BANK, mine)], banks[3][:, :, 0:mine])
         place(3, 0, HALF, dx)
-        dr_line = mx("dr_second", PASSES * J_TILE, 63488 + 1024)
+        dr_line = mx("dr_second", PASSES * J_TILE, 79872 + 1024)
         quantize(dr_line, whole, left[:], E4M3)
-        quantize(dr_line, span(J_TILE, 3 * BANK), left_last[:, most, :], E4M3)
-        quantize(dr_line, span(J_TILE + 3 * BANK, BANK), left_last[:, rest, :], E4M3)
-        weigh_and_place(3, HALF, HALF, scaled("dx31", acc[:, halves[1]], 3, HALF, 63488), wgo_sb[0][:, halves[1]])
+        for h in (1, 0):
+            quantize(dr_line, span(J_TILE + h * HALF, HALF), left_last[:, halves[h], :], E4M3)
+        weigh_and_place(3, HALF, HALF, scaled("dx31", acc[:, halves[1]], 3, HALF, 79872), wgo_sb[0][:, halves[1]])
 
         second_steps = [(g, dq_second[g], 0, J_TILE, E5M2, 0) for g in range(PASSES)]
         second_steps = second_steps + [(0, dr_line, 0, J_TILE, E4M3, 0)]
-        cut = [(1, dr_line, J_TILE + first, count, E4M3, first) for first, count in [(0, HALF), (HALF, BANK), (3 * BANK, BANK)]]
+        cut = [(1, dr_line, J_TILE + first, count, E4M3, first) for first, count in [(HALF, HALF), (0, HALF)]]
         for n in range(N_TILES):
-            last = cut if n == 0 else [(1, dr_line, J_TILE, J_TILE, E4M3, 0)]
-            acc = accumulate(weights(n), J_TILE, second_steps + last, [2, "decode2"][n % 2])
+            steps = second_steps + cut if n == 0 else second_steps[0:2] + [(1, dr_line, J_TILE, J_TILE, E4M3, 0)] + second_steps[2:3]
+            acc = accumulate(weights(n), J_TILE, steps, [2, "decode3"][n % 2])
             weigh_and_place(n, J_TILE, J_TILE, scaled("dx_second%d" % n, acc[:], n, J_TILE), wgo_sb[1][:])
             nc.sync.dma_start(out=out[n * P : (n + 1) * P, :], in_=windows[n][:])

@@ -78,16 +78,12 @@ def tile_list_embg_tgf32_ls_kernel(tc, dy, w, ls, wgo, offs, out):
         wgo_sb = [sb("wgo%d" % s, [P, J_TILE], F32) for s in range(2)]
         dy_first = {(g, h): sb("dy_first%d%d" % (g, h), [P, PACK, HALF], F32, {(0, 1): 71680, (1, 1): 57344}.get((g, h))) for h in range(2) for g in range(PASSES)}
         dy_second = [sb("dy_second%d" % g, [P, PACK, J_TILE], F32) for g in range(PASSES)]
-        w_early = {(n, g): sb("w_early%d%d" % (n, g), [P, PACK, P], F32) for n in range(2) for g in range(PASSES)}
+        w_early = [sb("w_early%d" % g, [P, PACK, 2 * P], F32) for g in range(PASSES)]
         w_third = [sb("w_third%d" % g, [P, PACK, P], F32, [8192, 40960][g]) for g in range(PASSES)]
-        w_last = [sb("w_last%d" % g, [P, PACK, P], F32, [None, 12288][g]) for g in range(PASSES)]
+        w_last = [sb("w_last%d" % g, [P, PACK, P], F32, [14336, 12288][g]) for g in range(PASSES)]
 
         def load_dy(g, h):
             nc.sync.dma_start(out=dy_first[g, h][:], in_=k_rows(dy, g, halves[h]))
-
-        def load_w(n):
-            for g in range(PASSES):
-                nc.sync.dma_start(out=w_early[n, g][:], in_=k_rows(w, g, span(n * P, P)))
 
         for b in range(2):
             cols = span(b * BANK, BANK)
@@ -95,8 +91,8 @@ def tile_list_embg_tgf32_ls_kernel(tc, dy, w, ls, wgo, offs, out):
         load_dy(1, 0)
         load_dy(0, 1)
         load_dy(1, 1)
-        load_w(0)
-        load_w(1)
+        for g in range(PASSES):
+            nc.sync.dma_start(out=w_early[g][:], in_=k_rows(w, g, span(0, 2 * P)))
         with nc.allow_non_contiguous_dma(reason="one factor for each partition and n tile"):
             nc.sync.dma_start(out=ls_sb[:], in_=ls.rearrange("(c p) -> p c", p=P))
         nc.sync.dma_start(offsets[:], offs)
@@ -207,7 +203,7 @@ def tile_list_embg_tgf32_ls_kernel(tc, dy, w, ls, wgo, offs, out):
         def group_weights(n, at=None):
             grouped = sb("w_grouped%d" % n, [P, PASSES * P, PACK], BF16, at)
             for g in range(PASSES):
-                group(nc.scalar.copy, grouped[:, span(g * P, P), :], w_early[n, g][:])
+                group(nc.scalar.copy, grouped[:, span(g * P, P), :], w_early[g][:, :, span(n * P, P)])
             return grouped
 
         w_mx = {n: mx("w%d" % n, PASSES * P, [0 + 75776, 71680, None, 12288][n]) for n in range(N_TILES)}
@@ -293,7 +289,7 @@ def tile_list_embg_tgf32_ls_kernel(tc, dy, w, ls, wgo, offs, out):
         for b in range(2):
             unload(values[:, span(b * BANK, BANK), :], early[b])
         quantize(dq_second[1], whole, dy_grouped, E5M2)
-        dx = weigh("dx2", acc[:], 2, wgo_sb[0][:], J_TILE, 13312)
+        dx = weigh("dx2", acc[:], 2, wgo_sb[0][:], J_TILE, 14336)
         quantize(w_mx[3], span(0, PASSES * P), w_grouped, E4M3)
         place(2, 0, J_TILE, dx)
         acc = accumulate(weights(3), J_TILE, first_steps(0, 0) + first_steps(1, HALF), 1)
@@ -342,6 +338,6 @@ def tile_list_embg_tgf32_ls_kernel(tc, dy, w, ls, wgo, offs, out):
         cut = [(1, dr_line, J_TILE + first, count, E4M3, first) for first, count in [(HALF, HALF), (0, HALF)]]
         for n in range(N_TILES):
             steps = second_steps + cut if n == 0 else second_steps[0:2] + [(1, dr_line, J_TILE, J_TILE, E4M3, 0)] + second_steps[2:3]
-            acc = accumulate(weights(n), J_TILE, steps, [2, "decode3"][n % 2])
+            acc = accumulate(weights(n), J_TILE, steps, [2, "decode1"][n % 2])
             weigh_and_place(n, J_TILE, J_TILE, scaled("dx_second%d" % n, acc[:], n, J_TILE), wgo_sb[1][:])
             nc.sync.dma_start(out=out[n * P : (n + 1) * P, :], in_=windows[n][:])

@@ -33,7 +33,6 @@ QUAD = 32
 STRIP = K_PASS + 1
 GPSIMD_PIECES = [slice(0, 128), slice(128, 256), slice(256, 512)]
 TURNED = 2
-GPSIMD_REST = 32
 
 
 def tile_list_embg_tgf32_ls_kernel(tc, dy, w, ls, wgo, offs, out):
@@ -284,7 +283,7 @@ def tile_list_embg_tgf32_ls_kernel(tc, dy, w, ls, wgo, offs, out):
         acc = accumulate(weights(2), J_TILE, first_steps(0, 0) + first_steps(1, HALF), 0)
 
         dy_grouped, w_grouped = stage(1, w_last, 40960)
-        values = sb("values0", [P, J_TILE + GPSIMD_REST, PACK], F32, 79872)
+        values = sb("values0", [P, J_TILE, PACK], F32, 79872)
         early = [decode(dq_second[0], b * BANK, b) for b in range(4)]
         for b in range(2):
             unload(values[:, span(b * BANK, BANK), :], early[b])
@@ -298,10 +297,12 @@ def tile_list_embg_tgf32_ls_kernel(tc, dy, w, ls, wgo, offs, out):
 
         negated = [sb("negated%d" % b, [P, PACK, BANK], F32) for b in range(TURNED)]
         rounded = [sb("rounded%d" % b, [P, 2, P, 2], BF16) for b in range(TURNED)]
+        banks = {}
         for b in range(TURNED):
             nc.scalar.activation(out=negated[b][:], in_=decode(dq_second[1], b * BANK, b)[:], func=COPY, scale=-1.0)
-        for b in range(TURNED):
             unload(values[:, span((2 + b) * BANK, BANK), :], early[2 + b])
+            banks[2 + b] = decode(dq_second[1], (2 + b) * BANK, 2 + b)
+        for b in range(TURNED):
             sums = psum.tile([P, PACK, P], F32, name="sums", tag=["acc3", "decode0"][b])
             terms = [dy_second[1][:, t, span(b * BANK, BANK)] for t in range(PACK)] + [negated[b][:, t, :] for t in range(PACK)]
             for i, term in enumerate(terms):
@@ -318,14 +319,9 @@ def tile_list_embg_tgf32_ls_kernel(tc, dy, w, ls, wgo, offs, out):
         )
         for cols in GPSIMD_PIECES:
             gpsimd_subtract(left[:, cols, :], dy_second[0][:, :, cols], values[:, cols, :])
-        banks = {b: decode(dq_second[1], b * BANK, b) for b in range(TURNED, 4)}
         dx = weigh("dx30", acc[:, halves[0]], 3, wgo_sb[0][:, halves[0]], HALF)
-        mine = BANK - GPSIMD_REST
-        theirs = span(J_TILE - GPSIMD_REST, GPSIMD_REST)
-        nc.scalar.copy(out=values[:, span(J_TILE, GPSIMD_REST), :], in_=banks[3][:, :, mine:BANK].rearrange("p t c -> p c t"))
-        gpsimd_subtract(left_last[:, theirs, :], dy_second[1][:, :, theirs], values[:, span(J_TILE, GPSIMD_REST), :])
-        subtract(left_last[:, span(2 * BANK, BANK), :], dy_second[1][:, :, span(2 * BANK, BANK)], banks[2])
-        subtract(left_last[:, span(3 * BANK, mine), :], dy_second[1][:, :, span(3 * BANK, mine)], banks[3][:, :, 0:mine])
+        for b in range(TURNED, 4):
+            subtract(left_last[:, span(b * BANK, BANK), :], dy_second[1][:, :, span(b * BANK, BANK)], banks[b])
         place(3, 0, HALF, dx)
         dr_line = mx("dr_second", PASSES * J_TILE, 79872 + 1024)
         quantize(dr_line, whole, left[:], E4M3)

@@ -31,7 +31,7 @@ RUN = 4
 PAIR = 2
 QUAD = 32
 STRIP = K_PASS + 1
-GPSIMD_PIECES = [slice(0, 128), slice(128, 256), slice(256, 512)]
+GPSIMD_PIECES = [slice(0, 128), slice(128, 512)]
 TURNED = 2
 
 
@@ -75,7 +75,7 @@ def tile_list_embg_tgf32_ls_kernel(tc, dy, w, ls, wgo, offs, out):
         offsets = keep.tile([P, J // LIST_GROUP], U16, name="offsets")
         ls_sb = sb("ls_sb", [P, N_TILES], F32)
         wgo_sb = [sb("wgo%d" % s, [P, J_TILE], F32) for s in range(2)]
-        dy_first = {(g, h): sb("dy_first%d%d" % (g, h), [P, PACK, HALF], F32, {(0, 1): 71680, (1, 1): 57344}.get((g, h))) for h in range(2) for g in range(PASSES)}
+        dy_first = {(g, h): sb("dy_first%d%d" % (g, h), [P, PACK, HALF], F32, {(0, 1): 71680}.get((g, h))) for h in range(2) for g in range(PASSES)}
         dy_second = [sb("dy_second%d" % g, [P, PACK, J_TILE], F32) for g in range(PASSES)]
         w_early = [sb("w_early%d" % g, [P, PACK, 2 * P], F32) for g in range(PASSES)]
         w_third = [sb("w_third%d" % g, [P, PACK, P], F32, [8192, 40960][g]) for g in range(PASSES)]
@@ -258,7 +258,7 @@ def tile_list_embg_tgf32_ls_kernel(tc, dy, w, ls, wgo, offs, out):
 
         accs = {(n, h): accumulate(weights(n), HALF, first_steps(h, 0), 2 * h + n) for h in range(2) for n in range(2)}
         for n in range(2):
-            dx = scaled("dx%d0" % n, accs[n, 0][:], n, HALF, [57344, None][n])
+            dx = scaled("dx%d0" % n, accs[n, 0][:], n, HALF, [72704, None][n])
             weigh_and_place(n, 0, HALF, dx, wgo_sb[0][:, halves[0]])
 
         def stage(s, w_tile, at):
@@ -272,7 +272,7 @@ def tile_list_embg_tgf32_ls_kernel(tc, dy, w, ls, wgo, offs, out):
         identity = sb("identity", [P, P], F32)
         nc.scalar.copy(out=identity[:], in_=strip[:, 0:K_PASS:PACK])
 
-        dq_second = [mx("dq_second%d" % g, J_TILE, [57344, None][g]) for g in range(PASSES)]
+        dq_second = [mx("dq_second%d" % g, J_TILE, [72704, None][g]) for g in range(PASSES)]
         dy_grouped, w_grouped = stage(0, w_third, 27648)
         quantize(dq_second[0], whole, dy_grouped, E5M2)
         quantize(w_mx[2], span(0, PASSES * P), w_grouped, E4M3)
@@ -285,7 +285,7 @@ def tile_list_embg_tgf32_ls_kernel(tc, dy, w, ls, wgo, offs, out):
         dy_grouped, w_grouped = stage(1, w_last, 40960)
         values = sb("values0", [P, J_TILE, PACK], F32, 79872)
         early = [decode(dq_second[0], b * BANK, b) for b in range(4)]
-        for b in range(2):
+        for b in range(4):
             unload(values[:, span(b * BANK, BANK), :], early[b])
         quantize(dq_second[1], whole, dy_grouped, E5M2)
         dx = weigh("dx2", acc[:], 2, wgo_sb[0][:], J_TILE, 14336)
@@ -300,7 +300,6 @@ def tile_list_embg_tgf32_ls_kernel(tc, dy, w, ls, wgo, offs, out):
         banks = {}
         for b in range(TURNED):
             nc.scalar.activation(out=negated[b][:], in_=decode(dq_second[1], b * BANK, b)[:], func=COPY, scale=-1.0)
-            unload(values[:, span((2 + b) * BANK, BANK), :], early[2 + b])
             banks[2 + b] = decode(dq_second[1], (2 + b) * BANK, 2 + b)
         for b in range(TURNED):
             sums = psum.tile([P, PACK, P], F32, name="sums", tag=["acc3", "decode0"][b])

@@ -33,6 +33,7 @@ QUAD = 32
 STRIP = K_PASS + 1
 GPSIMD_PIECES = [slice(0, 128), slice(128, 512)]
 TURNED = 2
+GPSIMD_REST = 64
 
 
 def tile_list_embg_tgf32_ls_kernel(tc, dy, w, ls, wgo, offs, out):
@@ -134,10 +135,12 @@ def tile_list_embg_tgf32_ls_kernel(tc, dy, w, ls, wgo, offs, out):
             )
 
         def unload(values, bank):
-            nc.scalar.copy(out=values, in_=bank[:].rearrange("p t c -> p c t"))
+            nc.scalar.copy(out=values, in_=bank.rearrange("p t (c i) -> p c t i", i=PAIR))
 
         def gpsimd_subtract(left, rows, values):
-            nc.gpsimd.tensor_tensor(left, rows.rearrange("p t c -> p c t"), values, SUBTRACT)
+            nc.gpsimd.tensor_tensor(
+                left.rearrange("p (c i) t -> p c t i", i=PAIR), rows.rearrange("p t (c i) -> p c t i", i=PAIR), values, SUBTRACT
+            )
 
         def accumulate(weights, width, steps, tag):
             acc = psum.tile([P, width], F32, name="acc", tag=tag if isinstance(tag, str) else "acc%d" % tag)
@@ -283,10 +286,14 @@ def tile_list_embg_tgf32_ls_kernel(tc, dy, w, ls, wgo, offs, out):
         acc = accumulate(weights(2), J_TILE, first_steps(0, 0) + first_steps(1, HALF), 0)
 
         dy_grouped, w_grouped = stage(1, w_last, 40960)
-        values = sb("values0", [P, J_TILE, PACK], F32, 79872)
+        values = sb("values0", [P, (J_TILE + GPSIMD_REST) // PAIR, PACK, PAIR], F32, 79872)
+
+        def pairs_of(first, count):
+            return values[:, span(first // PAIR, count // PAIR), :, :]
+
         early = [decode(dq_second[0], b * BANK, b) for b in range(4)]
         for b in range(4):
-            unload(values[:, span(b * BANK, BANK), :], early[b])
+            unload(pairs_of(b * BANK, BANK), early[b][:])
         quantize(dq_second[1], whole, dy_grouped, E5M2)
         dx = weigh("dx2", acc[:], 2, wgo_sb[0][:], J_TILE, 14336)
         quantize(w_mx[3], span(0, PASSES * P), w_grouped, E4M3)
@@ -298,9 +305,13 @@ def tile_list_embg_tgf32_ls_kernel(tc, dy, w, ls, wgo, offs, out):
         negated = [sb("negated%d" % b, [P, PACK, BANK], F32) for b in range(TURNED)]
         rounded = [sb("rounded%d" % b, [P, 2, P, 2], BF16) for b in range(TURNED)]
         banks = {}
+        mine = BANK - GPSIMD_REST
+        theirs = span(J_TILE - GPSIMD_REST, GPSIMD_REST)
         for b in range(TURNED):
             nc.scalar.activation(out=negated[b][:], in_=decode(dq_second[1], b * BANK, b)[:], func=COPY, scale=-1.0)
-            banks[2 + b] = decode(dq_second[1], (2 + b) * BANK, 2 + b)
+            banks[3 - b] = decode(dq_second[1], (3 - b) * BANK, 3 - b)
+            if b == 0:
+                unload(pairs_of(J_TILE, GPSIMD_REST), banks[3][:, :, mine:BANK])
         for b in range(TURNED):
             sums = psum.tile([P, PACK, P], F32, name="sums", tag=["acc3", "decode0"][b])
             terms = [dy_second[1][:, t, span(b * BANK, BANK)] for t in range(PACK)] + [negated[b][:, t, :] for t in range(PACK)]
@@ -317,10 +328,11 @@ def tile_list_embg_tgf32_ls_kernel(tc, dy, w, ls, wgo, offs, out):
             in_=words[:].rearrange("p b u j -> p b j u"),
         )
         for cols in GPSIMD_PIECES:
-            gpsimd_subtract(left[:, cols, :], dy_second[0][:, :, cols], values[:, cols, :])
+            gpsimd_subtract(left[:, cols, :], dy_second[0][:, :, cols], pairs_of(cols.start, cols.stop - cols.start))
+        gpsimd_subtract(left_last[:, theirs, :], dy_second[1][:, :, theirs], pairs_of(J_TILE, GPSIMD_REST))
         dx = weigh("dx30", acc[:, halves[0]], 3, wgo_sb[0][:, halves[0]], HALF)
-        for b in range(TURNED, 4):
-            subtract(left_last[:, span(b * BANK, BANK), :], dy_second[1][:, :, span(b * BANK, BANK)], banks[b])
+        subtract(left_last[:, span(2 * BANK, BANK), :], dy_second[1][:, :, span(2 * BANK, BANK)], banks[2])
+        subtract(left_last[:, span(3 * BANK, mine), :], dy_second[1][:, :, span(3 * BANK, mine)], banks[3][:, :, 0:mine])
         place(3, 0, HALF, dx)
         dr_line = mx("dr_second", PASSES * J_TILE, 79872 + 1024)
         quantize(dr_line, whole, left[:], E4M3)

@@ -51,10 +51,10 @@ def tile_list_embg_tgf32_ls_kernel(tc, dy, w, ls, wgo, offs, out):
         def mx(name, width, at=None):
             return sb(name + "_codes", [P, width], U32, at), sb(name + "_scales", [P, width], U8)
 
-        def group(copy, grouped, rows):
+        def group(copy, grouped, rows, run=RUN):
             copy(
-                out=grouped.rearrange("p (c i) t -> p c t i", i=RUN),
-                in_=rows.rearrange("p t (c i) -> p c t i", i=RUN),
+                out=grouped.rearrange("p (c i) t -> p c t i", i=run),
+                in_=rows.rearrange("p t (c i) -> p c t i", i=run),
             )
 
         def scalar_cast(out, in_):
@@ -205,7 +205,7 @@ def tile_list_embg_tgf32_ls_kernel(tc, dy, w, ls, wgo, offs, out):
         def group_weights(n, at=None):
             grouped = sb("w_grouped%d" % n, [P, PASSES * P, PACK], BF16, at)
             for g in range(PASSES):
-                group(nc.scalar.copy, grouped[:, span(g * P, P), :], w_early[g][:, :, span(n * P, P)])
+                group(nc.scalar.copy, grouped[:, span(g * P, P), :], w_early[g][:, :, span(n * P, P)], PAIR)
             return grouped
 
         w_mx = {n: mx("w%d" % n, PASSES * P, [0 + 75776, 71680, None, 12288][n]) for n in range(N_TILES)}
@@ -228,7 +228,7 @@ def tile_list_embg_tgf32_ls_kernel(tc, dy, w, ls, wgo, offs, out):
             cols = span(b * BANK, BANK)
             group(scalar_cast, first[b][:], dy_first[0, 0][:, :, cols])
         for g, h in [(1, 0), (0, 1), (1, 1)]:
-            group(scalar_cast, grouped[g, h][:], dy_first[g, h][:])
+            group(scalar_cast, grouped[g, h][:], dy_first[g, h][:], PAIR)
         quantize(dq_first[0], span(0, BANK), first[0][:], E5M2)
         banks[0, 0, 0] = decode(dq_first[0], 0, 0)
         window(1, nc.vector.memset, 0)
@@ -267,9 +267,9 @@ def tile_list_embg_tgf32_ls_kernel(tc, dy, w, ls, wgo, offs, out):
         def stage(s, w_tile, at):
             grouped = sb("stage%d" % s, [P, J_TILE + PASSES * P, PACK], BF16, at)
             for h in range(2):
-                group(scalar_cast, grouped[:, halves[h], :], dy_second[s][:, :, halves[h]])
+                group(scalar_cast, grouped[:, halves[h], :], dy_second[s][:, :, halves[h]], [RUN, PAIR][h])
             for g in range(PASSES):
-                group(nc.scalar.copy, grouped[:, span(J_TILE + g * P, P), :], w_tile[g][:])
+                group(nc.scalar.copy, grouped[:, span(J_TILE + g * P, P), :], w_tile[g][:], PAIR)
             return grouped[:, 0:J_TILE, :], grouped[:, span(J_TILE, PASSES * P), :]
 
         identity = sb("identity", [P, P], F32)

from contextlib import ExitStack

import concourse.mybir as mybir

K, N, T, J = 1024, 512, 2048, 1024
FLOPS = 2 * (2 * K * N * J) + 2 * K * 512 * J

F32 = mybir.dt.float32
BF16 = mybir.dt.bfloat16
U32 = mybir.dt.uint32
U16 = mybir.dt.uint16
U8 = mybir.dt.uint8
E4M3 = mybir.dt.float8_e4m3fn_x4
E5M2 = mybir.dt.float8_e5m2_x4
COPY = mybir.ActivationFunctionType.Copy
MULT = mybir.AluOpType.mult
ADD = mybir.AluOpType.add
IS_EQUAL = mybir.AluOpType.is_equal
SUBTRACT = mybir.AluOpType.subtract

P = 128
PACK = 4
K_PASS = P * PACK
PASSES = K // K_PASS
J_TILE = 512
HALF = J_TILE // 2
BANK = J_TILE // PACK
N_TILES = N // P
LIST_GROUP = 16
RUN = 4
PAIR = 2
QUAD = 32
STRIP = K_PASS + 1
GPSIMD_PIECES = [slice(0, 128), slice(128, 512)]
TURNED = 2
GPSIMD_REST = 64


def tile_list_embg_tgf32_ls_kernel(tc, dy, w, ls, wgo, offs, out):
    nc = tc.nc
    with ExitStack() as ctx:
        keep = ctx.enter_context(tc.tile_pool(name="keep", bufs=1))
        turns = ctx.enter_context(tc.tile_pool(name="turns", bufs=1))
        psum = ctx.enter_context(tc.psum_pool(name="psum", bufs=1))

        def sb(name, shape, dtype, at=None):
            if at is None:
                return keep.tile(shape, dtype, name=name, tag=name, align_bytes=64)
            return turns.tile(shape, dtype, name=name, tag=name, align_bytes=64, offset=at)

        def mx(name, width, at=None):
            return sb(name + "_codes", [P, width], U32, at), sb(name + "_scales", [P, width], U8)

        def group(copy, grouped, rows, run=RUN):
            copy(
                out=grouped.rearrange("p (c i) t -> p c t i", i=run),
                in_=rows.rearrange("p t (c i) -> p c t i", i=run),
            )

        def scalar_cast(out, in_):
            nc.scalar.activation(out=out, in_=in_, func=COPY)

        def quantize(operand, cols, grouped, fmt):
            codes, scales = operand
            nc.vector.quantize_mx(out=codes[:, cols].bitcast(fmt), scales=scales[:, cols], in_=grouped.rearrange("p c t -> p (c t)"))

        def k_rows(x, g, cols):
            return x[g * K_PASS : (g + 1) * K_PASS, cols].rearrange("(p t) c -> p t c", t=PACK)

        def span(first, count):
            return slice(first, first + count)

        halves = [span(h * HALF, HALF) for h in range(2)]
        whole = span(0, J_TILE)

        offsets = keep.tile([P, J // LIST_GROUP], U16, name="offsets")
        ls_sb = sb("ls_sb", [P, N_TILES], F32)
        wgo_sb = [sb("wgo%d" % s, [P, J_TILE], F32) for s in range(2)]
        dy_first = {(g, h): sb("dy_first%d%d" % (g, h), [P, PACK, HALF], F32, {(0, 1): 71680}.get((g, h))) for h in range(2) for g in range(PASSES)}
        dy_second = [sb("dy_second%d" % g, [P, PACK, J_TILE], F32) for g in range(PASSES)]
        w_early = [sb("w_early%d" % g, [P, PACK, 2 * P], F32) for g in range(PASSES)]
        w_third = [sb("w_third%d" % g, [P, PACK, P], F32, [8192, 40960][g]) for g in range(PASSES)]
        w_last = [sb("w_last%d" % g, [P, PACK, P], F32, [14336, 12288][g]) for g in range(PASSES)]

        def load_dy(g, h):
            nc.sync.dma_start(out=dy_first[g, h][:], in_=k_rows(dy, g, halves[h]))

        for b in range(2):
            cols = span(b * BANK, BANK)
            nc.sync.dma_start(out=dy_first[0, 0][:, :, cols], in_=k_rows(dy, 0, cols))
        load_dy(1, 0)
        load_dy(0, 1)
        load_dy(1, 1)
        for g in range(PASSES):
            nc.sync.dma_start(out=w_early[g][:], in_=k_rows(w, g, span(0, 2 * P)))
        with nc.allow_non_contiguous_dma(reason="one factor for each partition and n tile"):
            nc.sync.dma_start(out=ls_sb[:], in_=ls.rearrange("(c p) -> p c", p=P))
        nc.sync.dma_start(offsets[:], offs)
        nc.sync.dma_start(out=wgo_sb[0][:], in_=wgo[:, 0:J_TILE])
        for s, w_tile in enumerate([w_third, w_last]):
            for h in range(2):
                nc.sync.dma_start(out=dy_second[s][:, :, halves[h]], in_=k_rows(dy, s, span(J_TILE + h * HALF, HALF)))
            for g in range(PASSES):
                nc.sync.dma_start(out=w_tile[g][:], in_=k_rows(w, g, span((2 + s) * P, P)))
        nc.sync.dma_start(out=wgo_sb[1][:], in_=wgo[:, J_TILE:J])


        windows = {}

        def window(n, memset, at=None):
            windows[n] = sb("window%d" % n, [P, T], F32, at)
            memset(windows[n][:].bitcast(U32), 0)

        def decode(operand, first, tag):
            codes, scales = operand
            bank = psum.tile([P, PACK, BANK], F32, name="decoded", tag="decode%d" % tag)
            for t in range(PACK):
                nc.tensor.matmul_mx(
                    out=bank[:, t, :],
                    lhsT=eye_codes[:, span(t * P, P)].bitcast(E4M3),
                    lhsT_scale=eye_scales[:, span(t * P, P)],
                    rhs=codes[:, span(first, BANK)].bitcast(E5M2),
                    rhs_scale=scales[:, span(first, BANK)],
                    start=True,
                    stop=True,
                )
            return bank

        def subtract(left, rows, bank):
            nc.vector.tensor_tensor(
                left.rearrange("p (c i) t -> p c t i", i=PAIR),
                rows.rearrange("p t (c i) -> p c t i", i=PAIR),
                bank[:, :, :].rearrange("p t (c i) -> p c t i", i=PAIR),
                SUBTRACT,
            )

        def unload(values, bank):
            nc.scalar.copy(out=values, in_=bank.rearrange("p t (c i) -> p c t i", i=PAIR))

        def gpsimd_subtract(left, rows, values):
            nc.gpsimd.tensor_tensor(
                left.rearrange("p (c i) t -> p c t i", i=PAIR), rows.rearrange("p t (c i) -> p c t i", i=PAIR), values, SUBTRACT
            )

        def accumulate(weights, width, steps, tag):
            acc = psum.tile([P, width], F32, name="acc", tag=tag if isinstance(tag, str) else "acc%d" % tag)
            for i, (g, (codes, scales), first, count, fmt, col) in enumerate(steps):
                (w_codes, w_scales), w_first = weights(g)
                nc.tensor.matmul_mx(
                    out=acc[:, span(col, count)],
                    lhsT=w_codes[:, span(w_first, P)].bitcast(E4M3),
                    lhsT_scale=w_scales[:, span(w_first, P)],
                    rhs=codes[:, span(first, count)].bitcast(fmt),
                    rhs_scale=scales[:, span(first, count)],
                    start=(i == 0),
                    stop=(i == len(steps) - 1),
                )
            return acc

        def lists(first, count):
            return offsets[:, span(first // LIST_GROUP, count // LIST_GROUP)]

        def weigh(name, acc_cols, n, wgo_cols, count, at=None):
            dx = sb(name, [P, count], F32, at)
            nc.vector.scalar_tensor_tensor(dx[:], acc_cols, ls_sb[:, n : n + 1], wgo_cols, MULT, MULT)
            return dx

        def place(n, first, count, dx):
            nc.vector.tensor_copy(windows[n][:].indirect(lists(first, count)), dx[:])

        def scaled(name, acc_cols, n, count, at=None):
            dx = sb(name, [P, count], F32, at)
            nc.scalar.activation(out=dx[:], in_=acc_cols, func=COPY, scale=ls_sb[:, n : n + 1])
            return dx

        def weigh_and_place(n, first, count, dx, wgo_cols):
            nc.vector.tensor_tensor(windows[n][:].indirect(lists(first, count)), dx[:], wgo_cols, MULT)

        ones = sb("ones", [P, QUAD + 1], F32)
        nc.vector.memset(ones[:], 1.0)
        column = sb("column", [P, QUAD], F32)
        nc.vector.tensor_tensor_scan(column[:], ones[:, 0:QUAD], ones[:, 0:QUAD], 0.0, MULT, ADD)
        row = sb("row", [P, QUAD], F32)
        nc.vector.transpose(row[:], column[:])
        strip = sb("strip", [P, STRIP + 1], BF16)
        nc.vector.memset(strip[:].bitcast(U32), 0)
        for b in range(P // QUAD):
            lanes = slice(b * QUAD, (b + 1) * QUAD)
            nc.vector.tensor_tensor(strip[lanes, b * P : (b + 1) * P : PACK], column[lanes, :], row[lanes, :], IS_EQUAL)
        eye = sb("eye", [P, PACK * STRIP], BF16)
        eye_codes = sb("eye_codes", [P, PACK * P], U32)
        eye_scales = sb("eye_scales", [P, PACK * P], U8)
        for c in range(2):
            nc.vector.tensor_copy(
                out=eye[:, 2 * c * STRIP : 2 * (c + 1) * STRIP].rearrange("p (t x) -> p t x", t=2),
                in_=strip[:, 0:STRIP].unsqueeze(1).to_broadcast([P, 2, STRIP]),
            )
        for c in range(2):
            words = slice(c * HALF, (c + 1) * HALF)
            values = eye[:, PACK * words.start : PACK * words.stop]
            nc.vector.quantize_mx(out=eye_codes[:, words].bitcast(E4M3), scales=eye_scales[:, words], in_=values)

        window(0, nc.gpsimd.memset)

        def group_weights(n, at=None):
            grouped = sb("w_grouped%d" % n, [P, PASSES * P, PACK], BF16, at)
            for g in range(PASSES):
                group(nc.scalar.copy, grouped[:, span(g * P, P), :], w_early[g][:, :, span(n * P, P)], PAIR)
            return grouped

        w_mx = {n: mx("w%d" % n, PASSES * P, [0 + 75776, 71680, None, 12288][n]) for n in range(N_TILES)}
        dq_first = [mx("dq_first%d" % h, PASSES * HALF) for h in range(2)]
        dr_first = [mx("dr_first%d" % h, PASSES * HALF) for h in range(2)]
        grouped = {(g, h): sb("grouped%d%d" % (g, h), [P, HALF, PACK], BF16, {(1, 1): 75776}.get((g, h))) for g, h in [(1, 0), (0, 1), (1, 1)]}
        first = [sb("first%d" % b, [P, BANK, PACK], BF16, [0, None][b]) for b in range(2)]
        lefts = [sb("left%d" % h, [P, PASSES * HALF, PACK], BF16, [None, 19456][h]) for h in range(2)]
        banks = {}

        def first_tier(g, h):
            quantize(dq_first[h], halves[g], grouped[g, h][:], E5M2)
            for b in range(2):
                banks[g, h, b] = decode(dq_first[h], g * HALF + b * BANK, 2 * g + b)

        def residual(g, h, b):
            subtract(lefts[h][:, span(g * HALF + b * BANK, BANK), :], dy_first[g, h][:, :, span(b * BANK, BANK)], banks[g, h, b])

        for b in range(2):
            cols = span(b * BANK, BANK)
            group(scalar_cast, first[b][:], dy_first[0, 0][:, :, cols])
        for g, h in [(1, 0), (0, 1), (1, 1)]:
            group(scalar_cast, grouped[g, h][:], dy_first[g, h][:], PAIR)
        quantize(dq_first[0], span(0, BANK), first[0][:], E5M2)
        banks[0, 0, 0] = decode(dq_first[0], 0, 0)
        window(1, nc.vector.memset, 0)
        quantize(dq_first[0], span(BANK, BANK), first[1][:], E5M2)
        banks[0, 0, 1] = decode(dq_first[0], BANK, 1)
        residual(0, 0, 0)
        first_tier(1, 0)
        residual(0, 0, 1)
        first_tier(0, 1)
        residual(1, 0, 0)
        residual(1, 0, 1)
        residual(0, 1, 0)
        quantize(dr_first[0], whole, lefts[0][:], E4M3)
        first_tier(1, 1)
        residual(0, 1, 1)
        quantize(w_mx[0], span(0, PASSES * P), group_weights(0)[:], E4M3)
        residual(1, 1, 0)
        residual(1, 1, 1)
        left = lefts[1]
        quantize(w_mx[1], span(0, PASSES * P), group_weights(1, 26624)[:], E4M3)
        quantize(dr_first[1], whole, left[:], E4M3)
        window(2, nc.gpsimd.memset, 19456)

        def weights(n):
            return lambda g: (w_mx[n], g * P)

        def first_steps(h, col):
            steps = [(g, dq_first[h], g * HALF, HALF, E5M2, col) for g in range(PASSES)]
            return steps + [(g, dr_first[h], g * HALF, HALF, E4M3, col) for g in range(PASSES)]

        accs = {(n, h): accumulate(weights(n), HALF, first_steps(h, 0), 2 * h + n) for h in range(2) for n in range(2)}
        for n in range(2):
            dx = scaled("dx%d0" % n, accs[n, 0][:], n, HALF, [72704, None][n])
            weigh_and_place(n, 0, HALF, dx, wgo_sb[0][:, halves[0]])

        def stage(s, w_tile, at):
            grouped = sb("stage%d" % s, [P, J_TILE + PASSES * P, PACK], BF16, at)
            for h in range(2):
                group(scalar_cast, grouped[:, halves[h], :], dy_second[s][:, :, halves[h]], [RUN, PAIR][h])
            for g in range(PASSES):
                group(nc.scalar.copy, grouped[:, span(J_TILE + g * P, P), :], w_tile[g][:], PAIR)
            return grouped[:, 0:J_TILE, :], grouped[:, span(J_TILE, PASSES * P), :]

        identity = sb("identity", [P, P], F32)
        nc.scalar.copy(out=identity[:], in_=strip[:, 0:K_PASS:PACK])

        dq_second = [mx("dq_second%d" % g, J_TILE, [72704, None][g]) for g in range(PASSES)]
        dy_grouped, w_grouped = stage(0, w_third, 27648)
        quantize(dq_second[0], whole, dy_grouped, E5M2)
        quantize(w_mx[2], span(0, PASSES * P), w_grouped, E4M3)
        window(3, nc.gpsimd.memset, 32768)
        for n in range(2):
            dx = scaled("dx%d1" % n, accs[n, 1][:], n, HALF, 8192 + 1024 * n)
            weigh_and_place(n, HALF, HALF, dx, wgo_sb[0][:, halves[1]])
        acc = accumulate(weights(2), J_TILE, first_steps(0, 0) + first_steps(1, HALF), 0)

        dy_grouped, w_grouped = stage(1, w_last, 40960)
        values = sb("values0", [P, (J_TILE + GPSIMD_REST) // PAIR, PACK, PAIR], F32, 79872)

        def pairs_of(first, count):
            return values[:, span(first // PAIR, count // PAIR), :, :]

        early = [decode(dq_second[0], b * BANK, b) for b in range(4)]
        for b in range(4):
            unload(pairs_of(b * BANK, BANK), early[b][:])
        quantize(dq_second[1], whole, dy_grouped, E5M2)
        dx = weigh("dx2", acc[:], 2, wgo_sb[0][:], J_TILE, 14336)
        quantize(w_mx[3], span(0, PASSES * P), w_grouped, E4M3)
        place(2, 0, J_TILE, dx)
        acc = accumulate(weights(3), J_TILE, first_steps(0, 0) + first_steps(1, HALF), 1)
        left = sb("left20", [P, J_TILE, PACK], BF16, 43008)
        left_last = sb("left21", [P, J_TILE, PACK], BF16)

        negated = [sb("negated%d" % b, [P, PACK, BANK], F32) for b in range(TURNED)]
        rounded = [sb("rounded%d" % b, [P, 2, P, 2], BF16) for b in range(TURNED)]
        banks = {}
        mine = BANK - GPSIMD_REST
        theirs = span(J_TILE - GPSIMD_REST, GPSIMD_REST)
        for b in range(TURNED):
            nc.scalar.activation(out=negated[b][:], in_=decode(dq_second[1], b * BANK, b)[:], func=COPY, scale=-1.0)
            banks[3 - b] = decode(dq_second[1], (3 - b) * BANK, 3 - b)
            if b == 0:
                unload(pairs_of(J_TILE, GPSIMD_REST), banks[3][:, :, mine:BANK])
        for b in range(TURNED):
            sums = psum.tile([P, PACK, P], F32, name="sums", tag=["acc3", "decode0"][b])
            terms = [dy_second[1][:, t, span(b * BANK, BANK)] for t in range(PACK)] + [negated[b][:, t, :] for t in range(PACK)]
            for i, term in enumerate(terms):
                nc.tensor.matmul(sums[:, i % PACK, :], term, identity[:], start=(i == 0), stop=(i == len(terms) - 1), is_transpose=True)
            nc.scalar.copy(out=rounded[b][:], in_=sums[:].rearrange("j (u e) p -> j u p e", e=2))
        words = psum.tile([P, TURNED, 2, BANK], F32, name="words", tag="decode1")
        for b in range(TURNED):
            pairs = rounded[b][:].rearrange("j u p e -> j (u p e)").bitcast(F32)
            for u in range(2):
                nc.tensor.transpose(words[:, b, u, :], pairs[:, span(u * P, P)], identity[:])
        nc.scalar.copy(
            out=left_last[:, 0 : TURNED * BANK, :].rearrange("p c t -> p (c t)").bitcast(F32).rearrange("p (b j u) -> p b j u", b=TURNED, u=2),
            in_=words[:].rearrange("p b u j -> p b j u"),
        )
        for cols in GPSIMD_PIECES:
            gpsimd_subtract(left[:, cols, :], dy_second[0][:, :, cols], pairs_of(cols.start, cols.stop - cols.start))
        gpsimd_subtract(left_last[:, theirs, :], dy_second[1][:, :, theirs], pairs_of(J_TILE, GPSIMD_REST))
        dx = weigh("dx30", acc[:, halves[0]], 3, wgo_sb[0][:, halves[0]], HALF)
        subtract(left_last[:, span(2 * BANK, BANK), :], dy_second[1][:, :, span(2 * BANK, BANK)], banks[2])
        subtract(left_last[:, span(3 * BANK, mine), :], dy_second[1][:, :, span(3 * BANK, mine)], banks[3][:, :, 0:mine])
        place(3, 0, HALF, dx)
        dr_line = mx("dr_second", PASSES * J_TILE, 79872 + 1024)
        quantize(dr_line, whole, left[:], E4M3)
        for h in (1, 0):
            quantize(dr_line, span(J_TILE + h * HALF, HALF), left_last[:, halves[h], :], E4M3)
        weigh_and_place(3, HALF, HALF, scaled("dx31", acc[:, halves[1]], 3, HALF, 79872), wgo_sb[0][:, halves[1]])

        second_steps = [(g, dq_second[g], 0, J_TILE, E5M2, 0) for g in range(PASSES)]
        second_steps = second_steps + [(0, dr_line, 0, J_TILE, E4M3, 0)]
        cut = [(1, dr_line, J_TILE + first, count, E4M3, first) for first, count in [(HALF, HALF), (0, HALF)]]
        for n in range(N_TILES):
            steps = second_steps + cut if n == 0 else second_steps[0:2] + [(1, dr_line, J_TILE, J_TILE, E4M3, 0)] + second_steps[2:3]
            acc = accumulate(weights(n), J_TILE, steps, [2, "decode1"][n % 2])
            weigh_and_place(n, J_TILE, J_TILE, scaled("dx_second%d" % n, acc[:], n, J_TILE), wgo_sb[1][:])
            nc.sync.dma_start(out=out[n * P : (n + 1) * P, :], in_=windows[n][:])
